import numpy as np, ml_dtypes
CORES = [35,38,43,46]
N = 4
BF = ml_dtypes.bfloat16
def gentries(a):
    return np.ascontiguousarray(a.reshape(8, 16, -1).transpose(0, 2, 1)).reshape(8, -1)
def gtable(e):
    e = np.asarray(e); return np.ascontiguousarray(e.reshape(8, -1, 16).transpose(0, 2, 1)).reshape(128, -1).astype(np.int32)
W, R, PG, V, H = 4096, 16, 256, 5, 1
K = PG * R
def parts(rng):
    x = rng.integers(0, 256, (N, 8, 16, W)); e = rng.integers(0, 256, (N, 8, 16, PG)); w = rng.integers(0, 16, (N, 8, 16))
    h = rng.choice(np.array([1000, 1300, 1600, 1900]), (N, 8, 1)) + rng.integers(-300, 301, (N, 8, 16))
    l = rng.integers(0, W, (N, 8, K)); share = np.repeat(rng.choice(np.array([0.0, 0.3, 0.6, 0.9]), (N, 8, PG)), R, axis=2)
    s = np.where(rng.random((N, 8, K)) < share, l, rng.integers(0, W, (N, 8, K)))
    c = rng.random((N, 8, K)); p = np.where(c < 0.3, s, np.where(c < 0.4, l, rng.integers(0, W, (N, 8, K))))
    return x, e, w, h, p, s, l, rng.integers(0, W, (N, 8, K))
def pack(x, e, w, h, p, s, l, q):
    r = {"xt": x.reshape(N, 128, W).astype(np.float32).astype(BF), "ed": e.reshape(N, 128, PG).astype(np.float32).astype(BF),
         "wt": np.ascontiguousarray(w.reshape(N, 128, 1)).astype(np.int32), "th": np.ascontiguousarray(h.reshape(N, 128, 1)).astype(np.int32)}
    for k, z in (("pl", p), ("sl", s), ("ll", l), ("ql", q)): r[k] = np.stack([gtable(a) for a in z])
    return r
def setup_inputs(rng):
    return pack(*parts(rng))
def setup_inputs_spread(rng):
    x, e, w, h, p, s, l, q = parts(rng)
    x = np.minimum((np.exp2(8 * rng.random((N, 8, 1, W))) * rng.random((N, 8, 16, W))).astype(np.int64), 255)
    e = np.minimum((np.exp2(8 * rng.random((N, 8, 1, PG))) * rng.random((N, 8, 16, PG))).astype(np.int64), 255)
    w = (16 * rng.random((N, 8, 16)) ** 3).astype(np.int64); h = np.minimum(np.exp2(12 * rng.random((N, 8, 16))).astype(np.int64) - 1, 4080)
    p, s, l, q = [(W * rng.random((N, 8, K)) ** 3).astype(np.int64) for z in range(4)]
    s = np.where(rng.random((N, 8, K)) < np.repeat(rng.random((N, 8, PG)), R, axis=2), l, s)
    return pack(x, e, w, h, p, s, l, q)
def setup_inputs_ends(rng):
    x = 255 * rng.integers(0, 2, (N, 8, 16, W)); e = 255 * rng.integers(0, 2, (N, 8, 16, PG)); w = 15 * rng.integers(0, 2, (N, 8, 16)); h = 4080 * rng.integers(0, 2, (N, 8, 16))
    kind = rng.integers(0, 3, (N, 8, 1)); kind[:, 7] = 0; kind[0, 0] = 0; kind[1, 1] = 1
    x[..., 0] = np.where(kind == 0, 0, np.where(kind == 1, 255, x[..., 0])); x[..., W - 1] = np.where(kind == 0, 255, np.where(kind == 1, 0, x[..., W - 1]))
    w[:, :, 5] = 0; w[:, 7] = 15; w[:, :, 2] = 15; w[:, :, 13] = 15
    h[:, :, 0] = 0; h[:, :, 15] = 0; h[:, :, 1] = 4080; h[:, :, 14] = 4080
    p, s, l, q = [np.where(rng.random((N, 8, K)) < 0.75, (W - 1) * rng.integers(0, 2, (N, 8, K)), rng.integers(0, W, (N, 8, K))) for z in range(4)]
    pv, sv, lv = [z.reshape(N, 8, PG, R) for z in (p, s, l)]; k = np.arange(R)
    for i in (0, 1, 2, 3, PG - 4, PG - 3, PG - 2, PG - 1):
        pv[:, :, i] = 0; sv[:, :, i] = W - 1; lv[:, :, i] = W - 1
    lv[:, :, [0, PG - 1]] = np.where(k % 4 == 1, 0, W - 1)
    lv[:, :, [1, PG - 2]] = np.where((k % 4 == 1) | (k == 2), 0, W - 1)
    lv[:, :, [3, PG - 4]] = 0
    e[..., [0, PG - 1]] = 0; e[:, :, 2, [0, PG - 1]] = 255; e[:, :, 13, [0, PG - 1]] = 18
    e[..., [2, PG - 3]] = 0; e[..., [3, PG - 4]] = 255
    return pack(x, e, w, h, p, s, l, q)
def setup_inputs_corners(rng):
    x, e, w, h, p, s, l, q = parts(rng)
    cnt = np.roll(np.array([31, 32, 0, 8 * PG, 33, 1, 8 * PG - 1, 64])[:N], int(rng.integers(0, N))); fl = np.zeros((N, 8 * PG), bool)
    for r in range(N): fl[r, rng.permutation(8 * PG)[:int(cnt[r])]] = True
    fr = np.repeat(fl.reshape(N, 8, PG), R, axis=2)
    lv = l.reshape(N, 8, PG, R); lv[:, :, [0, PG - 1]] = (W - 1) * rng.integers(0, 2, (N, 8, 2, R))
    far = (l + rng.integers(1, W, l.shape)) % W; half = np.repeat(rng.random((N, 8, PG)) < 0.5, R, axis=2)
    s = np.where(fr, far, l); p = np.where(fr | half, l, rng.integers(0, W, l.shape))
    for g in range(8):
        if g % 4 < 3: q[:, g] = (l, s, p)[g % 4][:, g]
    w[:, 0] = 0; w[:, 7] = 15; w[:, 4] = 15; w[:, 3] = 0; w[:, 3, 15] = 15; w[:, 5] = 0; w[:, 5, 0] = 1
    h = np.where(rng.random(h.shape) < 0.5, rng.choice(np.array([0, 1, 4079, 4080]), h.shape), h)
    e[..., [0, PG - 1]] = 0; e[:, :, 2, [0, PG - 1]] = 255; e[:, :, 13, [0, PG - 1]] = 18
    e[..., 1] = 255; e[..., PG - 2] = 0
    return pack(x, e, w, h, p, s, l, q)
def setup_inputs_alike(rng):
    x, e, w, h, p, s, l, q = parts(rng)
    step = rng.choice(np.array([1, 4, 8, 32]), (N, 8, 1, 1)); lane = rng.integers(0, 8, (N, 8, 16, 1))
    x = step * (rng.integers(0, 8, (N, 8, 1, W)) ^ lane); e = step * (rng.integers(0, 8, (N, 8, 1, PG)) ^ lane)
    h = step[..., 0] * rng.integers(20, 81, (N, 8, 16))
    return pack(x, e, w, h, p, s, l, q)
def setup_inputs_near(rng):
    x, e, w, h, p, s, l, q = parts(rng); n = np.arange(N); f = rng.integers(0, 16, N); k = np.arange(R)
    s[:, 0] = l[:, 0]; h[:, 0] = 0
    h[:, 7] = 4080; x[:, 7, :, :2] = 0; x[:, 7, :, W - 2:] = 255; x[n, 7, f, 1] = 1; x[n, 7, f, W - 2] = 254
    pv, sv, lv, qv = [z.reshape(N, 8, PG, R)[:, 7] for z in (p, s, l, q)]
    for z in (pv, sv, lv): z[:, PG - 1] = W - 1; z[:, PG - 3] = W - 1
    pv[:, PG - 1, R - 4:] = 0; sv[:, PG - 1, R - 4:] = 0; qv[:, PG - 1, R - 4:] = W - 2
    pv[:, PG - 2] = 0; sv[:, PG - 2] = W - 1; sv[:, PG - 2, 0] = W - 2; lv[:, PG - 2] = np.where(k % 4 == 1, 0, W - 1)
    e[:, 7, :, PG - 3] = 0; e[n, 7, f, PG - 3] = 1
    pv[:, PG - 4] = 1; sv[:, PG - 4] = 0; lv[:, PG - 4] = W - 1
    return pack(x, e, w, h, p, s, l, q)
def check_inputs(d):
    bad = []
    for k, hi in (("xt", 255), ("ed", 255), ("wt", 15), ("th", 4080), ("pl", W - 1), ("sl", W - 1), ("ll", W - 1), ("ql", W - 1)):
        v = np.asarray(d[k]).astype(np.float64)
        if not (np.min(v) >= 0 and np.max(v) <= hi): bad.append("range of " + k)
        elif np.any(v != np.floor(v)): bad.append("whole numbers of " + k)
    return bad
def dist(y, z):
    return np.add.reduce(np.abs(y - z), axis=1, dtype=np.int32)
def reference(xt, ed, wt, th, pl, sl, ll, ql):
    x = xt.astype(np.float32).astype(np.int16).reshape(N, 8, 16, W); e = ed.astype(np.float32).astype(np.int16).reshape(N, 8, 16, PG)
    w = wt.astype(np.int32).reshape(N, 8, 16, 1); h = th.astype(np.int32).reshape(N, 8, 16)[:, :, np.arange(K) % 16]
    p, s, l, q = [np.stack([gentries(a) for a in z]).astype(np.int64) for z in (pl, sl, ll, ql)]
    more = 37 * (np.arange(K) % R); A = np.zeros(N, np.int64)
    for t in range(V):
        new = np.zeros_like(l); failed = np.zeros((N, 8, PG), bool); m = np.zeros((N, 8, 16, PG), np.int16)
        for r in range(N):
            vp, vs, vl, vq = [np.take_along_axis(x[r], z[r][:, None, :], 2) for z in (p, s, l, q)]
            a = dist(vp, vs); b = dist(vs, vl); c = dist(vp, vl); d = dist(vq, vs); o = dist(vl, np.repeat(e[r], R, axis=2))
            failed[r] = 2 * np.sum((c - b).reshape(8, PG, R), axis=2) < np.sum(a.reshape(8, PG, R), axis=2)
            u = np.repeat(np.sum(w[r] * e[r], axis=1) & (W - 1), R, axis=1).astype(np.int64)
            change = ((l[r] * u >> 5) + l[r] + more + A[r]) & (W - 1)
            new[r] = np.where(np.repeat(failed[r], R, axis=1) & (c < b), p[r], np.where(d < b, q[r], np.where(o >= h[r], change, l[r])))
            m[r] = np.max(vl.reshape(8, 16, PG, R), axis=3)
        got = np.roll(m, N // 2, axis=0)
        e = np.where(failed[:, :, None, :], np.abs(e - got), (e + got) >> 1)
        A = np.sum(failed, axis=(1, 2)).astype(np.int64) & 31
        q = np.where(new != l, l, q); p, s, l = s, l, new
        if t < V - 1: p, s, l, q = [np.roll(z, H, axis=0) for z in (p, s, l, q)]
    out = [np.stack([gtable(a) for a in z]).astype(np.float32) for z in (p, s, l, q)]
    return {"yp": out[0], "ys": out[1], "yl": out[2], "yq": out[3], "ye": e.reshape(N, 128, PG).astype(np.float32).astype(BF)}

@@ -1,0 +1,603 @@
+import numpy as np
+from concourse.mybir import AluOpType as OP, ActivationFunctionType as AF, AxisListType as AX
+
+V, H2 = 5, 2
+PCS = 2
+PE_NS, CY_NS, GATH = 0.4167, 0.83, 1.5
+LAT, WAKE = 5.0, 0.08
+SPREAD, SEED, TRIES, TURNS = 2.0, 849, 6, 6
+SC = 2.0 ** 23
+CF, CQ, CP = 8192.0, 2.0 ** 20, 2.0 ** 21
+GATE = 2.0 ** 22
+OMAX = set()
+
+SCRATCH, SEMAPHORES = {}, ["sT", "sV", "sS", "sG", "lsem"]
+
+
+def _buf(name, cols, dtype, where="sbuf"):
+    SCRATCH[name] = (where, [128, cols], dtype)
+
+
+for _n in ("d0", "d1", "d2", "bA0", "bA1", "bB", "bD", "bE"):
+    _buf(_n, 512, "float32", "psum")
+for _t in range(4):
+    _buf("x%d" % _t, 4096 + 16, "bfloat16")
+    _buf("thm%d" % _t, 256, "bfloat16")
+    _buf("wb%d" % _t, 128, "bfloat16")
+for _h in range(2):
+    for _n in ("sg", "lg", "da", "dd", "ra", "rd", "ab", "ac", "ao", "mx"):
+        _buf(_n + str(_h), 2048, "bfloat16")
+    for _n in ("fl", "fz", "absd"):
+        _buf(_n + str(_h), 128, "bfloat16")
+ITMP, FTMP = ("ui", "uj", "z", "zs", "y", "r1", "nw", "t2"), ("m3", "r3", "m1", "ne", "sc")
+_buf("itmp", len(ITMP) * 256, "int32")
+_buf("ftmp", len(FTMP) * 256, "float32")
+_buf("mo", V * 256, "bfloat16")
+_buf("mi", V * 256, "bfloat16")
+_buf("u16l", 7 * 256, "uint16")
+_buf("u16q", 5 * 256, "uint16")
+_buf("lst", 5 * 256, "float32")
+_buf("lh", 6 * 256, "float16")
+_buf("qst", 6 * 256, "float32")
+_buf("qh", 6 * 256, "float16")
+_buf("outs", 4 * 256, "float32")
+for _t in range(V + 1):
+    for _h in range(2):
+        _buf("e%d%d" % (_t, _h), 144, "bfloat16")
+        if _t < V:
+            _buf("eo%d%d" % (_t, _h), 144, "bfloat16")
+            SEMAPHORES.append("rm%d%d" % (_t, _h))
+            if _t:
+                SEMAPHORES.append("re%d%d" % (_t, _h))
+SEMAPHORES += ["rx1", "rx2", "rx3"]
+for _n in ("pl", "sl", "ll", "ql"):
+    _buf("i_" + _n, 256, "int32")
+    _buf("f_" + _n, 256, "float16")
+_buf("i_tw", 2, "int32")
+_buf("i_th", 2, "int32")
+_buf("ka", 128, "float16")
+_buf("k37", 128, "float32")
+_buf("acol", 2, "int32")
+_buf("cnt", 1, "float32")
+_buf("onec", 128, "bfloat16")
+_buf("one32", 128, "float32")
+_buf("i32", 128, "float32")
+_buf("i16", 128, "float16")
+_buf("n16", 128, "float16")
+for _n in ("one", "ib", "nib", "i1024", "im512", "bt", "b128"):
+    _buf(_n, 128, "bfloat16")
+_buf("msk", 2048 // PCS, "bfloat16")
+_buf("mskk", 2048 // PCS, "bfloat16")
+_buf("fun", 96, "bfloat16")
+_buf("rowb", 256, "bfloat16")
+_buf("rowlo", 512, "bfloat16")
+LOADS = ["sl", "xt", "pl", "th", "wt", "ll", "ql", "ed0", "ed1"]
+STORES = ["%s%d" % (_n, _h) for _n in ("yp", "ys", "yl", "yq", "ye") for _h in range(2)]
+SEMAPHORES += ["d_" + _n for _n in LOADS + STORES]
+
+
+class _Bank(dict):
+    pass
+
+
+def _plan(g, core, T, topo):
+    rank, N = T.rank_of(core), len(T.cores)
+    ops, last_w, readers, accs, banks, half = [], {}, {}, {}, {}, ["0"]
+
+    def op(q, cost, fns, r=(), w=(), a=(), b=(), sig=None, lat=0.0, after=()):
+        o = {"q": q, "c": cost, "f": fns, "d": {}, "sig": sig, "lat": lat, "i": len(ops), "n": (list(w) + list(a) + list(r) + ["?"])[0]}
+        for x in after:
+            o["d"][x["i"]] = 1
+        r, w, a, b = [[k + half[0] if k in ("A", "A1", "bA") else k for k in ks] for ks in (r, w, a, b)]
+        for k in r:
+            for x in [last_w.get(k)] + accs.get(k, []):
+                if x is not None:
+                    o["d"][x["i"]] = 1
+        for k in a:
+            if last_w.get(k) is not None:
+                o["d"][last_w[k]["i"]] = 1
+            for x in readers.get(k, []):
+                o["d"][x["i"]] = 1
+        for k in w:
+            for x in [last_w.get(k)] + accs.get(k, []) + readers.get(k, []):
+                if x is not None:
+                    o["d"][x["i"]] = 1
+        for k in r:
+            readers.setdefault(k, []).append(o)
+        for k in a:
+            accs.setdefault(k, []).append(o)
+        for k in w:
+            last_w[k], accs[k], readers[k] = o, [], []
+        for k in b:
+            bk = banks.setdefault(k, {"q": None, "cur": [], "prev": []})
+            if bk["q"] != q:
+                bk["q"], bk["prev"], bk["cur"] = q, bk["cur"], []
+            for x in bk["prev"]:
+                o["d"][x["i"]] = 1
+            bk["cur"].append(o)
+        o["d"].pop(o["i"], None)
+        ops.append(o)
+        return o
+
+    def vec(n, cyc=1.0):
+        return max(64.0, n * cyc) * CY_NS / 1000
+
+    def mm(fns, cyc, **kw):
+        return op("T", cyc * PE_NS / 1000, fns, **kw)
+
+    def MM(out, lhsT, rhs, start, stop):
+        return lambda: g.tensor.matmul(out, lhsT, rhs, start, stop)
+
+    def v(fn, n, cyc=1.0, **kw):
+        return op("V", vec(n, cyc), [fn], **kw)
+
+    def s(fn, n, **kw):
+        return op("S", vec(n), [fn], **kw)
+
+    def tt(out, a, b, o):
+        return lambda: g.vector.tensor_tensor(out, a, b, o)
+
+    def ts(out, a, s1, o1, s2=None, o2=None):
+        if o2 is None:
+            return lambda: g.vector.tensor_scalar(out, a, s1, None, o1)
+        return lambda: g.vector.tensor_scalar(out, a, s1, s2, o1, o2)
+
+    def cp(out, a):
+        return lambda: g.vector.tensor_copy(out, a)
+
+    def act(out, a, f, bias=0.0, scale=1.0):
+        return lambda: g.scalar.activation(out, a, f, bias=bias, scale=scale)
+
+    def load(name, out, in_, key):
+        return op("Y", 0.1, [lambda: g.sync.dma_start(out, in_)], w=[key], sig=("d_" + name, 16), lat=4.0 if name == "xt" else 2.2)
+
+    def send(name, out, in_, dst, eng, key, lat, rkey, after=()):
+        eng = [e for e in eng]
+        m = sum(1 << e for e in eng)
+        rid, pid, _ = topo.addr(dst)
+        so = op("G", 1.3, [lambda: g.remote_dma(out, in_, T.sem[name], T.sem["lsem"], pid, rid, m)], r=[key], sig=("send", len(eng)), after=after)
+        op("R", 0.0, [], w=[rkey], sig=(name, len(eng)), after=[so], lat=lat)
+        return so
+
+    def dst(k):
+        return T.cores[(rank + k) % N]
+
+    def cb(name, i, h, n=128):
+        c = i * 256 + h * 128
+        return T[name][:, c:c + n]
+
+    load("sl", T.i_sl[:], T.sl[:], "i_sl")
+    load("xt", T.x0[:, 0:4096], T.xt[:], "x0")
+    load("pl", T.i_pl[:], T.pl[:], "i_pl")
+    load("th", T.i_tw[:, 0:1], T.th[:], "i_th")
+    load("wt", T.i_tw[:, 1:2], T.wt[:], "i_wt")
+    load("ll", T.i_ll[:], T.ll[:], "i_ll")
+    load("ql", T.i_ql[:], T.ql[:], "i_ql")
+    load("ed0", T.e00[:, 0:128], T.ed[:, 0:128], "e00")
+    load("ed1", T.e01[:, 0:128], T.ed[:, 128:256], "e01")
+    ms = lambda ap, c: (lambda: g.vector.memset(ap, c))
+    v(ms(T.one32[:], 1.0), 128, w=["one32"])
+    v(ms(T.one[:], 1.0), 128, 0.5, w=["one"])
+    v(ms(T.onec[:], 1.0 / GATE), 128, 0.5, w=["onec"])
+    gq = lambda fn, n, **kw: op("G", 0.2 + n * 2 * CY_NS / 1000, [fn], **kw)
+    gq(lambda: g.affine_select(T.i32[:], T.one32[:], [[-1, 128]], OP.is_equal, 0.0, 0, 1), 128, r=["one32"], w=["i32"])
+    gq(lambda: g.affine_select(T.bt[:], T.one[:], [[-16, 8], [0, 16]], OP.is_ge, 0.0, 0, 1), 128, r=["one"], w=["bt"])
+    gq(lambda: g.affine_select(T.b128[:], T.bt[:], [[16, 8], [0, 16]], OP.is_ge, 0.0, 15, -1), 128, r=["bt"], w=["b128"])
+    gq(lambda: g.iota(T.mskk[:], [[0, 128 // PCS], [1, 16]], 0, 0, allow_small_or_imprecise_dtypes=True), 2048 // PCS, w=["mskk"])
+    gq(lambda: g.iota(T.k37[:], [[0, 8], [37, 16]], 0, 0, allow_small_or_imprecise_dtypes=True), 128, w=["k37"])
+    for nm, c in (("ib", 1.0), ("nib", -1.0), ("i1024", 1024.0 / GATE), ("im512", -512.0 / GATE), ("i16", 1.0), ("n16", -1.0)):
+        if nm in ("i16", "n16"):
+            v(ts(T[nm][:], T.i32[:], c, OP.mult), 128, r=["i32"], w=[nm])
+        else:
+            s(act(T[nm][:], T.i32[:], AF.Copy, 0.0, c), 128, r=["i32"], w=[nm])
+    v(ts(T.msk[:], T.mskk[:], 0.0, OP.is_gt), 2048 // PCS, 0.5, r=["mskk"], w=["msk"])
+    FUN = {"ab": (0, 24), "ac": (24, 40), "ra": (40, 48), "da": (48, 56), "rd": (56, 64), "dd": (64, 72), "ao": (72, 80)}
+    for i, c in enumerate((SC, SC, -2.0, -SC, 2.0, -2.0, 1.0, -2 * SC, SC, SC, 2 * SC, -SC)):
+        s(act(T.fun[:, 8 * i:8 * i + 8], T.b128[:, 0::16], AF.Copy, 0.0, c), 8, r=["b128"], w=["fun%d" % i])
+    for nm, a, b, c in (("rowlo", 0, 256, -SC / 2), ("rowlo", 256, 384, 0.0), ("rowlo", 384, 512, SC / 2),
+                        ("rowb", 0, 128, 2048.0), ("rowb", 128, 256, 2048.0 + CF)):
+        v(ms(T[nm][0:1, a:b], c), b - a, w=[nm + str(a)])
+    for h in range(H2):
+        v(ms(T["fz%d" % h][:], 0.0), 128, 0.5, w=["fz0%d" % h])
+    CK = ["rowlo0", "rowlo256", "rowlo384"]
+    CB_ = ["rowb0", "rowb128"]
+    FK = ["fun%d" % i for i in range(12)]
+    one_row = T.one[0:1, :]
+    v(ts(T.i_th[:, 0:1], T.i_tw[:, 0:1], 4, OP.arith_shift_right), 1, r=["i_th"], w=["thh"])
+    v(ts(T.i_th[:, 1:2], T.i_tw[:, 0:1], 15, OP.bitwise_and), 1, r=["i_th"], w=["thl"])
+    v(ms(T.x0[:, 4096:4112], 0.0), 16, w=["xe0"])
+    v(ts(T.x0[:, 4096:4097], T.i_th[:, 0:1], -SC * 16, OP.mult), 1, r=["thh"], w=["xe0"])
+    v(ts(T.x0[:, 4097:4098], T.i_th[:, 1:2], -SC, OP.mult), 1, r=["thl"], w=["xe0"])
+    v(cp(T.x0[:, 4098:4099], T.i_tw[:, 1:2]), 1, r=["i_wt"], w=["xe0"])
+    tab_ready = [o for o in ops if o["i"] in (last_w["x0"]["i"], last_w["xe0"]["i"])]
+
+    first = {}
+
+    def relayed(home, t):
+        c, c1, c0 = T.cores[home], T.cores[(home + 1) % N], T.cores[(home + t) % N]
+        return t > 1 and topo.chip(c) != topo.chip(c0) and topo.chip(c) == topo.chip(c1)
+
+    def send_table(t, after):
+        def tab_engines(a, b):
+            en = topo.engines(a, b)
+            return en if len(en) >= 16 or t == 1 else en[0:8:2]
+
+        back = (rank - t) % N
+        outs = [] if relayed(back, t) else [(T.cores[back], "x0", tab_ready)]
+        if relayed((rank - 1) % N, t):
+            outs.append((dst(-1), "x%d" % (t - 1), []))
+        for d, src, rd in outs:
+            en = tab_engines(core, d)
+            m = sum(1 << k for k in en)
+            rid, pid, _ = topo.addr(d)
+            op("G", 1.3, [lambda src=src, rid=rid, pid=pid, m=m: g.remote_dma(T["x%d" % t][:], T[src][:], T.sem["rx%d" % t], T.sem["lsem"], pid, rid, m)],
+               r=[src], sig=("send", len(en)), after=rd + (after if src == "x0" else [first[(t - 2, 1)]]))
+        frm = dst(1) if relayed(rank, t) else dst(t)
+        op("R", 0.0, [], w=["x%d" % t], sig=("rx%d" % t, len(tab_engines(frm, core))), after=tab_ready + after, lat=16.0 if t == 1 else 30.0)
+
+    send_table(1, [])
+    for nm, i in (("sl", 1), ("pl", 0), ("ll", 2)):
+        v(cp(T.u16l[:, 256 * i:256 * i + 256], T["i_" + nm][:]), 256, r=["i_" + nm], w=["u16l%d0" % i, "u16l%d1" % i])
+    v(cp(T.u16q[:, 0:256], T.i_ql[:]), 256, r=["i_ql"], w=["u16q00", "u16q01"])
+    for nm in ("ll", "ql", "pl", "sl"):
+        v(ts(T["f_" + nm][:], T["i_" + nm][:], 2048.0, OP.subtract), 256, r=["i_" + nm], w=["f_" + nm])
+
+    def first_page_form(h):
+        hs = slice(128 * h, 128 * h + 128)
+        for c, nm in enumerate(("ll", "ql", "pl", "sl")):
+            mm([MM(T.bE[:, 128 * c:128 * c + 128], T["f_" + nm][:, hs], T.i16[:], True, True)], 128, r=["f_" + nm, "i16"], w=["bE%d" % c], b=["bE"])
+        v(cp(cb("lh", 0, h), T.bE[:, 0:128]), 128, r=["bE0"], w=["lh0%d" % h], b=["bE"])
+        v(cp(cb("qh", 0, h), T.bE[:, 128:256]), 128, r=["bE1"], w=["qh0%d" % h], b=["bE"])
+        s(act(cb("qst", 0, h), T.bE[:, 128:256], AF.Copy, CQ + 2048.0), 128, r=["bE1"], w=["qst0%d" % h], b=["bE"])
+        for i, c in ((2, 0), (0, 2), (1, 3)):
+            s(act(cb("lst", i, h), T.bE[:, 128 * c:128 * c + 128], AF.Copy, CP + 2048.0), 128, r=["bE%d" % c], w=["lst%d%d" % (i, h)], b=["bE"])
+
+    P = 2048 // PCS
+    dn = [0]
+
+    def tabs(t):
+        x = "x%d" % t
+        e = ["xe0"] if t == 0 else [x]
+        late = [first[(t - 1, 1)]] if t else []
+        v(ts(T["thm%d" % t][:, 0:128], T.ib[:], T[x][:, 4096:4097], OP.mult), 128, 0.5, r=["ib"] + e, w=["thm%d" % t], after=late)
+        v(ts(T["thm%d" % t][:, 128:256], T.ib[:], T[x][:, 4097:4098], OP.mult), 128, 0.5, r=["ib"] + e, w=["thn%d" % t], after=late)
+        v(ts(T["wb%d" % t][:], T.b128[:], T[x][:, 4098:4099], OP.mult), 128, 0.5, r=["b128"] + e, w=["wb%d" % t], after=late)
+
+    def big(t, h):
+        hh = str(h)
+        x = "x%d" % (t % 4)
+        win = T[x][:, 0:4096]
+        B = {n: T[n + hh] for n in ("sg", "lg", "da", "dd", "ra", "rd", "ab", "ac", "ao", "mx")}
+
+        def off(buf, i, j):
+            c = i * 256 + h * 128 + j * (128 // PCS)
+            return T[buf][:, c:c + 128 // PCS]
+
+        K = lambda n, j: n + hh + "p%d" % j
+        for j in range(PCS):
+            sl = slice(P * j, P * j + P)
+            kw = dict(r=[x, "u16l%d%d" % (t + 1, h)], w=[K("sg", j)])
+            if (t, h) == (0, 0) and j:
+                v(cp(B["sg"][:, sl], win.indirect(off("u16l", t + 1, j))), P * GATH, **kw)
+            else:
+                s(act(B["sg"][:, sl], win.indirect(off("u16l", t + 1, j)), AF.Copy), P * GATH, **kw)
+        for j in range(PCS):
+            sl = slice(P * j, P * j + P)
+            s(act(B["lg"][:, sl], win.indirect(off("u16l", t + 2, j)), AF.Copy), P * GATH, r=[x, "u16l%d%d" % (t + 2, h)], w=[K("lg", j)])
+        for j in range(PCS):
+            sl = slice(P * j, P * j + P)
+            o = v(tt(B["da"][:, sl], win.indirect(off("u16l", t, j)), B["sg"][:, sl], OP.subtract), P * GATH,
+                  r=[x, "u16l%d%d" % (t, h), K("sg", j)], w=[K("da", j)])
+            first[(t, h)] = o
+            v(ts(B["ra"][:, sl], B["da"][:, sl], 0.0, OP.max), P, 0.5, r=[K("da", j)], w=[K("ra", j)])
+        for j in range(PCS):
+            sl = slice(P * j, P * j + P)
+            v(lambda a=B["mx"][:, sl], b=B["lg"][:, sl]: g.vector.tensor_tensor_scan(a, T.msk[:], b, 0.0, OP.mult, OP.max), P, 0.5,
+              r=["msk", K("lg", j)], w=[K("mx", j)])
+        mo = "mo%d%d" % (t, h)
+        v(cp(cb("mo", t, h), B["mx"][:, 15::16]), 128, 0.5, r=[K("mx", j) for j in range(PCS)], w=[mo])
+        d2 = dst(2)
+        send("rm%d%d" % (t, h), cb("mi", t, h), cb("mo", t, h), d2, topo.engines(core, d2)[1:8:2], mo, LAT, "mi%d%d" % (t, h))
+        for j in range(PCS):
+            sl = slice(P * j, P * j + P)
+            v(tt(B["dd"][:, sl], win.indirect(off("u16q", t, j)), B["sg"][:, sl], OP.subtract), P * GATH,
+              r=[x, "u16q%d%d" % (t, h), K("sg", j)], w=[K("dd", j)])
+            v(ts(B["rd"][:, sl], B["dd"][:, sl], 0.0, OP.max), P, 0.5, r=[K("dd", j)], w=[K("rd", j)])
+        def size_b(j):
+            d, sl, gp = "d%d" % (dn[0] % 3), slice(512 * j, 512 * j + 512), 512 * j // P
+            for nm, mat, st, sp in (("sg", "ib", True, False), ("lg", "nib", False, True)):
+                mm([MM(T[d][:], T[mat][:], B[nm][:, sl], st, sp)], 512, r=[K(nm, gp), mat] + ([] if st else [d]), w=[d], b=[d])
+            s(act(B["ab"][:, sl], T[d][:], AF.Abs), 512, r=[d], w=["ab%sp%d" % (hh, j)], b=[d])
+            dn[0] += 1
+
+        def size_c(j):
+            d, sl, gp = "d%d" % (dn[0] % 3), slice(512 * j, 512 * j + 512), 512 * j // P
+            for nm, mat in (("sg", "ib"), ("da", "ib"), ("lg", "nib")):
+                mm([MM(T[d][:], T[mat][:], B[nm][:, sl], nm == "sg", nm == "lg")], 512, r=[K(nm, gp), mat] + ([] if nm == "sg" else [d]), w=[d], b=[d])
+            s(act(B["ac"][:, sl], T[d][:], AF.Abs), 512, r=[d], w=["ac%sp%d" % (hh, j)], b=[d])
+            dn[0] += 1
+
+        for j in range(4):
+            size_b(j)
+        for j in range(4):
+            size_c(j)
+        e = "e%d%d" % (t, h)
+        for j in range(4):
+            d = "d%d" % ((dn[0] + j) % 3)
+            if (t, h, j) in OMAX:
+                mm([MM(T[d][:, 0:128], T.ib[:], T[e][:, 0:128], True, True)], 128, r=[e, "ib"], w=[d], b=[d])
+                for i in range(4):
+                    k = 4 * j + i
+                    v(tt(B["ao"][:, 128 * k:128 * k + 128], B["lg"][:, k::16], T[d][:, 0:128], OP.max), 128,
+                      r=[K("lg", jj) for jj in range(PCS)] + [d], w=["ao%sp%dk%d" % (hh, j, i)], b=[d])
+                continue
+            fn = []
+            for i in range(4):
+                o_ = T[d][:, 128 * i:128 * i + 128]
+                fn += [MM(o_, T.ib[:], B["lg"][:, 4 * j + i::16], True, False), MM(o_, T.nib[:], T[e][:, 0:128], False, True)]
+            mm(fn, 1024, r=[K("lg", jj) for jj in range(PCS)] + [e, "ib", "nib"], w=[d], b=[d])
+            s(act(B["ao"][:, 512 * j:512 * j + 512], T[d][:], AF.Abs), 512, r=[d], w=["ao%sp%d" % (hh, j)], b=[d])
+        dn[0] += 4
+
+    def logic(t, h):
+        hh, n = str(h), 128
+        tm = t % 4
+        B = {nm: T[nm + hh] for nm in ("lg", "da", "dd", "ra", "rd", "ab", "ac", "ao")}
+        A, Bb, D, E = T["bA" + hh], T.bB, T.bD, T.bE
+        half[0] = hh
+        k_ = lambda nm: nm + hh
+        pcs = lambda nm: [nm + hh + "p%d" % j for j in range(4 if nm[0] == "a" else PCS)]
+        fl = T["fl" + hh]
+        it = lambda nm: cb("itmp", ITMP.index(nm), h)
+        ft = lambda nm: cb("ftmp", FTMP.index(nm), h)
+        e, eo, mi = "e%d%d" % (t, h), "eo%d%d" % (t, h), "mi%d%d" % (t, h)
+        if t == 0:
+            first_page_form(h)
+        mm([MM(A[:], one_row, T.rowlo[0:1, :], True, False)], 512, r=["one"] + CK, w=["A"], b=["bA"])
+        mm([MM(A[:, 384:512], T.one[:], T["thm%d" % tm][:, 0:128], False, False)], 128, r=["one", "thm%d" % tm], a=["A"], b=["bA"])
+
+        def sums(nm, a, b):
+            fn = []
+            for k in range(16):
+                lt = B[nm][:, 128 * k:128 * k + 128] if nm == "ao" else B[nm][:, k::16]
+                if nm == "ao" and (t, h, k // 4) in OMAX:
+                    fn.append(MM(A[:, a + k:b:16], lt, T.fun[:, 80:88], False, False))
+                    mm([MM(A[:, a + k:b:16], B["lg"][:, k::16], T.fun[:, 88:96], False, False),
+                        MM(A[:, a + k:b:16], T[e][:, 0:128], T.fun[:, 88:96], False, False)], 128, r=pcs("lg") + [e] + FK, a=["A"], b=["bA"])
+                else:
+                    fn.append(MM(A[:, a + k:b:16], lt, T.fun[:, FUN[nm][0]:FUN[nm][1]], False, False))
+            rr = pcs(nm)
+            if nm == "ao":
+                for j in range(4):
+                    if (t, h, j) in OMAX:
+                        rr += ["ao%sp%dk%d" % (hh, j, i) for i in range(4)]
+            mm(fn, 64 * len(fn), r=rr + FK, a=["A"], b=["bA"])
+
+        sums("ra", 256, 384)
+        sums("da", 256, 384)
+        sums("rd", 0, 128)
+        sums("dd", 0, 128)
+        sums("ab", 0, 384)
+        sums("ac", 128, 384)
+        sums("ao", 384, 512)
+        mm([MM(A[:, 384:512], T.one[:], T["thm%d" % tm][:, 128:256], False, True)], 128, r=["one", "thn%d" % tm], w=["A"], b=["bA"])
+        X2, X1, XF, X3 = [A[:, 128 * i:128 * i + 128] for i in range(4)]
+        mm([MM(D[:, 0:128], T[e][:, 0:128], T["wb%d" % tm][:], True, True)], 128, r=[e, "wb%d" % tm], w=["Du"], b=["bD"])
+        if h == 0:
+            if t == 0:
+                v(cp(T.ka[:], T.k37[:]), n, r=["k37"], w=["ka"])
+            else:
+                v(ts(T.ka[:], T.k37[:], T["e%d1" % t][:, 128:129], OP.add), n, r=["k37", "e%d1" % t], w=["ka"])
+        lh, qo = cb("lh", t, h), cb("qst", t, h)
+        PL, PY, PLQ = [Bb[:, 128 * i:128 * i + 128] for i in range(3)]
+        mm([MM(PL, one_row, T.rowb[0:1, 0:128], True, False), MM(PL, T.i16[:], lh, False, True),
+            MM(PY, one_row, T.rowb[0:1, 128:256], True, False), MM(PY, T.i16[:], lh, False, False), MM(PY, T.i16[:], T.ka[:], False, True),
+            MM(PLQ, T.i16[:], lh, True, False), MM(PLQ, T.n16[:], cb("qh", t, h), False, True)], 7 * 128,
+           r=["one", "i16", "n16", "lh%d%d" % (t, h), "qh%d%d" % (t, h), "ka"] + CB_, w=["B"], b=["bB"])
+        v(cp(it("ui"), D[:, 0:128]), n, r=["Du"], w=[k_("ui")], b=["bD"])
+        v(ts(it("uj"), it("ui"), 4095, OP.bitwise_and), n, r=[k_("ui")], w=[k_("uj")])
+        v(tt(it("z"), it("uj"), PL, OP.mult), n, r=[k_("uj"), "B"], w=[k_("z")], b=["bB"])
+        v(ts(it("zs"), it("z"), 5, OP.arith_shift_right), n, r=[k_("z")], w=[k_("zs")])
+        v(tt(it("y"), it("zs"), PY, OP.add), n, r=[k_("zs"), "B"], w=[k_("y")], b=["bB"])
+        ms_, fz = T.msk[:, 0:128], T["fz" + hh]
+        v(lambda: g.vector.tensor_tensor_scan(ft("sc"), ms_, XF, 0.0, OP.mult, OP.add), n, r=["A", "msk"], w=[k_("sc")], b=["bA"])
+        v(ts(fz[:, 0::16], T.ftmp[:, FTMP.index("sc") * 256 + 128 * h + 15:FTMP.index("sc") * 256 + 128 * h + 128:16], 0.0, OP.is_ge, GATE, OP.mult), 8,
+          r=[k_("sc"), "fz0" + hh], w=[k_("fz")])
+        v(lambda: g.vector.tensor_tensor_scan(fl[:], ms_, fz[:], 0.0, OP.mult, OP.add), n, 0.5, r=["msk", k_("fz")], w=[k_("fl") + "a"])
+        FL = [k_("fl") + "a"]
+        mm([MM(D[:, 256:384], T.ib[:], T[e][:, 0:128], True, False), MM(D[:, 256:384], T.nib[:], cb("mi", t, h), False, True)], 256,
+           r=[e, mi, "ib", "nib"], w=["Dd"], b=["bD"])
+        absd = T["absd" + hh][:]
+        s(act(absd, D[:, 256:384], AF.Abs), n, r=["Dd"], w=[k_("absd")], b=["bD"])
+        mm([MM(D[:, 384:512], T.ib[:], T[e][:, 0:128], True, False), MM(D[:, 384:512], T.ib[:], cb("mi", t, h), False, False),
+            MM(D[:, 384:512], fl[:], T.i1024[:], False, True),
+            MM(D[:, 128:256], fl[:], T.im512[:], True, False), MM(D[:, 128:256], T.ib[:], absd, False, True)], 5 * 128,
+           r=FL + [e, mi, k_("absd"), "ib", "im512", "i1024"], w=["De"], b=["bD"])
+        v(ts(it("t2"), D[:, 384:512], 0.5, OP.mult, 512.25, OP.subtract), n, r=["De"], w=[k_("t2")], b=["bD"])
+        v(tt(T[eo][:, 0:128], it("t2"), D[:, 128:256], OP.max), n, r=[k_("t2"), "De"], w=[eo], b=["bD"])
+        if t < V - 1:
+            if h == 1:
+                mm([MM(D[:, 0:8], T.onec[:], T["fl%d" % a][:, 0::16], a == 0, a == 1) for a in range(2)], 128, r=FL + ["fl0a", "onec"], w=["Du"], b=["bD"])
+                v(lambda: g.vector.tensor_reduce(T.cnt[:, 0:1], D[:, 0:8], AX.X, OP.add), 8, r=["Du"], w=["cnt"], b=["bD"])
+                v(ts(T.acol[:, 0:1], T.cnt[:, 0:1], -1.0, OP.mult), 1, r=["cnt"], w=["ac0"])
+                v(ts(T.acol[:, 1:2], T.acol[:, 0:1], 31, OP.bitwise_and), 1, r=["ac0"], w=["ac1"])
+                v(ms(T[eo][:, 128:144], 0.0), 16, w=[eo + "A"])
+                v(cp(T[eo][:, 128:129], T.acol[:, 1:2]), 1, r=["ac1"], w=[eo + "A"])
+            else:
+                v(ms(T[eo][:, 128:144], 0.0), 16, w=[eo + "A"])
+            d1 = dst(-1)
+            en = "e%d%d" % (t + 1, h)
+            send("re%d%d" % (t + 1, h), T[en][:], T[eo][:], d1, topo.engines(core, d1)[1:8:2], eo, LAT, en, after=[last_w[eo + "A"]])
+        else:
+            op("Y", 0.1, [lambda: g.sync.dma_start(T.ye[:, 128 * h:128 * h + 128], T[eo][:, 0:128])], r=[eo], sig=("d_ye%d" % h, 16), lat=2.0)
+        pst = cb("lst", t, h)
+        v(tt(ft("m3"), it("y"), X3, OP.min), n, r=[k_("y"), "A"], w=[k_("m3")], b=["bA"])
+        v(tt(ft("r3"), ft("m3"), PL, OP.max), n, r=[k_("m3"), "B"], w=[k_("r3")], b=["bB"])
+        v(tt(E[:, 0:128], qo, X2, OP.min), n, r=["qst%d%d" % (t, h), "A"], w=["bE0"], b=["bA", "bE"])
+        v(tt(E[:, 128:256], pst, X1, OP.min), n, r=["lst%d%d" % (t, h), "A"], w=["bE1"], b=["bA", "bE"])
+        v(tt(ft("m1"), E[:, 128:256], fl[:], OP.subtract), n, r=FL + ["bE1"], w=[k_("m1")], b=["bE"])
+        v(tt(E[:, 0:128], ft("r3"), E[:, 0:128], OP.max), n, r=[k_("r3"), "bE0"], w=["bE0"], b=["bE"])
+        v(tt(it("r1"), ft("m1"), E[:, 0:128], OP.max), n, r=[k_("m1"), "bE0"], w=[k_("r1")], b=["bE"])
+        nw = it("nw")
+        v(ts(nw, it("r1"), 4095, OP.bitwise_and), n, r=[k_("r1")], w=[k_("nw")])
+        v(ts(cb("lh", t + 1, h), nw, 2048.0, OP.subtract), n, r=[k_("nw")], w=["lh%d%d" % (t + 1, h)])
+        if t + 3 < 5:
+            v(ts(cb("lst", t + 3, h), nw, CP, OP.add), n, r=[k_("nw")], w=["lst%d%d" % (t + 3, h)])
+        qn = cb("qst", t + 1, h)
+        v(tt(ft("ne"), nw, PL, OP.not_equal), n, r=[k_("nw"), "B"], w=[k_("ne")], b=["bB"])
+        v(tt(E[:, 128:256], ft("ne"), PLQ, OP.mult), n, r=[k_("ne"), "B"], w=["bE1"], b=["bB", "bE"])
+        v(tt(qn, qo, E[:, 128:256], OP.add), n, r=["qst%d%d" % (t, h), "bE1"], w=["qst%d%d" % (t + 1, h)], b=["bE"])
+        mm([MM(E[:, 256:384], cb("lh", t + 1, h), T.i16[:], True, True)], 128, r=["i16", "lh%d%d" % (t + 1, h)], w=["bE2"], b=["bE"])
+        if t < V - 1:
+            v(ts(cb("u16l", t + 3, h), E[:, 256:384], 2048.0, OP.add), n, r=["bE2"], w=["u16l%d%d" % (t + 3, h)], b=["bE"])
+        v(ts(cb("qh", t + 1, h), qn, CQ + 2048.0, OP.subtract), n, r=["qst%d%d" % (t + 1, h)], w=["qh%d%d" % (t + 1, h)])
+        mm([MM(E[:, 384:512], cb("qh", t + 1, h), T.i16[:], True, True)], 128, r=["i16", "qh%d%d" % (t + 1, h)], w=["bE3"], b=["bE"])
+        if t < V - 1:
+            v(ts(cb("u16q", t + 1, h), E[:, 384:512], 2048.0, OP.add), n, r=["bE3"], w=["u16q%d%d" % (t + 1, h)], b=["bE"])
+        if t >= 2:
+            o_ = cb("outs", t - 2, h)
+            nm = ("yp", "ys", "yl")[t - 2]
+            s(act(o_, E[:, 256:384], AF.Copy, 2048.0), n, r=["bE2"], w=["outs%d%d" % (t - 2, h)], b=["bE"])
+            op("Y", 0.1, [lambda: g.sync.dma_start(T[nm][:, 128 * h:128 * h + 128], o_)], r=["outs%d%d" % (t - 2, h)], sig=("d_%s%d" % (nm, h), 16), lat=2.0)
+        if t == V - 1:
+            oq = cb("outs", 3, h)
+            s(act(oq, E[:, 384:512], AF.Copy, 2048.0), n, r=["bE3"], w=["outs3%d" % h], b=["bE"])
+            op("Y", 0.1, [lambda: g.sync.dma_start(T.yq[:, 128 * h:128 * h + 128], oq)], r=["outs3%d" % h], sig=("d_yq%d" % h, 16), lat=2.0)
+
+    for t in range(V):
+        if t < 4:
+            tabs(t)
+        for h in range(H2):
+            big(t, h)
+            logic(t, h)
+        if t == 1:
+            send_table(2, [])
+        if t == 2:
+            send_table(3, [first[(0, 1)]])
+    return ops
+
+
+def _order(ops):
+    n = len(ops)
+    pred = [sorted(o["d"]) for o in ops]
+    succ = [[] for _ in range(n)]
+    for i in range(n):
+        for d in pred[i]:
+            succ[d].append(i)
+    q, c, lat = [o["q"] for o in ops], [o["c"] for o in ops], [o["lat"] for o in ops]
+
+    def list_pass(before, after, prio, forward):
+        left = [len(b) for b in before]
+        ready_t = [0.0 if forward or after[i] else lat[i] for i in range(n)]
+        start, free, ready, seq = [0.0] * n, {}, {}, []
+        for i in range(n):
+            if not left[i]:
+                ready.setdefault(q[i], []).append(i)
+        while len(seq) < n:
+            best = None
+            for qq, lst in ready.items():
+                f = free.get(qq, 0.0)
+                for i in lst:
+                    key = (max(f, ready_t[i]), -prio[i], i)
+                    if best is None or key < best:
+                        best = key
+            st, _, i = best
+            ready[q[i]].remove(i)
+            seq.append(i)
+            start[i] = st
+            fin = st + c[i]
+            if q[i] != "R":
+                free[q[i]] = fin
+            for k in after[i]:
+                ready_t[k] = max(ready_t[k], fin + lat[i if forward else k] + WAKE)
+                left[k] -= 1
+                if not left[k]:
+                    ready.setdefault(q[k], []).append(k)
+        return start, seq
+
+    base = [0.0] * n
+    for i in reversed(range(n)):
+        base[i] = max([base[k] for k in succ[i]] + [0.0]) + c[i] + lat[i] + WAKE
+    rs = np.random.RandomState(SEED)
+    best = None
+    for trial in range(TRIES):
+        prio = [float(p + (SPREAD * x if trial else 0.0)) for p, x in zip(base, rs.random_sample(n))]
+        for turn in range(TURNS):
+            start, seq = list_pass(pred, succ, prio, True)
+            span = max(start[i] + c[i] + lat[i] for i in range(n))
+            if best is None or span < best[0] - 1e-9:
+                best = (span, start, seq)
+            back, _ = list_pass(succ, pred, [start[i] + c[i] for i in range(n)], False)
+            prio = [back[i] + c[i] for i in range(n)]
+    order = {}
+    for i in best[2]:
+        ops[i]["st"] = best[1][i]
+        order.setdefault(q[i], []).append(ops[i])
+    return order
+
+
+def rank_program(g, core, T, topo):
+    if T.rank_of(core) is None:
+        return
+    ops = _plan(g, core, T, topo)
+    order = _order(ops)
+    qs = {"T": g.tensor, "V": g.vector, "S": g.scalar, "G": g, "Y": g.sync}
+    qsem = {"T": "sT", "V": "sV", "S": "sS", "G": "sG"}
+    count = {q: 0 for q in qs}
+    known = {q: {} for q in qs}
+    sent = 0
+    glob = [o for q in order for o in order[q]]
+    for q in ("T", "V", "S", "G"):
+        c = 0
+        for o in order[q]:
+            if o["sig"] is None:
+                c += len(o["f"])
+                o["val"] = (qsem[q], c)
+            elif o["sig"][0] == "send":
+                o["val"] = None
+    for q in ("Y", "R"):
+        for o in order[q]:
+            o["val"] = o["sig"]
+    for o in sorted(glob, key=lambda o: (o["st"], o["i"])):
+        o["w"] = []
+        if o["q"] == "R":
+            o["clk"] = {o["val"][0]: o["val"][1]}
+            continue
+        kn = known[o["q"]]
+        need = {}
+        for d in o["d"]:
+            x = ops[d]
+            if x["val"] is None or (x["q"] == "T" and o["q"] == "T"):
+                continue
+            sm, vl = x["val"]
+            if kn.get(sm, 0) < vl and need.get(sm, (0, None))[0] < vl:
+                need[sm] = (vl, x)
+        for sm in sorted(need, key=lambda m: -need[m][1]["st"]):
+            vl, x = need[sm]
+            if kn.get(sm, 0) < vl:
+                o["w"].append((sm, vl))
+                for a, b in list(x["clk"].items()) + [(sm, vl)]:
+                    if kn.get(a, 0) < b:
+                        kn[a] = b
+        o["clk"] = dict(kn)
+        if o["val"] is not None:
+            o["clk"][o["val"][0]] = o["val"][1]
+    for q in qs:
+        eng = qs[q]
+        for o in order.get(q, []):
+            for sm, vl in o["w"]:
+                eng.wait_ge(T.sem[sm], vl)
+            for f in o["f"]:
+                ins = f()
+                if o["sig"] is None:
+                    ins.then_inc(T.sem[qsem[q]], 1)
+                elif o["sig"][0] == "send":
+                    sent += o["sig"][1]
+                else:
+                    ins.then_inc(T.sem[o["sig"][0]], 16)
+    for q in ("T", "V", "S", "G"):
+        tot = max([o["val"][1] for o in order[q] if o["val"] is not None] + [0])
+        g.sync.wait_ge(T.sem[qsem[q]], tot)
+    for nm in STORES:
+        g.sync.wait_ge(T.sem["d_" + nm], 16)
+    g.wait_ge(T.sem["lsem"], sent)

@@ -1,15 +1,59 @@
 import numpy as np
+from concourse.bass import DstId, RemoteDMATransfer
 from concourse.mybir import AluOpType as OP, ActivationFunctionType as AF, AxisListType as AX
 
 V, H2 = 5, 2
 PCS = 2
 PE_NS, CY_NS, GATH = 0.4167, 0.83, 1.5
-LAT, WAKE = 5.0, 0.08
+LAT, WAKE = 5.0, 0.14
 SPREAD, SEED, TRIES, TURNS = 2.0, 849, 6, 6
 SC = 2.0 ** 23
 CF, CQ, CP = 8192.0, 2.0 ** 20, 2.0 ** 21
 GATE = 2.0 ** 22
-OMAX = set()
+START, DFOLD, DSMALL, BACK = 2.0, 3.0, 0.4, 4.4
+LTAB, FIRST = (0.0, 15.0, 24.0, 28.0), 2.0
+XW = 4096 + 16
+EDGE = {"a": ("pg", "sg"), "b": ("sg", "lg"), "c": ("pg", "lg"), "d": ("qg", "sg")}
+TESTS = {"a": (0, 0, -1, 0), "b": (SC, SC, -2, 0), "c": (0, -SC, 2, 0), "d": (-SC, 0, 0, 0), "o": (0, 0, 0, SC)}
+BIAS = 1.0
+
+
+def FOLD(t, h):
+    return "a" if (t, h) == (V - 1, H2 - 1) else "ab"
+
+
+def _weights(t, h):
+    w = {}
+
+    def add(nm, e, c):
+        w[nm] = tuple(a + c * b for a, b in zip(w.get(nm, (0, 0, 0, 0)), TESTS[e]))
+
+    for e, (x, y) in EDGE.items():
+        if e in FOLD(t, h):
+            add("m" + e, e, 2), add(x, e, -1), add(y, e, -1)
+        elif e == "d":
+            add("md", e, 2), add("qg", e, -1)
+        else:
+            add("m" + e, e, 2), add(x, e, -1), add(y, e, 1)
+    add("ao", "o", 2), add("lg", "o", -1)
+    out = {}
+    for nm, c in w.items():
+        nz = [i for i in range(4) if c[i]]
+        if nz:
+            out[nm] = (nz[0], c[nz[0]:nz[-1] + 1])
+    return out
+
+
+RUNS = []
+for _t in range(V):
+    for _h in range(H2):
+        RUNS += [_c for _, _c in _weights(_t, _h).values()]
+COEF = []
+for _c in sorted(set(RUNS), key=lambda c: (-len(c), c)):
+    if not any(tuple(COEF[i:i + len(_c)]) == _c for i in range(len(COEF))):
+        COEF += list(_c)
+LONG = ("sg", "lg", "pg", "qg", "ma", "mb", "mc", "md", "ao", "mx")
+TWICE = ("sg", "pg", "qg")
 
 SCRATCH, SEMAPHORES = {}, ["sT", "sV", "sS", "sG", "lsem"]
 
@@ -18,15 +62,20 @@ def _buf(name, cols, dtype, where="sbuf"):
     SCRATCH[name] = (where, [128, cols], dtype)
 
 
-for _n in ("d0", "d1", "d2", "bA0", "bA1", "bB", "bD", "bE"):
+def _bn(nm, t, h):
+    return nm + str(h) + ("o" if nm in TWICE and t % 2 else "")
+
+
+for _n in ("d0", "d1", "bY", "bA0", "bA1", "bB", "bD", "bE"):
     _buf(_n, 512, "float32", "psum")
 for _t in range(4):
-    _buf("x%d" % _t, 4096 + 16, "bfloat16")
+    _buf("x%d" % _t, XW, "bfloat16")
     _buf("thm%d" % _t, 256, "bfloat16")
     _buf("wb%d" % _t, 128, "bfloat16")
+LANDS = sorted({_bn(_n, _t, _h) for _n in LONG for _t in range(2) for _h in range(2)})
+for _n in LANDS:
+    _buf(_n, 2048, "bfloat16")
 for _h in range(2):
-    for _n in ("sg", "lg", "da", "dd", "ra", "rd", "ab", "ac", "ao", "mx"):
-        _buf(_n + str(_h), 2048, "bfloat16")
     for _n in ("fl", "fz", "absd"):
         _buf(_n + str(_h), 128, "bfloat16")
 ITMP, FTMP = ("ui", "uj", "z", "zs", "y", "r1", "nw", "t2"), ("m3", "r3", "m1", "ne", "sc")
@@ -47,9 +96,10 @@ for _t in range(V + 1):
         if _t < V:
             _buf("eo%d%d" % (_t, _h), 144, "bfloat16")
             SEMAPHORES.append("rm%d%d" % (_t, _h))
+            SEMAPHORES += ["f%s%d%d" % (_e, _t, _h) for _e in FOLD(_t, _h)]
             if _t:
                 SEMAPHORES.append("re%d%d" % (_t, _h))
-SEMAPHORES += ["rx1", "rx2", "rx3"]
+SEMAPHORES += ["rx1", "rx2", "rx3", "px0", "px1", "px2", "px3"]
 for _n in ("pl", "sl", "ll", "ql"):
     _buf("i_" + _n, 256, "int32")
     _buf("f_" + _n, 256, "float16")
@@ -57,27 +107,74 @@ _buf("i_tw", 2, "int32")
 _buf("i_th", 2, "int32")
 _buf("ka", 128, "float16")
 _buf("k37", 128, "float32")
-_buf("acol", 2, "int32")
+_buf("acol", 32, "int32")
 _buf("cnt", 1, "float32")
 _buf("onec", 128, "bfloat16")
 _buf("one32", 128, "float32")
 _buf("i32", 128, "float32")
 _buf("i16", 128, "float16")
 _buf("n16", 128, "float16")
-for _n in ("one", "ib", "nib", "i1024", "im512", "bt", "b128"):
+for _n in ("one", "ib", "nib", "i1024", "im512", "bt", "b128", "bsc"):
     _buf(_n, 128, "bfloat16")
 _buf("msk", 2048 // PCS, "bfloat16")
 _buf("mskk", 2048 // PCS, "bfloat16")
-_buf("fun", 96, "bfloat16")
+_buf("fun", 8 * len(COEF), "bfloat16")
 _buf("rowb", 256, "bfloat16")
 _buf("rowlo", 512, "bfloat16")
-LOADS = ["sl", "xt", "pl", "th", "wt", "ll", "ql", "ed0", "ed1"]
+LOADS = ["sl", "xt0", "xt1", "pl", "th", "wt", "ll", "ql", "ed0", "ed1"]
 STORES = ["%s%d" % (_n, _h) for _n in ("yp", "ys", "yl", "yq", "ye") for _h in range(2)]
 SEMAPHORES += ["d_" + _n for _n in LOADS + STORES]
 
 
-class _Bank(dict):
-    pass
+def _helpers(T, topo):
+    port, hands = {}, {}
+    for c in T.cores:
+        free = [k for k in topo.cores_of(c) if T.rank_of(k) is None and topo.die(k) == topo.die(c)]
+        p = [k for k in free if all(topo.may_write(k, o) for o in T.cores)][0]
+        port.setdefault(topo.chip(c), {})[topo.die(c)] = p
+        hands[c] = [k for k in free if k != p]
+    return port, hands
+
+
+def _piece(ap, i):
+    return ap[:, i * XW // 2:(i + 1) * XW // 2]
+
+
+def _write(g, T, topo, items):
+    trs = []
+    for srcs, (c, d), en, sem in items:
+        rid, pid, _ = topo.addr(c)
+        trs.append(RemoteDMATransfer(dst_ids=[DstId(rid=rid, pnc=pid)], dma_engine_mask=sum(1 << e for e in en), remote_sem=T.sem[sem],
+                                     srcs=srcs, dsts=[d], alu_op=2 if len(srcs) > 1 else 0))
+    return g.remote_dma_fused(trs, local_sem=T.sem["lsem"])
+
+
+def _port_program(g, core, T, topo, die):
+    port, _ = _helpers(T, topo)
+    N, chip = len(T.cores), topo.chip(core)
+    here = [r for r in range(N) if topo.chip(T.cores[r]) == chip]
+    far = [r for r in range(N) if r not in here]
+    off = topo.engines(core, T.cores[far[0]])
+    on = [e for e in topo.engines(core, T.cores[here[0]]) if e not in off]
+    i = sorted(port[chip]).index(die)
+    jobs = [sorted(((r - h) % N, r, h, en) for r in here for h in homes if h != r) for homes, en in ((far, off), (here, on))]
+    for r in here:
+        g.wait_ge(T.sem["px%d" % r], 8)
+    for k in range(max(len(j) for j in jobs)):
+        _write(g, T, topo, [([_piece(T["x%d" % r], i)], (T.cores[h], _piece(T["x%d" % t], i)), en, "rx%d" % t)
+                            for t, r, h, en in [j[k] for j in jobs if k < len(j)]])
+    g.wait_ge(T.sem["lsem"], sum(len(j[3]) for js in jobs for j in js))
+
+
+def _hand_program(g, core, T, topo, owner, calls):
+    sent = 0
+    en = topo.engines(core, owner)
+    for c, land, sem, cnt, back in calls:
+        if c == core:
+            g.wait_ge(T.sem[sem], cnt)
+            _write(g, T, topo, [([T[land][:]], (owner, T[back][:]), en, sem)])
+            sent += len(en)
+    g.wait_ge(T.sem["lsem"], sent)
 
 
 def _plan(g, core, T, topo):
@@ -110,7 +207,7 @@ def _plan(g, core, T, topo):
             last_w[k], accs[k], readers[k] = o, [], []
         for k in b:
             bk = banks.setdefault(k, {"q": None, "cur": [], "prev": []})
-            if bk["q"] != q:
+            if bk["q"] != q or q == "X":
                 bk["q"], bk["prev"], bk["cur"] = q, bk["cur"], []
             for x in bk["prev"]:
                 o["d"][x["i"]] = 1
@@ -134,6 +231,20 @@ def _plan(g, core, T, topo):
     def s(fn, n, **kw):
         return op("S", vec(n), [fn], **kw)
 
+    def vs(fv, fs, n, **kw):
+        o = op("X", vec(n), None, **kw)
+        o["alt"] = {"V": [fv], "S": [fs]}
+        return o
+
+    def scaled(out, a, c, n, **kw):
+        return vs(ts(out, a, float(c), OP.mult), act(out, a, AF.Copy, 0.0, float(c)), n, **kw)
+
+    def shifted(out, a, c, n, **kw):
+        return vs(ts(out, a, float(c), OP.add), act(out, a, AF.Copy, float(c)), n, **kw)
+
+    def relu(out, a, n, **kw):
+        return vs(ts(out, a, 0.0, OP.max), act(out, a, AF.Relu), n, **kw)
+
     def tt(out, a, b, o):
         return lambda: g.vector.tensor_tensor(out, a, b, o)
 
@@ -149,13 +260,14 @@ def _plan(g, core, T, topo):
         return lambda: g.scalar.activation(out, a, f, bias=bias, scale=scale)
 
     def load(name, out, in_, key):
-        return op("Y", 0.1, [lambda: g.sync.dma_start(out, in_)], w=[key], sig=("d_" + name, 16), lat=4.0 if name == "xt" else 2.2)
+        return op("Y", 0.1, [lambda: g.sync.dma_start(out, in_)], w=[key], sig=("d_" + name, 16), lat=3.6 if name[:2] == "xt" else 2.2)
 
     def send(name, out, in_, dst, eng, key, lat, rkey, after=()):
         eng = [e for e in eng]
         m = sum(1 << e for e in eng)
         rid, pid, _ = topo.addr(dst)
         so = op("G", 1.3, [lambda: g.remote_dma(out, in_, T.sem[name], T.sem["lsem"], pid, rid, m)], r=[key], sig=("send", len(eng)), after=after)
+        so["dma"] = DSMALL
         op("R", 0.0, [], w=[rkey], sig=(name, len(eng)), after=[so], lat=lat)
         return so
 
@@ -167,7 +279,8 @@ def _plan(g, core, T, topo):
         return T[name][:, c:c + n]
 
     load("sl", T.i_sl[:], T.sl[:], "i_sl")
-    load("xt", T.x0[:, 0:4096], T.xt[:], "x0")
+    load("xt1", T.x0[:, XW // 2:4096], T.xt[:, XW // 2:4096], "x0b")
+    load("xt0", T.x0[:, 0:XW // 2], T.xt[:, 0:XW // 2], "x0")
     load("pl", T.i_pl[:], T.pl[:], "i_pl")
     load("th", T.i_tw[:, 0:1], T.th[:], "i_th")
     load("wt", T.i_tw[:, 1:2], T.wt[:], "i_wt")
@@ -189,11 +302,11 @@ def _plan(g, core, T, topo):
         if nm in ("i16", "n16"):
             v(ts(T[nm][:], T.i32[:], c, OP.mult), 128, r=["i32"], w=[nm])
         else:
-            s(act(T[nm][:], T.i32[:], AF.Copy, 0.0, c), 128, r=["i32"], w=[nm])
+            scaled(T[nm][:], T.i32[:], c, 128, r=["i32"], w=[nm])
+    scaled(T.bsc[:], T.b128[:], SC, 128, r=["b128"], w=["bsc"])
     v(ts(T.msk[:], T.mskk[:], 0.0, OP.is_gt), 2048 // PCS, 0.5, r=["mskk"], w=["msk"])
-    FUN = {"ab": (0, 24), "ac": (24, 40), "ra": (40, 48), "da": (48, 56), "rd": (56, 64), "dd": (64, 72), "ao": (72, 80)}
-    for i, c in enumerate((SC, SC, -2.0, -SC, 2.0, -2.0, 1.0, -2 * SC, SC, SC, 2 * SC, -SC)):
-        s(act(T.fun[:, 8 * i:8 * i + 8], T.b128[:, 0::16], AF.Copy, 0.0, c), 8, r=["b128"], w=["fun%d" % i])
+    for i, c in enumerate(COEF):
+        scaled(T.fun[:, 8 * i:8 * i + 8], T.b128[:, 0::16], c, 8, r=["b128"], w=["fun%d" % i])
     for nm, a, b, c in (("rowlo", 0, 256, -SC / 2), ("rowlo", 256, 384, 0.0), ("rowlo", 384, 512, SC / 2),
                         ("rowb", 0, 128, 2048.0), ("rowb", 128, 256, 2048.0 + CF)):
         v(ms(T[nm][0:1, a:b], c), b - a, w=[nm + str(a)])
@@ -201,7 +314,6 @@ def _plan(g, core, T, topo):
         v(ms(T["fz%d" % h][:], 0.0), 128, 0.5, w=["fz0%d" % h])
     CK = ["rowlo0", "rowlo256", "rowlo384"]
     CB_ = ["rowb0", "rowb128"]
-    FK = ["fun%d" % i for i in range(12)]
     one_row = T.one[0:1, :]
     v(ts(T.i_th[:, 0:1], T.i_tw[:, 0:1], 4, OP.arith_shift_right), 1, r=["i_th"], w=["thh"])
     v(ts(T.i_th[:, 1:2], T.i_tw[:, 0:1], 15, OP.bitwise_and), 1, r=["i_th"], w=["thl"])
@@ -209,33 +321,32 @@ def _plan(g, core, T, topo):
     v(ts(T.x0[:, 4096:4097], T.i_th[:, 0:1], -SC * 16, OP.mult), 1, r=["thh"], w=["xe0"])
     v(ts(T.x0[:, 4097:4098], T.i_th[:, 1:2], -SC, OP.mult), 1, r=["thl"], w=["xe0"])
     v(cp(T.x0[:, 4098:4099], T.i_tw[:, 1:2]), 1, r=["i_wt"], w=["xe0"])
-    tab_ready = [o for o in ops if o["i"] in (last_w["x0"]["i"], last_w["xe0"]["i"])]
-
     first = {}
+    port, hands = _helpers(T, topo)
+    pc = [port[topo.chip(core)][d] for d in sorted(port[topo.chip(core)])]
+    every = topo.engines(core, pc[0])
+    so = op("G", 1.3, [lambda: _write(g, T, topo, [([_piece(T.x0, i)], (pc[i], _piece(T["x%d" % rank], i)), every[8 * i:8 * i + 8], "px%d" % rank)
+                                                   for i in range(2)])], r=["x0", "x0b", "xe0"], sig=("send", 16))
+    so["dma"] = DFOLD
+    for t in range(1, N):
+        op("R", 0.0, [], w=["x%d" % t], sig=("rx%d" % t, 16), after=[so], lat=LTAB[t])
+    landed = {c: 0 for c in hands[core]}
 
-    def relayed(home, t):
-        c, c1, c0 = T.cores[home], T.cores[(home + 1) % N], T.cores[(home + t) % N]
-        return t > 1 and topo.chip(c) != topo.chip(c0) and topo.chip(c) == topo.chip(c1)
+    def fold(t, h, edges):
+        n, items, calls = 16 // len(edges), [], []
+        for i, e in enumerate(edges):
+            c = hands[core][(i + h) % 2]
+            land = LANDS[landed[c]]
+            landed[c] += 1
+            items.append(([T[_bn(x, t, h)][:] for x in EDGE[e]], (c, T[land][:]), every[n * i:n * i + n], "f%s%d%d" % (e, t, h)))
+            calls.append((c, land, "f%s%d%d" % (e, t, h), n, _bn("m" + e, t, h)))
+        rd = {e: [_bn(x, t, h) + "p%d" % j for x in EDGE[e] for j in range(PCS)] for e in edges}
+        wr = {e: [_bn("m" + e, t, h) + "p%d" % j for j in range(4)] for e in edges}
+        so = op("G", 1.3, [lambda: _write(g, T, topo, items)], r=sum(rd.values(), []), w=sum(wr.values(), []), sig=("send", 16))
+        so["calls"], so["dma"] = calls, DFOLD * len(edges)
+        for e in edges:
+            op("R", 0.0, [], r=rd[e], w=wr[e], sig=("f%s%d%d" % (e, t, h), 16), after=[so], lat=START + so["dma"] + BACK + (FIRST if t == 0 else 0.0))
 
-    def send_table(t, after):
-        def tab_engines(a, b):
-            en = topo.engines(a, b)
-            return en if len(en) >= 16 or t == 1 else en[0:8:2]
-
-        back = (rank - t) % N
-        outs = [] if relayed(back, t) else [(T.cores[back], "x0", tab_ready)]
-        if relayed((rank - 1) % N, t):
-            outs.append((dst(-1), "x%d" % (t - 1), []))
-        for d, src, rd in outs:
-            en = tab_engines(core, d)
-            m = sum(1 << k for k in en)
-            rid, pid, _ = topo.addr(d)
-            op("G", 1.3, [lambda src=src, rid=rid, pid=pid, m=m: g.remote_dma(T["x%d" % t][:], T[src][:], T.sem["rx%d" % t], T.sem["lsem"], pid, rid, m)],
-               r=[src], sig=("send", len(en)), after=rd + (after if src == "x0" else [first[(t - 2, 1)]]))
-        frm = dst(1) if relayed(rank, t) else dst(t)
-        op("R", 0.0, [], w=["x%d" % t], sig=("rx%d" % t, len(tab_engines(frm, core))), after=tab_ready + after, lat=16.0 if t == 1 else 30.0)
-
-    send_table(1, [])
     for nm, i in (("sl", 1), ("pl", 0), ("ll", 2)):
         v(cp(T.u16l[:, 256 * i:256 * i + 256], T["i_" + nm][:]), 256, r=["i_" + nm], w=["u16l%d0" % i, "u16l%d1" % i])
     v(cp(T.u16q[:, 0:256], T.i_ql[:]), 256, r=["i_ql"], w=["u16q00", "u16q01"])
@@ -248,9 +359,9 @@ def _plan(g, core, T, topo):
             mm([MM(T.bE[:, 128 * c:128 * c + 128], T["f_" + nm][:, hs], T.i16[:], True, True)], 128, r=["f_" + nm, "i16"], w=["bE%d" % c], b=["bE"])
         v(cp(cb("lh", 0, h), T.bE[:, 0:128]), 128, r=["bE0"], w=["lh0%d" % h], b=["bE"])
         v(cp(cb("qh", 0, h), T.bE[:, 128:256]), 128, r=["bE1"], w=["qh0%d" % h], b=["bE"])
-        s(act(cb("qst", 0, h), T.bE[:, 128:256], AF.Copy, CQ + 2048.0), 128, r=["bE1"], w=["qst0%d" % h], b=["bE"])
-        for i, c in ((2, 0), (0, 2), (1, 3)):
-            s(act(cb("lst", i, h), T.bE[:, 128 * c:128 * c + 128], AF.Copy, CP + 2048.0), 128, r=["bE%d" % c], w=["lst%d%d" % (i, h)], b=["bE"])
+        shifted(cb("qst", 0, h), T.bE[:, 128:256], CQ + 2048.0, 128, r=["bE1"], w=["qst0%d" % h], b=["bE"])
+        for i, c in ((0, 2), (1, 3), (2, 0)):
+            shifted(cb("lst", i, h), T.bE[:, 128 * c:128 * c + 128], CP + 2048.0, 128, r=["bE%d" % c], w=["lst%d%d" % (i, h)], b=["bE"])
 
     P = 2048 // PCS
     dn = [0]
@@ -267,29 +378,41 @@ def _plan(g, core, T, topo):
         hh = str(h)
         x = "x%d" % (t % 4)
         win = T[x][:, 0:4096]
-        B = {n: T[n + hh] for n in ("sg", "lg", "da", "dd", "ra", "rd", "ab", "ac", "ao", "mx")}
+        B = {n: T[_bn(n, t, h)] for n in LONG}
+        xk = [x, "x0b"] if t % 4 == 0 else [x]
+        fo = FOLD(t, h)
 
         def off(buf, i, j):
             c = i * 256 + h * 128 + j * (128 // PCS)
             return T[buf][:, c:c + 128 // PCS]
 
-        K = lambda n, j: n + hh + "p%d" % j
-        for j in range(PCS):
-            sl = slice(P * j, P * j + P)
-            kw = dict(r=[x, "u16l%d%d" % (t + 1, h)], w=[K("sg", j)])
-            if (t, h) == (0, 0) and j:
-                v(cp(B["sg"][:, sl], win.indirect(off("u16l", t + 1, j))), P * GATH, **kw)
-            else:
-                s(act(B["sg"][:, sl], win.indirect(off("u16l", t + 1, j)), AF.Copy), P * GATH, **kw)
-        for j in range(PCS):
-            sl = slice(P * j, P * j + P)
-            s(act(B["lg"][:, sl], win.indirect(off("u16l", t + 2, j)), AF.Copy), P * GATH, r=[x, "u16l%d%d" % (t + 2, h)], w=[K("lg", j)])
-        for j in range(PCS):
-            sl = slice(P * j, P * j + P)
-            o = v(tt(B["da"][:, sl], win.indirect(off("u16l", t, j)), B["sg"][:, sl], OP.subtract), P * GATH,
-                  r=[x, "u16l%d%d" % (t, h), K("sg", j)], w=[K("da", j)])
-            first[(t, h)] = o
-            v(ts(B["ra"][:, sl], B["da"][:, sl], 0.0, OP.max), P, 0.5, r=[K("da", j)], w=[K("ra", j)])
+        K = lambda n, j: _bn(n, t, h) + "p%d" % j
+
+        def gather(nm, lst, i):
+            for j in range(PCS):
+                sl = slice(P * j, P * j + P)
+                kw = dict(r=xk + ["%s%d%d" % (lst, i, h)], w=[K(nm, j)])
+                src = win.indirect(off(lst, i, j))
+                o = vs(cp(B[nm][:, sl], src), act(B[nm][:, sl], src, AF.Copy), P * GATH, **kw)
+            return o
+
+        def size(e):
+            for j in range(4):
+                d, sl, gp = "d%d" % (dn[0] % 2), slice(512 * j, 512 * j + 512), 512 * j // P
+                for nm, mat, st in zip(EDGE[e], ("ib", "nib"), (True, False)):
+                    mm([MM(T[d][:], T[mat][:], B[nm][:, sl], st, not st)], 512, r=[K(nm, gp), mat] + ([] if st else [d]), w=[d], b=[d])
+                relu(B["m" + e][:, sl], T[d][:], 512, r=[d], w=[K("m" + e, j)], b=[d])
+                dn[0] += 1
+
+        gather("sg", "u16l", t + 1)
+        first[(t, h)] = gather("pg", "u16l", t)
+        gather("lg", "u16l", t + 2)
+        if "d" in fo:
+            gather("qg", "u16q", t)
+        for grp in ("a", "d", "bc"):
+            ed = [e for e in grp if e in fo]
+            if ed:
+                fold(t, h, ed)
         for j in range(PCS):
             sl = slice(P * j, P * j + P)
             v(lambda a=B["mx"][:, sl], b=B["lg"][:, sl]: g.vector.tensor_tensor_scan(a, T.msk[:], b, 0.0, OP.mult, OP.max), P, 0.5,
@@ -298,55 +421,34 @@ def _plan(g, core, T, topo):
         v(cp(cb("mo", t, h), B["mx"][:, 15::16]), 128, 0.5, r=[K("mx", j) for j in range(PCS)], w=[mo])
         d2 = dst(2)
         send("rm%d%d" % (t, h), cb("mi", t, h), cb("mo", t, h), d2, topo.engines(core, d2)[1:8:2], mo, LAT, "mi%d%d" % (t, h))
-        for j in range(PCS):
-            sl = slice(P * j, P * j + P)
-            v(tt(B["dd"][:, sl], win.indirect(off("u16q", t, j)), B["sg"][:, sl], OP.subtract), P * GATH,
-              r=[x, "u16q%d%d" % (t, h), K("sg", j)], w=[K("dd", j)])
-            v(ts(B["rd"][:, sl], B["dd"][:, sl], 0.0, OP.max), P, 0.5, r=[K("dd", j)], w=[K("rd", j)])
-        def size_b(j):
-            d, sl, gp = "d%d" % (dn[0] % 3), slice(512 * j, 512 * j + 512), 512 * j // P
-            for nm, mat, st, sp in (("sg", "ib", True, False), ("lg", "nib", False, True)):
-                mm([MM(T[d][:], T[mat][:], B[nm][:, sl], st, sp)], 512, r=[K(nm, gp), mat] + ([] if st else [d]), w=[d], b=[d])
-            s(act(B["ab"][:, sl], T[d][:], AF.Abs), 512, r=[d], w=["ab%sp%d" % (hh, j)], b=[d])
-            dn[0] += 1
-
-        def size_c(j):
-            d, sl, gp = "d%d" % (dn[0] % 3), slice(512 * j, 512 * j + 512), 512 * j // P
-            for nm, mat in (("sg", "ib"), ("da", "ib"), ("lg", "nib")):
-                mm([MM(T[d][:], T[mat][:], B[nm][:, sl], nm == "sg", nm == "lg")], 512, r=[K(nm, gp), mat] + ([] if nm == "sg" else [d]), w=[d], b=[d])
-            s(act(B["ac"][:, sl], T[d][:], AF.Abs), 512, r=[d], w=["ac%sp%d" % (hh, j)], b=[d])
-            dn[0] += 1
-
-        for j in range(4):
-            size_b(j)
-        for j in range(4):
-            size_c(j)
+        if "d" not in fo:
+            for j in range(PCS):
+                sl = slice(P * j, P * j + P)
+                v(tt(B["qg"][:, sl], win.indirect(off("u16q", t, j)), B["sg"][:, sl], OP.subtract), P * GATH,
+                  r=xk + ["u16q%d%d" % (t, h), K("sg", j)], w=[K("qg", j)])
+                v(ts(B["md"][:, sl], B["qg"][:, sl], 0.0, OP.max), P, 0.5, r=[K("qg", j)], w=[K("md", jj) for jj in range(4) if 512 * jj // P == j])
+        for e in "abc":
+            if e not in fo:
+                size(e)
         e = "e%d%d" % (t, h)
         for j in range(4):
-            d = "d%d" % ((dn[0] + j) % 3)
-            if (t, h, j) in OMAX:
-                mm([MM(T[d][:, 0:128], T.ib[:], T[e][:, 0:128], True, True)], 128, r=[e, "ib"], w=[d], b=[d])
-                for i in range(4):
-                    k = 4 * j + i
-                    v(tt(B["ao"][:, 128 * k:128 * k + 128], B["lg"][:, k::16], T[d][:, 0:128], OP.max), 128,
-                      r=[K("lg", jj) for jj in range(PCS)] + [d], w=["ao%sp%dk%d" % (hh, j, i)], b=[d])
-                continue
+            d = "d%d" % ((dn[0] + j) % 2)
             fn = []
             for i in range(4):
                 o_ = T[d][:, 128 * i:128 * i + 128]
                 fn += [MM(o_, T.ib[:], B["lg"][:, 4 * j + i::16], True, False), MM(o_, T.nib[:], T[e][:, 0:128], False, True)]
             mm(fn, 1024, r=[K("lg", jj) for jj in range(PCS)] + [e, "ib", "nib"], w=[d], b=[d])
-            s(act(B["ao"][:, 512 * j:512 * j + 512], T[d][:], AF.Abs), 512, r=[d], w=["ao%sp%d" % (hh, j)], b=[d])
+            relu(B["ao"][:, 512 * j:512 * j + 512], T[d][:], 512, r=[d], w=[K("ao", j)], b=[d])
         dn[0] += 4
 
     def logic(t, h):
         hh, n = str(h), 128
         tm = t % 4
-        B = {nm: T[nm + hh] for nm in ("lg", "da", "dd", "ra", "rd", "ab", "ac", "ao")}
+        B = {nm: T[_bn(nm, t, h)] for nm in LONG}
         A, Bb, D, E = T["bA" + hh], T.bB, T.bD, T.bE
         half[0] = hh
         k_ = lambda nm: nm + hh
-        pcs = lambda nm: [nm + hh + "p%d" % j for j in range(4 if nm[0] == "a" else PCS)]
+        pcs = lambda nm: [_bn(nm, t, h) + "p%d" % j for j in range(PCS if nm[1] == "g" else 4)]
         fl = T["fl" + hh]
         it = lambda nm: cb("itmp", ITMP.index(nm), h)
         ft = lambda nm: cb("ftmp", FTMP.index(nm), h)
@@ -356,49 +458,37 @@ def _plan(g, core, T, topo):
         mm([MM(A[:], one_row, T.rowlo[0:1, :], True, False)], 512, r=["one"] + CK, w=["A"], b=["bA"])
         mm([MM(A[:, 384:512], T.one[:], T["thm%d" % tm][:, 0:128], False, False)], 128, r=["one", "thm%d" % tm], a=["A"], b=["bA"])
 
-        def sums(nm, a, b):
+        def sums(nm, i, run):
+            c = [j for j in range(len(COEF)) if tuple(COEF[j:j + len(run)]) == run][0]
             fn = []
             for k in range(16):
                 lt = B[nm][:, 128 * k:128 * k + 128] if nm == "ao" else B[nm][:, k::16]
-                if nm == "ao" and (t, h, k // 4) in OMAX:
-                    fn.append(MM(A[:, a + k:b:16], lt, T.fun[:, 80:88], False, False))
-                    mm([MM(A[:, a + k:b:16], B["lg"][:, k::16], T.fun[:, 88:96], False, False),
-                        MM(A[:, a + k:b:16], T[e][:, 0:128], T.fun[:, 88:96], False, False)], 128, r=pcs("lg") + [e] + FK, a=["A"], b=["bA"])
-                else:
-                    fn.append(MM(A[:, a + k:b:16], lt, T.fun[:, FUN[nm][0]:FUN[nm][1]], False, False))
-            rr = pcs(nm)
-            if nm == "ao":
-                for j in range(4):
-                    if (t, h, j) in OMAX:
-                        rr += ["ao%sp%dk%d" % (hh, j, i) for i in range(4)]
-            mm(fn, 64 * len(fn), r=rr + FK, a=["A"], b=["bA"])
+                fn.append(MM(A[:, 128 * i + k:128 * (i + len(run)):16], lt, T.fun[:, 8 * c:8 * (c + len(run))], False, False))
+            mm(fn, 64 * len(fn), r=pcs(nm) + ["fun%d" % j for j in range(c, c + len(run))], a=["A"], b=["bA"])
 
-        sums("ra", 256, 384)
-        sums("da", 256, 384)
-        sums("rd", 0, 128)
-        sums("dd", 0, 128)
-        sums("ab", 0, 384)
-        sums("ac", 128, 384)
-        sums("ao", 384, 512)
+        for nm, (i, run) in _weights(t, h).items():
+            sums(nm, i, run)
+        mm([MM(A[:, 384:512], T[e][:, 0:128], T.bsc[:], False, False)], 128, r=[e, "bsc"], a=["A"], b=["bA"])
         mm([MM(A[:, 384:512], T.one[:], T["thm%d" % tm][:, 128:256], False, True)], 128, r=["one", "thn%d" % tm], w=["A"], b=["bA"])
         X2, X1, XF, X3 = [A[:, 128 * i:128 * i + 128] for i in range(4)]
         mm([MM(D[:, 0:128], T[e][:, 0:128], T["wb%d" % tm][:], True, True)], 128, r=[e, "wb%d" % tm], w=["Du"], b=["bD"])
-        if h == 0:
-            if t == 0:
-                v(cp(T.ka[:], T.k37[:]), n, r=["k37"], w=["ka"])
-            else:
-                v(ts(T.ka[:], T.k37[:], T["e%d1" % t][:, 128:129], OP.add), n, r=["k37", "e%d1" % t], w=["ka"])
+        if (t, h) == (0, 0):
+            v(cp(T.ka[:], T.k37[:]), n, r=["k37"], w=["ka"])
         lh, qo = cb("lh", t, h), cb("qst", t, h)
-        PL, PY, PLQ = [Bb[:, 128 * i:128 * i + 128] for i in range(3)]
+        PL, PLQ, PY = Bb[:, 0:128], Bb[:, 128:256], T.bY[:, 0:128]
         mm([MM(PL, one_row, T.rowb[0:1, 0:128], True, False), MM(PL, T.i16[:], lh, False, True),
-            MM(PY, one_row, T.rowb[0:1, 128:256], True, False), MM(PY, T.i16[:], lh, False, False), MM(PY, T.i16[:], T.ka[:], False, True),
-            MM(PLQ, T.i16[:], lh, True, False), MM(PLQ, T.n16[:], cb("qh", t, h), False, True)], 7 * 128,
-           r=["one", "i16", "n16", "lh%d%d" % (t, h), "qh%d%d" % (t, h), "ka"] + CB_, w=["B"], b=["bB"])
+            MM(PLQ, T.i16[:], lh, True, False), MM(PLQ, T.n16[:], cb("qh", t, h), False, True)], 4 * 128,
+           r=["one", "i16", "n16", "lh%d%d" % (t, h), "qh%d%d" % (t, h)] + CB_, w=["B"], b=["bB"])
+        mm([MM(PY, one_row, T.rowb[0:1, 128:256], True, False), MM(PY, T.i16[:], lh, False, False), MM(PY, T.i16[:], T.ka[:], False, t == 0)],
+           3 * 128, r=["one", "i16", "lh%d%d" % (t, h), "ka"] + CB_, w=["PY"], b=["bY"])
+        if t:
+            mm([MM(T.bY[:, 16 * i:16 * i + 16], one_row, T["e%d1" % t][0:1, 128:144], False, i == 7) for i in range(8)], 8 * 64,
+               r=["one", "e%d1" % t], w=["PY"], b=["bY"])
         v(cp(it("ui"), D[:, 0:128]), n, r=["Du"], w=[k_("ui")], b=["bD"])
         v(ts(it("uj"), it("ui"), 4095, OP.bitwise_and), n, r=[k_("ui")], w=[k_("uj")])
         v(tt(it("z"), it("uj"), PL, OP.mult), n, r=[k_("uj"), "B"], w=[k_("z")], b=["bB"])
         v(ts(it("zs"), it("z"), 5, OP.arith_shift_right), n, r=[k_("z")], w=[k_("zs")])
-        v(tt(it("y"), it("zs"), PY, OP.add), n, r=[k_("zs"), "B"], w=[k_("y")], b=["bB"])
+        v(tt(it("y"), it("zs"), PY, OP.add), n, r=[k_("zs"), "PY"], w=[k_("y")], b=["bY"])
         ms_, fz = T.msk[:, 0:128], T["fz" + hh]
         v(lambda: g.vector.tensor_tensor_scan(ft("sc"), ms_, XF, 0.0, OP.mult, OP.add), n, r=["A", "msk"], w=[k_("sc")], b=["bA"])
         v(ts(fz[:, 0::16], T.ftmp[:, FTMP.index("sc") * 256 + 128 * h + 15:FTMP.index("sc") * 256 + 128 * h + 128:16], 0.0, OP.is_ge, GATE, OP.mult), 8,
@@ -419,15 +509,14 @@ def _plan(g, core, T, topo):
             if h == 1:
                 mm([MM(D[:, 0:8], T.onec[:], T["fl%d" % a][:, 0::16], a == 0, a == 1) for a in range(2)], 128, r=FL + ["fl0a", "onec"], w=["Du"], b=["bD"])
                 v(lambda: g.vector.tensor_reduce(T.cnt[:, 0:1], D[:, 0:8], AX.X, OP.add), 8, r=["Du"], w=["cnt"], b=["bD"])
-                v(ts(T.acol[:, 0:1], T.cnt[:, 0:1], -1.0, OP.mult), 1, r=["cnt"], w=["ac0"])
-                v(ts(T.acol[:, 1:2], T.acol[:, 0:1], 31, OP.bitwise_and), 1, r=["ac0"], w=["ac1"])
-                v(ms(T[eo][:, 128:144], 0.0), 16, w=[eo + "A"])
-                v(cp(T[eo][:, 128:129], T.acol[:, 1:2]), 1, r=["ac1"], w=[eo + "A"])
-            else:
-                v(ms(T[eo][:, 128:144], 0.0), 16, w=[eo + "A"])
+                v(ts(T.acol[:, 0:16], T.one32[:, 0:16], T.cnt[:, 0:1], OP.mult, -1.0, OP.mult), 16, r=["cnt", "one32"], w=["ac0"])
+                v(ts(T.acol[:, 16:32], T.acol[:, 0:16], 31, OP.bitwise_and), 16, r=["ac0"], w=["ac1"])
+                v(cp(T[eo][:, 128:144], T.acol[:, 16:32]), 16, r=["ac1"], w=[eo + "A"])
             d1 = dst(-1)
             en = "e%d%d" % (t + 1, h)
-            send("re%d%d" % (t + 1, h), T[en][:], T[eo][:], d1, topo.engines(core, d1)[1:8:2], eo, LAT, en, after=[last_w[eo + "A"]])
+            wd = 128 + 16 * h
+            send("re%d%d" % (t + 1, h), T[en][:, 0:wd], T[eo][:, 0:wd], d1, topo.engines(core, d1)[1:8:2], eo, LAT, en,
+                 after=[last_w[eo + "A"]] if h else [])
         else:
             op("Y", 0.1, [lambda: g.sync.dma_start(T.ye[:, 128 * h:128 * h + 128], T[eo][:, 0:128])], r=[eo], sig=("d_ye%d" % h, 16), lat=2.0)
         pst = cb("lst", t, h)
@@ -457,11 +546,11 @@ def _plan(g, core, T, topo):
         if t >= 2:
             o_ = cb("outs", t - 2, h)
             nm = ("yp", "ys", "yl")[t - 2]
-            s(act(o_, E[:, 256:384], AF.Copy, 2048.0), n, r=["bE2"], w=["outs%d%d" % (t - 2, h)], b=["bE"])
+            shifted(o_, E[:, 256:384], 2048.0, n, r=["bE2"], w=["outs%d%d" % (t - 2, h)], b=["bE"])
             op("Y", 0.1, [lambda: g.sync.dma_start(T[nm][:, 128 * h:128 * h + 128], o_)], r=["outs%d%d" % (t - 2, h)], sig=("d_%s%d" % (nm, h), 16), lat=2.0)
         if t == V - 1:
             oq = cb("outs", 3, h)
-            s(act(oq, E[:, 384:512], AF.Copy, 2048.0), n, r=["bE3"], w=["outs3%d" % h], b=["bE"])
+            shifted(oq, E[:, 384:512], 2048.0, n, r=["bE3"], w=["outs3%d" % h], b=["bE"])
             op("Y", 0.1, [lambda: g.sync.dma_start(T.yq[:, 128 * h:128 * h + 128], oq)], r=["outs3%d" % h], sig=("d_yq%d" % h, 16), lat=2.0)
 
     for t in range(V):
@@ -470,10 +559,6 @@ def _plan(g, core, T, topo):
         for h in range(H2):
             big(t, h)
             logic(t, h)
-        if t == 1:
-            send_table(2, [])
-        if t == 2:
-            send_table(3, [first[(0, 1)]])
     return ops
 
 
@@ -485,35 +570,43 @@ def _order(ops):
         for d in pred[i]:
             succ[d].append(i)
     q, c, lat = [o["q"] for o in ops], [o["c"] for o in ops], [o["lat"] for o in ops]
+    dma = [o.get("dma", 0.0) for o in ops]
 
-    def list_pass(before, after, prio, forward):
+    def list_pass(before, after, prio, forward, q):
         left = [len(b) for b in before]
         ready_t = [0.0 if forward or after[i] else lat[i] for i in range(n)]
-        start, free, ready, seq = [0.0] * n, {}, {}, []
+        start, free, ready, seq, took = [0.0] * n, {}, {}, [], list(q)
         for i in range(n):
             if not left[i]:
                 ready.setdefault(q[i], []).append(i)
         while len(seq) < n:
             best = None
             for qq, lst in ready.items():
+                if qq == "X":
+                    qq = "V" if free.get("V", 0.0) + BIAS < free.get("S", 0.0) else "S"
                 f = free.get(qq, 0.0)
                 for i in lst:
-                    key = (max(f, ready_t[i]), -prio[i], i)
+                    key = (max(f, ready_t[i]), -prio[i], i, qq)
                     if best is None or key < best:
                         best = key
-            st, _, i = best
+            st, _, i, took[i] = best
+            if q[i] == "X" and free.get("S", 0.0) <= st:
+                took[i] = "S"
             ready[q[i]].remove(i)
             seq.append(i)
             start[i] = st
             fin = st + c[i]
             if q[i] != "R":
-                free[q[i]] = fin
+                free[took[i]] = fin
+            if dma[i] and forward:
+                free["D"] = max(fin + START, free.get("D", 0.0)) + dma[i]
+                fin = free["D"] - START - dma[i]
             for k in after[i]:
                 ready_t[k] = max(ready_t[k], fin + lat[i if forward else k] + WAKE)
                 left[k] -= 1
                 if not left[k]:
                     ready.setdefault(q[k], []).append(k)
-        return start, seq
+        return start, seq, took
 
     base = [0.0] * n
     for i in reversed(range(n)):
@@ -523,27 +616,36 @@ def _order(ops):
     for trial in range(TRIES):
         prio = [float(p + (SPREAD * x if trial else 0.0)) for p, x in zip(base, rs.random_sample(n))]
         for turn in range(TURNS):
-            start, seq = list_pass(pred, succ, prio, True)
+            start, seq, took = list_pass(pred, succ, prio, True, q)
             span = max(start[i] + c[i] + lat[i] for i in range(n))
             if best is None or span < best[0] - 1e-9:
-                best = (span, start, seq)
-            back, _ = list_pass(succ, pred, [start[i] + c[i] for i in range(n)], False)
+                best = (span, start, seq, took)
+            back = list_pass(succ, pred, [start[i] + c[i] for i in range(n)], False, q)[0]
             prio = [back[i] + c[i] for i in range(n)]
     order = {}
     for i in best[2]:
-        ops[i]["st"] = best[1][i]
-        order.setdefault(q[i], []).append(ops[i])
+        ops[i]["st"], ops[i]["q"] = best[1][i], best[3][i]
+        if q[i] == "X":
+            ops[i]["f"] = ops[i]["alt"][best[3][i]]
+        order.setdefault(ops[i]["q"], []).append(ops[i])
     return order
 
 
 def rank_program(g, core, T, topo):
     if T.rank_of(core) is None:
+        port, hands = _helpers(T, topo)
+        for die, c in port.get(topo.chip(core), {}).items():
+            if c == core:
+                _port_program(g, core, T, topo, die)
+        for owner in hands:
+            if core in hands[owner]:
+                calls = [c for o in _order(_plan(g, owner, T, topo))["G"] for c in o.get("calls", [])]
+                _hand_program(g, core, T, topo, owner, calls)
         return
     ops = _plan(g, core, T, topo)
     order = _order(ops)
     qs = {"T": g.tensor, "V": g.vector, "S": g.scalar, "G": g, "Y": g.sync}
     qsem = {"T": "sT", "V": "sV", "S": "sS", "G": "sG"}
-    count = {q: 0 for q in qs}
     known = {q: {} for q in qs}
     sent = 0
     glob = [o for q in order for o in order[q]]

@@ -15,11 +15,24 @@ LTAB, FIRST = (0.0, 15.0, 24.0, 28.0), 2.0
 XW = 4096 + 16
 EDGE = {"a": ("pg", "sg"), "b": ("sg", "lg"), "c": ("pg", "lg"), "d": ("qg", "sg")}
 TESTS = {"a": (0, 0, -1, 0), "b": (SC, SC, -2, 0), "c": (0, -SC, 2, 0), "d": (-SC, 0, 0, 0), "o": (0, 0, 0, SC)}
+THETA = 0.3
 BIAS = 1.0
 
 
 def FOLD(t, h):
     return "a" if (t, h) == (V - 1, H2 - 1) else "ab"
+
+
+def ENG(n, t, h):
+    return "X"
+
+
+def FUSED(t, h):
+    return t == 0 and "d" not in FOLD(t, h)
+
+
+def OMAX(t, h):
+    return True
 
 
 def _weights(t, h):
@@ -29,13 +42,15 @@ def _weights(t, h):
         w[nm] = tuple(a + c * b for a, b in zip(w.get(nm, (0, 0, 0, 0)), TESTS[e]))
 
     for e, (x, y) in EDGE.items():
+        if e == "d" and t:
+            continue
         if e in FOLD(t, h):
             add("m" + e, e, 2), add(x, e, -1), add(y, e, -1)
-        elif e == "d":
+        elif e == "d" and FUSED(t, h):
             add("md", e, 2), add("qg", e, -1)
         else:
             add("m" + e, e, 2), add(x, e, -1), add(y, e, 1)
-    add("ao", "o", 2), add("lg", "o", -1)
+    add("ao", "o", 2), add("sg" if t else "lg", "o", -1)
     out = {}
     for nm, c in w.items():
         nz = [i for i in range(4) if c[i]]
@@ -114,7 +129,7 @@ _buf("one32", 128, "float32")
 _buf("i32", 128, "float32")
 _buf("i16", 128, "float16")
 _buf("n16", 128, "float16")
-for _n in ("one", "ib", "nib", "i1024", "im512", "bt", "b128", "bsc"):
+for _n in ("one", "ib", "nib", "i1024", "im512", "bt", "b128", "bsc", "nbsc"):
     _buf(_n, 128, "bfloat16")
 _buf("msk", 2048 // PCS, "bfloat16")
 _buf("mskk", 2048 // PCS, "bfloat16")
@@ -180,6 +195,7 @@ def _hand_program(g, core, T, topo, owner, calls):
 def _plan(g, core, T, topo):
     rank, N = T.rank_of(core), len(T.cores)
     ops, last_w, readers, accs, banks, half = [], {}, {}, {}, {}, ["0"]
+    now = [-1, 0]
 
     def op(q, cost, fns, r=(), w=(), a=(), b=(), sig=None, lat=0.0, after=()):
         o = {"q": q, "c": cost, "f": fns, "d": {}, "sig": sig, "lat": lat, "i": len(ops), "n": (list(w) + list(a) + list(r) + ["?"])[0]}
@@ -234,6 +250,9 @@ def _plan(g, core, T, topo):
     def vs(fv, fs, n, **kw):
         o = op("X", vec(n), None, **kw)
         o["alt"] = {"V": [fv], "S": [fs]}
+        e = ENG(o["n"], *now)
+        if e != "X":
+            o["q"], o["f"] = e, o["alt"][e]
         return o
 
     def scaled(out, a, c, n, **kw):
@@ -304,6 +323,7 @@ def _plan(g, core, T, topo):
         else:
             scaled(T[nm][:], T.i32[:], c, 128, r=["i32"], w=[nm])
     scaled(T.bsc[:], T.b128[:], SC, 128, r=["b128"], w=["bsc"])
+    scaled(T.nbsc[:], T.b128[:], -SC, 128, r=["b128"], w=["nbsc"])
     v(ts(T.msk[:], T.mskk[:], 0.0, OP.is_gt), 2048 // PCS, 0.5, r=["mskk"], w=["msk"])
     for i, c in enumerate(COEF):
         scaled(T.fun[:, 8 * i:8 * i + 8], T.b128[:, 0::16], c, 8, r=["b128"], w=["fun%d" % i])
@@ -393,7 +413,7 @@ def _plan(g, core, T, topo):
                 sl = slice(P * j, P * j + P)
                 kw = dict(r=xk + ["%s%d%d" % (lst, i, h)], w=[K(nm, j)])
                 src = win.indirect(off(lst, i, j))
-                o = vs(cp(B[nm][:, sl], src), act(B[nm][:, sl], src, AF.Copy), P * GATH, **kw)
+                o = vs(cp(B[nm][:, sl], src), act(B[nm][:, sl], src, AF.Copy), P * GATH + 70, **kw)
             return o
 
         def size(e):
@@ -407,7 +427,7 @@ def _plan(g, core, T, topo):
         gather("sg", "u16l", t + 1)
         first[(t, h)] = gather("pg", "u16l", t)
         gather("lg", "u16l", t + 2)
-        if "d" in fo:
+        if t == 0 and not FUSED(t, h):
             gather("qg", "u16q", t)
         for grp in ("a", "d", "bc"):
             ed = [e for e in grp if e in fo]
@@ -421,23 +441,31 @@ def _plan(g, core, T, topo):
         v(cp(cb("mo", t, h), B["mx"][:, 15::16]), 128, 0.5, r=[K("mx", j) for j in range(PCS)], w=[mo])
         d2 = dst(2)
         send("rm%d%d" % (t, h), cb("mi", t, h), cb("mo", t, h), d2, topo.engines(core, d2)[1:8:2], mo, LAT, "mi%d%d" % (t, h))
-        if "d" not in fo:
+        if FUSED(t, h):
             for j in range(PCS):
                 sl = slice(P * j, P * j + P)
                 v(tt(B["qg"][:, sl], win.indirect(off("u16q", t, j)), B["sg"][:, sl], OP.subtract), P * GATH,
                   r=xk + ["u16q%d%d" % (t, h), K("sg", j)], w=[K("qg", j)])
                 v(ts(B["md"][:, sl], B["qg"][:, sl], 0.0, OP.max), P, 0.5, r=[K("qg", j)], w=[K("md", jj) for jj in range(4) if 512 * jj // P == j])
-        for e in "abc":
+        for e in "abc" if t or FUSED(t, h) else "abcd":
             if e not in fo:
                 size(e)
-        e = "e%d%d" % (t, h)
+        e, ol = "e%d%d" % (t, h), "sg" if t else "lg"
+        if OMAX(t, h):
+            d = "d%d" % (dn[0] % 2)
+            dn[0] += 1
+            mm([MM(T[d][:, 0:128], T.ib[:], T[e][:, 0:128], True, True)], 128, r=[e, "ib"], w=[d], b=[d])
+            for k in range(16):
+                v(tt(B["ao"][:, 128 * k:128 * k + 128], B[ol][:, k::16], T[d][:, 0:128], OP.max), 128,
+                  r=[K(ol, jj) for jj in range(PCS)] + [d], a=[K("ao", k // 4)], b=[d])
+            return
         for j in range(4):
             d = "d%d" % ((dn[0] + j) % 2)
             fn = []
             for i in range(4):
                 o_ = T[d][:, 128 * i:128 * i + 128]
-                fn += [MM(o_, T.ib[:], B["lg"][:, 4 * j + i::16], True, False), MM(o_, T.nib[:], T[e][:, 0:128], False, True)]
-            mm(fn, 1024, r=[K("lg", jj) for jj in range(PCS)] + [e, "ib", "nib"], w=[d], b=[d])
+                fn += [MM(o_, T.ib[:], B[ol][:, 4 * j + i::16], True, False), MM(o_, T.nib[:], T[e][:, 0:128], False, True)]
+            mm(fn, 1024, r=[K(ol, jj) for jj in range(PCS)] + [e, "ib", "nib"], w=[d], b=[d])
             relu(B["ao"][:, 512 * j:512 * j + 512], T[d][:], 512, r=[d], w=[K("ao", j)], b=[d])
         dn[0] += 4
 
@@ -468,10 +496,11 @@ def _plan(g, core, T, topo):
 
         for nm, (i, run) in _weights(t, h).items():
             sums(nm, i, run)
-        mm([MM(A[:, 384:512], T[e][:, 0:128], T.bsc[:], False, False)], 128, r=[e, "bsc"], a=["A"], b=["bA"])
+        mm([MM(A[:, 384:512], T[e][:, 0:128], T["nbsc" if OMAX(t, h) else "bsc"][:], False, False)], 128, r=[e, "bsc", "nbsc"], a=["A"], b=["bA"])
         mm([MM(A[:, 384:512], T.one[:], T["thm%d" % tm][:, 128:256], False, True)], 128, r=["one", "thn%d" % tm], w=["A"], b=["bA"])
         X2, X1, XF, X3 = [A[:, 128 * i:128 * i + 128] for i in range(4)]
-        mm([MM(D[:, 0:128], T[e][:, 0:128], T["wb%d" % tm][:], True, True)], 128, r=[e, "wb%d" % tm], w=["Du"], b=["bD"])
+        mm([MM(T.bY[:, 128:256], T[e][:, 0:128], T["wb%d" % tm][:], True, True)], 128, r=[e, "wb%d" % tm], w=["U"], b=["bY"])
+        v(cp(it("ui"), T.bY[:, 128:256]), n, r=["U"], w=[k_("ui")], b=["bY"])
         if (t, h) == (0, 0):
             v(cp(T.ka[:], T.k37[:]), n, r=["k37"], w=["ka"])
         lh, qo = cb("lh", t, h), cb("qst", t, h)
@@ -484,7 +513,6 @@ def _plan(g, core, T, topo):
         if t:
             mm([MM(T.bY[:, 16 * i:16 * i + 16], one_row, T["e%d1" % t][0:1, 128:144], False, i == 7) for i in range(8)], 8 * 64,
                r=["one", "e%d1" % t], w=["PY"], b=["bY"])
-        v(cp(it("ui"), D[:, 0:128]), n, r=["Du"], w=[k_("ui")], b=["bD"])
         v(ts(it("uj"), it("ui"), 4095, OP.bitwise_and), n, r=[k_("ui")], w=[k_("uj")])
         v(tt(it("z"), it("uj"), PL, OP.mult), n, r=[k_("uj"), "B"], w=[k_("z")], b=["bB"])
         v(ts(it("zs"), it("z"), 5, OP.arith_shift_right), n, r=[k_("z")], w=[k_("zs")])
@@ -532,17 +560,16 @@ def _plan(g, core, T, topo):
         v(ts(cb("lh", t + 1, h), nw, 2048.0, OP.subtract), n, r=[k_("nw")], w=["lh%d%d" % (t + 1, h)])
         if t + 3 < 5:
             v(ts(cb("lst", t + 3, h), nw, CP, OP.add), n, r=[k_("nw")], w=["lst%d%d" % (t + 3, h)])
+        mm([MM(E[:, 256:384], cb("lh", t + 1, h), T.i16[:], True, True)], 128, r=["i16", "lh%d%d" % (t + 1, h)], w=["bE2"], b=["bE"])
+        if t < V - 1:
+            v(ts(cb("u16l", t + 3, h), E[:, 256:384], 2048.0, OP.add), n, r=["bE2"], w=["u16l%d%d" % (t + 3, h)], b=["bE"])
         qn = cb("qst", t + 1, h)
         v(tt(ft("ne"), nw, PL, OP.not_equal), n, r=[k_("nw"), "B"], w=[k_("ne")], b=["bB"])
         v(tt(E[:, 128:256], ft("ne"), PLQ, OP.mult), n, r=[k_("ne"), "B"], w=["bE1"], b=["bB", "bE"])
         v(tt(qn, qo, E[:, 128:256], OP.add), n, r=["qst%d%d" % (t, h), "bE1"], w=["qst%d%d" % (t + 1, h)], b=["bE"])
-        mm([MM(E[:, 256:384], cb("lh", t + 1, h), T.i16[:], True, True)], 128, r=["i16", "lh%d%d" % (t + 1, h)], w=["bE2"], b=["bE"])
-        if t < V - 1:
-            v(ts(cb("u16l", t + 3, h), E[:, 256:384], 2048.0, OP.add), n, r=["bE2"], w=["u16l%d%d" % (t + 3, h)], b=["bE"])
         v(ts(cb("qh", t + 1, h), qn, CQ + 2048.0, OP.subtract), n, r=["qst%d%d" % (t + 1, h)], w=["qh%d%d" % (t + 1, h)])
-        mm([MM(E[:, 384:512], cb("qh", t + 1, h), T.i16[:], True, True)], 128, r=["i16", "qh%d%d" % (t + 1, h)], w=["bE3"], b=["bE"])
-        if t < V - 1:
-            v(ts(cb("u16q", t + 1, h), E[:, 384:512], 2048.0, OP.add), n, r=["bE3"], w=["u16q%d%d" % (t + 1, h)], b=["bE"])
+        if t == V - 1:
+            mm([MM(E[:, 384:512], cb("qh", t + 1, h), T.i16[:], True, True)], 128, r=["i16", "qh%d%d" % (t + 1, h)], w=["bE3"], b=["bE"])
         if t >= 2:
             o_ = cb("outs", t - 2, h)
             nm = ("yp", "ys", "yl")[t - 2]
@@ -557,6 +584,7 @@ def _plan(g, core, T, topo):
         if t < 4:
             tabs(t)
         for h in range(H2):
+            now[:] = [t, h]
             big(t, h)
             logic(t, h)
     return ops
@@ -572,7 +600,7 @@ def _order(ops):
     q, c, lat = [o["q"] for o in ops], [o["c"] for o in ops], [o["lat"] for o in ops]
     dma = [o.get("dma", 0.0) for o in ops]
 
-    def list_pass(before, after, prio, forward, q):
+    def list_pass(before, after, prio, forward, q, theta=THETA):
         left = [len(b) for b in before]
         ready_t = [0.0 if forward or after[i] else lat[i] for i in range(n)]
         start, free, ready, seq, took = [0.0] * n, {}, {}, [], list(q)
@@ -580,18 +608,16 @@ def _order(ops):
             if not left[i]:
                 ready.setdefault(q[i], []).append(i)
         while len(seq) < n:
-            best = None
+            can = []
             for qq, lst in ready.items():
-                if qq == "X":
-                    qq = "V" if free.get("V", 0.0) + BIAS < free.get("S", 0.0) else "S"
-                f = free.get(qq, 0.0)
                 for i in lst:
-                    key = (max(f, ready_t[i]), -prio[i], i, qq)
-                    if best is None or key < best:
-                        best = key
-            st, _, i, took[i] = best
-            if q[i] == "X" and free.get("S", 0.0) <= st:
-                took[i] = "S"
+                    e = qq
+                    if qq == "X":
+                        e = "V" if free.get("V", 0.0) + BIAS < free.get("S", 0.0) and ready_t[i] < free.get("S", 0.0) else "S"
+                    can.append((max(free.get(e, 0.0), ready_t[i]), i, e))
+            end, e = min((s + theta * c[i], e) for s, i, e in can)
+            _, i, st = min((-prio[i], i, s) for s, i, ee in can if ee == e and s <= end)
+            took[i] = e
             ready[q[i]].remove(i)
             seq.append(i)
             start[i] = st

@@ -4,19 +4,22 @@ from concourse.mybir import AluOpType as OP, ActivationFunctionType as AF, AxisL
 
 V, H2 = 5, 2
 PCS = 2
-PE_NS, CY_NS, GATH = 0.4167, 0.83, 1.5
-LAT, WAKE = 5.0, 0.14
-SPREAD, SEED, TRIES, TURNS = 2.0, 849, 6, 6
+PE_NS, CY_NS, GATH = 0.4167, 0.83, 1.56
+LAT, WAKE = 4.5, 0.14
+SPREAD, SEED, TRIES, TURNS = 1.0, 849, 150, 6
 SC = 2.0 ** 23
-CF, CQ, CP = 8192.0, 2.0 ** 20, 2.0 ** 21
-GATE = 2.0 ** 22
-START, DFOLD, DSMALL, BACK = 2.0, 3.0, 0.4, 4.4
-LTAB, FIRST = (0.0, 15.0, 24.0, 28.0), 2.0
+CL, CF, CP = -2.0 ** 21, 8192.0, 2.0 ** 21
+GATE = 2.0 ** 23
+START, DFOLD, DSMALL, BACK = 1.9, 2.8, 0.4, 2.8
+LTAB, FIRST = (0.0, 14.0, 25.0, 31.0), 2.0
 XW = 4096 + 16
 EDGE = {"a": ("pg", "sg"), "b": ("sg", "lg"), "c": ("pg", "lg"), "d": ("qg", "sg")}
 TESTS = {"a": (0, 0, -1, 0), "b": (SC, SC, -2, 0), "c": (0, -SC, 2, 0), "d": (-SC, 0, 0, 0), "o": (0, 0, 0, SC)}
-THETA = 0.3
-BIAS = 1.0
+_CHOSEN = {}
+SLOW = (1.0, 1.1)
+SETTINGS = ((1.0, 1.0, 1.0, 50.0), (1.12, 0.83, 0.95, 105.0), (1.25, 1.0, 0.95, 125.0), (1.45, 1.22, 0.95, 158.0), (1.1, 1.0, 1.3, 120.0))
+THETA = (0.1, 0.5)
+BIAS = (0.3, 1.2)
 
 
 def FOLD(t, h):
@@ -27,12 +30,36 @@ def ENG(n, t, h):
     return "X"
 
 
+def QUARTERS(e, t, h):
+    return 4
+
+
+def EFIRST(t, h):
+    return 0
+
+
+def BOTH(t, h):
+    return t == 4
+
+
+def CALLS(e, t, h):
+    return 1
+
+
+def PIECES(nm, t, h):
+    return 2
+
+
+def BANKS(t, h):
+    return ("d0", "d0", "d0") if (t, h) == (4, 1) else ("bE", "bE", "d1")
+
+
 def FUSED(t, h):
     return t == 0 and "d" not in FOLD(t, h)
 
 
 def OMAX(t, h):
-    return True
+    return 4 * 1
 
 
 def _weights(t, h):
@@ -93,16 +120,17 @@ for _n in LANDS:
 for _h in range(2):
     for _n in ("fl", "fz", "absd"):
         _buf(_n + str(_h), 128, "bfloat16")
-ITMP, FTMP = ("ui", "uj", "z", "zs", "y", "r1", "nw", "t2"), ("m3", "r3", "m1", "ne", "sc")
+ITMP, FTMP = ("z", "zs", "y", "r1", "t2"), ("m3", "r3", "m1", "ne", "sc")
 _buf("itmp", len(ITMP) * 256, "int32")
 _buf("ftmp", len(FTMP) * 256, "float32")
 _buf("mo", V * 256, "bfloat16")
 _buf("mi", V * 256, "bfloat16")
 _buf("u16l", 7 * 256, "uint16")
-_buf("u16q", 5 * 256, "uint16")
+_buf("u16q", 256, "uint16")
 _buf("lst", 5 * 256, "float32")
 _buf("lh", 6 * 256, "float16")
-_buf("qst", 6 * 256, "float32")
+_buf("raw", 6 * 256, "int32")
+_buf("qst", 256, "float32")
 _buf("qh", 6 * 256, "float16")
 _buf("outs", 4 * 256, "float32")
 for _t in range(V + 1):
@@ -111,10 +139,10 @@ for _t in range(V + 1):
         if _t < V:
             _buf("eo%d%d" % (_t, _h), 144, "bfloat16")
             SEMAPHORES.append("rm%d%d" % (_t, _h))
-            SEMAPHORES += ["f%s%d%d" % (_e, _t, _h) for _e in FOLD(_t, _h)]
+            SEMAPHORES += ["f%s%d%d%d" % (_e, _t, _h, _w) for _e in FOLD(_t, _h) for _w in range(CALLS(_e, _t, _h))]
             if _t:
                 SEMAPHORES.append("re%d%d" % (_t, _h))
-SEMAPHORES += ["rx1", "rx2", "rx3", "px0", "px1", "px2", "px3"]
+SEMAPHORES += ["rx1", "rx2", "rx3"] + ["px%d%d" % (_r, _w) for _r in range(4) for _w in range(2)]
 for _n in ("pl", "sl", "ll", "ql"):
     _buf("i_" + _n, 256, "int32")
     _buf("f_" + _n, 256, "float16")
@@ -129,12 +157,11 @@ _buf("one32", 128, "float32")
 _buf("i32", 128, "float32")
 _buf("i16", 128, "float16")
 _buf("n16", 128, "float16")
-for _n in ("one", "ib", "nib", "i1024", "im512", "bt", "b128", "bsc", "nbsc"):
+for _n in ("one", "ib", "nib", "i1024", "im512", "i4096", "bt", "b128", "nbsc", "uj0", "uj1"):
     _buf(_n, 128, "bfloat16")
 _buf("msk", 2048 // PCS, "bfloat16")
-_buf("mskk", 2048 // PCS, "bfloat16")
 _buf("fun", 8 * len(COEF), "bfloat16")
-_buf("rowb", 256, "bfloat16")
+_buf("rowb", 384, "bfloat16")
 _buf("rowlo", 512, "bfloat16")
 LOADS = ["sl", "xt0", "xt1", "pl", "th", "wt", "ll", "ql", "ed0", "ed1"]
 STORES = ["%s%d" % (_n, _h) for _n in ("yp", "ys", "yl", "yq", "ye") for _h in range(2)]
@@ -152,7 +179,7 @@ def _helpers(T, topo):
 
 
 def _piece(ap, i):
-    return ap[:, i * XW // 2:(i + 1) * XW // 2]
+    return ap[:, i * XW // 4:(i + 1) * XW // 4]
 
 
 def _write(g, T, topo, items):
@@ -173,21 +200,23 @@ def _port_program(g, core, T, topo, die):
     on = [e for e in topo.engines(core, T.cores[here[0]]) if e not in off]
     i = sorted(port[chip]).index(die)
     jobs = [sorted(((r - h) % N, r, h, en) for r in here for h in homes if h != r) for homes, en in ((far, off), (here, on))]
-    for r in here:
-        g.wait_ge(T.sem["px%d" % r], 8)
-    for k in range(max(len(j) for j in jobs)):
-        _write(g, T, topo, [([_piece(T["x%d" % r], i)], (T.cores[h], _piece(T["x%d" % t], i)), en, "rx%d" % t)
-                            for t, r, h, en in [j[k] for j in jobs if k < len(j)]])
-    g.wait_ge(T.sem["lsem"], sum(len(j[3]) for js in jobs for j in js))
+    item = lambda t, r, h, en, p: ([_piece(T["x%d" % r], p)], (T.cores[h], _piece(T["x%d" % t], p)), en, "rx%d" % t)
+    for w in range(2):
+        for r in here:
+            g.wait_ge(T.sem["px%d%d" % (r, w)], 8)
+        _write(g, T, topo, [item(*j[0], 2 * w + i) for j in jobs])
+    for k in range(1, max(len(j) for j in jobs)):
+        _write(g, T, topo, [item(t, r, h, en[4 * w:4 * w + 4], 2 * w + i) for t, r, h, en in [j[k] for j in jobs if k < len(j)] for w in range(2)])
+    g.wait_ge(T.sem["lsem"], sum(len(j[3]) for js in jobs for j in js + js[:1]))
 
 
 def _hand_program(g, core, T, topo, owner, calls):
     sent = 0
     en = topo.engines(core, owner)
-    for c, land, sem, cnt, back in calls:
+    for c, land, sem, cnt, back, _ in calls:
         if c == core:
             g.wait_ge(T.sem[sem], cnt)
-            _write(g, T, topo, [([T[land][:]], (owner, T[back][:]), en, sem)])
+            _write(g, T, topo, [([land], (owner, back), en, sem)])
             sent += len(en)
     g.wait_ge(T.sem["lsem"], sent)
 
@@ -221,13 +250,7 @@ def _plan(g, core, T, topo):
             accs.setdefault(k, []).append(o)
         for k in w:
             last_w[k], accs[k], readers[k] = o, [], []
-        for k in b:
-            bk = banks.setdefault(k, {"q": None, "cur": [], "prev": []})
-            if bk["q"] != q or q == "X":
-                bk["q"], bk["prev"], bk["cur"] = q, bk["cur"], []
-            for x in bk["prev"]:
-                o["d"][x["i"]] = 1
-            bk["cur"].append(o)
+        o["b"] = b
         o["d"].pop(o["i"], None)
         ops.append(o)
         return o
@@ -279,7 +302,8 @@ def _plan(g, core, T, topo):
         return lambda: g.scalar.activation(out, a, f, bias=bias, scale=scale)
 
     def load(name, out, in_, key):
-        return op("Y", 0.1, [lambda: g.sync.dma_start(out, in_)], w=[key], sig=("d_" + name, 16), lat=3.6 if name[:2] == "xt" else 2.2)
+        return op("Y", 0.0, [lambda: g.sync.dma_start(out, in_)], w=[key], sig=("d_" + name, 16),
+                  lat={"sl": 2.2, "xt0": 3.1, "xt1": 3.9}.get(name, 3.7 + 0.1 * len(ops)))
 
     def send(name, out, in_, dst, eng, key, lat, rkey, after=()):
         eng = [e for e in eng]
@@ -298,12 +322,12 @@ def _plan(g, core, T, topo):
         return T[name][:, c:c + n]
 
     load("sl", T.i_sl[:], T.sl[:], "i_sl")
-    load("xt1", T.x0[:, XW // 2:4096], T.xt[:, XW // 2:4096], "x0b")
     load("xt0", T.x0[:, 0:XW // 2], T.xt[:, 0:XW // 2], "x0")
-    load("pl", T.i_pl[:], T.pl[:], "i_pl")
+    load("xt1", T.x0[:, XW // 2:4096], T.xt[:, XW // 2:4096], "x0b")
+    load("ll", T.i_ll[:], T.ll[:], "i_ll")
     load("th", T.i_tw[:, 0:1], T.th[:], "i_th")
     load("wt", T.i_tw[:, 1:2], T.wt[:], "i_wt")
-    load("ll", T.i_ll[:], T.ll[:], "i_ll")
+    load("pl", T.i_pl[:], T.pl[:], "i_pl")
     load("ql", T.i_ql[:], T.ql[:], "i_ql")
     load("ed0", T.e00[:, 0:128], T.ed[:, 0:128], "e00")
     load("ed1", T.e01[:, 0:128], T.ed[:, 128:256], "e01")
@@ -315,25 +339,25 @@ def _plan(g, core, T, topo):
     gq(lambda: g.affine_select(T.i32[:], T.one32[:], [[-1, 128]], OP.is_equal, 0.0, 0, 1), 128, r=["one32"], w=["i32"])
     gq(lambda: g.affine_select(T.bt[:], T.one[:], [[-16, 8], [0, 16]], OP.is_ge, 0.0, 0, 1), 128, r=["one"], w=["bt"])
     gq(lambda: g.affine_select(T.b128[:], T.bt[:], [[16, 8], [0, 16]], OP.is_ge, 0.0, 15, -1), 128, r=["bt"], w=["b128"])
-    gq(lambda: g.iota(T.mskk[:], [[0, 128 // PCS], [1, 16]], 0, 0, allow_small_or_imprecise_dtypes=True), 2048 // PCS, w=["mskk"])
     gq(lambda: g.iota(T.k37[:], [[0, 8], [37, 16]], 0, 0, allow_small_or_imprecise_dtypes=True), 128, w=["k37"])
-    for nm, c in (("ib", 1.0), ("nib", -1.0), ("i1024", 1024.0 / GATE), ("im512", -512.0 / GATE), ("i16", 1.0), ("n16", -1.0)):
+    for nm, c in (("ib", 1.0), ("nib", -1.0), ("i1024", 1024.0 / GATE), ("im512", -512.0 / GATE), ("i4096", -4096.0), ("i16", 1.0), ("n16", -1.0)):
         if nm in ("i16", "n16"):
             v(ts(T[nm][:], T.i32[:], c, OP.mult), 128, r=["i32"], w=[nm])
         else:
             scaled(T[nm][:], T.i32[:], c, 128, r=["i32"], w=[nm])
-    scaled(T.bsc[:], T.b128[:], SC, 128, r=["b128"], w=["bsc"])
     scaled(T.nbsc[:], T.b128[:], -SC, 128, r=["b128"], w=["nbsc"])
-    v(ts(T.msk[:], T.mskk[:], 0.0, OP.is_gt), 2048 // PCS, 0.5, r=["mskk"], w=["msk"])
+    v(ms(T.msk[:], 1.0), 2048 // PCS, 0.5, w=["msk"])
+    v(ms(T.msk[:, 0::16], 0.0), 128 // PCS, 0.5, w=["msk"])
     for i, c in enumerate(COEF):
         scaled(T.fun[:, 8 * i:8 * i + 8], T.b128[:, 0::16], c, 8, r=["b128"], w=["fun%d" % i])
+    v(ms(T.rowb[0:2, 0:256], CL), 256, 0.5, w=["rowb0", "rowb128"])
     for nm, a, b, c in (("rowlo", 0, 256, -SC / 2), ("rowlo", 256, 384, 0.0), ("rowlo", 384, 512, SC / 2),
-                        ("rowb", 0, 128, 2048.0), ("rowb", 128, 256, 2048.0 + CF)):
-        v(ms(T[nm][0:1, a:b], c), b - a, w=[nm + str(a)])
+                        ("rowb", 0, 128, 2048.0), ("rowb", 128, 256, 2048.0 + CF), ("rowb", 256, 384, 129.0 * 4096)):
+        v(ms(T[nm][0:1, a:b], c), b - a, 0.5, w=[nm + str(a)])
     for h in range(H2):
         v(ms(T["fz%d" % h][:], 0.0), 128, 0.5, w=["fz0%d" % h])
     CK = ["rowlo0", "rowlo256", "rowlo384"]
-    CB_ = ["rowb0", "rowb128"]
+    CB_ = ["rowb0", "rowb128", "rowb256"]
     one_row = T.one[0:1, :]
     v(ts(T.i_th[:, 0:1], T.i_tw[:, 0:1], 4, OP.arith_shift_right), 1, r=["i_th"], w=["thh"])
     v(ts(T.i_th[:, 1:2], T.i_tw[:, 0:1], 15, OP.bitwise_and), 1, r=["i_th"], w=["thl"])
@@ -345,27 +369,32 @@ def _plan(g, core, T, topo):
     port, hands = _helpers(T, topo)
     pc = [port[topo.chip(core)][d] for d in sorted(port[topo.chip(core)])]
     every = topo.engines(core, pc[0])
-    so = op("G", 1.3, [lambda: _write(g, T, topo, [([_piece(T.x0, i)], (pc[i], _piece(T["x%d" % rank], i)), every[8 * i:8 * i + 8], "px%d" % rank)
-                                                   for i in range(2)])], r=["x0", "x0b", "xe0"], sig=("send", 16))
-    so["dma"] = DFOLD
+    so = None
+    for w, keys in enumerate((["x0"], ["x0b", "xe0"])):
+        items = [([_piece(T.x0, 2 * w + i)], (pc[i], _piece(T["x%d" % rank], 2 * w + i)), every[8 * i:8 * i + 8], "px%d%d" % (rank, w)) for i in range(2)]
+        so = op("G", 1.3, [lambda items=items: _write(g, T, topo, items)], r=keys, sig=("send", 16), after=[so] if so else [])
+        so["dma"] = DFOLD / 2
     for t in range(1, N):
-        op("R", 0.0, [], w=["x%d" % t], sig=("rx%d" % t, 16), after=[so], lat=LTAB[t])
-    landed = {c: 0 for c in hands[core]}
+        op("R", 0.0, [], w=["x%d" % t], sig=("rx%d" % t, 16 if t > 1 else 32), after=[so], lat=LTAB[t])
+    landed, sentE = [0], {}
 
     def fold(t, h, edges):
-        n, items, calls = 16 // len(edges), [], []
-        for i, e in enumerate(edges):
-            c = hands[core][(i + h) % 2]
-            land = LANDS[landed[c]]
-            landed[c] += 1
-            items.append(([T[_bn(x, t, h)][:] for x in EDGE[e]], (c, T[land][:]), every[n * i:n * i + n], "f%s%d%d" % (e, t, h)))
-            calls.append((c, land, "f%s%d%d" % (e, t, h), n, _bn("m" + e, t, h)))
-        rd = {e: [_bn(x, t, h) + "p%d" % j for x in EDGE[e] for j in range(PCS)] for e in edges}
-        wr = {e: [_bn("m" + e, t, h) + "p%d" % j for j in range(4)] for e in edges}
-        so = op("G", 1.3, [lambda: _write(g, T, topo, items)], r=sum(rd.values(), []), w=sum(wr.values(), []), sig=("send", 16))
-        so["calls"], so["dma"] = calls, DFOLD * len(edges)
         for e in edges:
-            op("R", 0.0, [], r=rd[e], w=wr[e], sig=("f%s%d%d" % (e, t, h), 16), after=[so], lat=START + so["dma"] + BACK + (FIRST if t == 0 else 0.0))
+            land = LANDS[landed[0]]
+            landed[0] += 1
+            nq = QUARTERS(e, t, h) // CALLS(e, t, h)
+            for w in range(CALLS(e, t, h)):
+                items, calls, sem = [], [], "f%s%d%d%d" % (e, t, h, w)
+                for i, c in enumerate(hands[core]):
+                    sl = slice(256 * nq * (2 * w + i), 256 * nq * (2 * w + i + 1))
+                    items.append(([T[_bn(x, t, h)][:, sl] for x in EDGE[e]], (c, T[land][:, sl]), every[8 * i:8 * i + 8], sem))
+                    calls.append((c, T[land][:, sl], sem, 8, T[_bn("m" + e, t, h)][:, sl], 256 * nq))
+                rd = [_bn(x, t, h) + "p%d" % j for x in EDGE[e] for j in range(nq * w, nq * w + nq)]
+                wr = [_bn("m" + e, t, h) + "p%d" % j for j in range(nq * w, nq * w + nq)]
+                so = op("G", 1.3, [lambda items=items: _write(g, T, topo, items)], r=rd, w=wr, sig=("send", 16),
+                        after=[sentE[h]] if e == "b" and t and EFIRST(t, h) else [])
+                so["calls"], so["dma"] = calls, DFOLD * nq / 4
+                op("R", 0.0, [], r=rd, w=wr, sig=(sem, 32), after=[so], lat=START + so["dma"] * 1.25 + BACK + (FIRST if t == 0 else 0.0))
 
     for nm, i in (("sl", 1), ("pl", 0), ("ll", 2)):
         v(cp(T.u16l[:, 256 * i:256 * i + 256], T["i_" + nm][:]), 256, r=["i_" + nm], w=["u16l%d0" % i, "u16l%d1" % i])
@@ -379,8 +408,9 @@ def _plan(g, core, T, topo):
             mm([MM(T.bE[:, 128 * c:128 * c + 128], T["f_" + nm][:, hs], T.i16[:], True, True)], 128, r=["f_" + nm, "i16"], w=["bE%d" % c], b=["bE"])
         v(cp(cb("lh", 0, h), T.bE[:, 0:128]), 128, r=["bE0"], w=["lh0%d" % h], b=["bE"])
         v(cp(cb("qh", 0, h), T.bE[:, 128:256]), 128, r=["bE1"], w=["qh0%d" % h], b=["bE"])
-        shifted(cb("qst", 0, h), T.bE[:, 128:256], CQ + 2048.0, 128, r=["bE1"], w=["qst0%d" % h], b=["bE"])
-        for i, c in ((0, 2), (1, 3), (2, 0)):
+        shifted(cb("qst", 0, h), T.bE[:, 128:256], 2048.0, 128, r=["bE1"], w=["qst0%d" % h], b=["bE"])
+        v(ts(cb("raw", 0, h), T.bE[:, 0:128], 2048.0, OP.add), 128, r=["bE0"], w=["raw0%d" % h], b=["bE"])
+        for i, c in ((0, 2), (1, 3)):
             shifted(cb("lst", i, h), T.bE[:, 128 * c:128 * c + 128], CP + 2048.0, 128, r=["bE%d" % c], w=["lst%d%d" % (i, h)], b=["bE"])
 
     P = 2048 // PCS
@@ -402,27 +432,34 @@ def _plan(g, core, T, topo):
         xk = [x, "x0b"] if t % 4 == 0 else [x]
         fo = FOLD(t, h)
 
-        def off(buf, i, j):
-            c = i * 256 + h * 128 + j * (128 // PCS)
-            return T[buf][:, c:c + 128 // PCS]
+        def off(buf, i, j, n=PCS):
+            c = i * 256 + h * 128 + j * (128 // n)
+            return T[buf][:, c:c + 128 // n]
 
         K = lambda n, j: _bn(n, t, h) + "p%d" % j
+        KP = lambda n, j, m=PCS: [K(n, jj) for jj in range(4 * j // m, 4 * (j + 1) // m)]
+
+        q4 = lambda d: [d + str(i) for i in range(4)]
+
+        def turn():
+            dn[0] += 1
+            return BANKS(t, h)[2] if BOTH(t, h) and dn[0] % 2 else "d%d" % h
 
         def gather(nm, lst, i):
-            for j in range(PCS):
-                sl = slice(P * j, P * j + P)
-                kw = dict(r=xk + ["%s%d%d" % (lst, i, h)], w=[K(nm, j)])
-                src = win.indirect(off(lst, i, j))
-                o = vs(cp(B[nm][:, sl], src), act(B[nm][:, sl], src, AF.Copy), P * GATH + 70, **kw)
+            n = PIECES(nm, t, h)
+            for j in range(n):
+                sl = slice(2048 // n * j, 2048 // n * (j + 1))
+                kw = dict(r=xk + ["%s%d%d" % (lst, i, h)], w=KP(nm, j, n))
+                src = win.indirect(off(lst, i, j, n))
+                o = vs(cp(B[nm][:, sl], src), act(B[nm][:, sl], src, AF.Copy), 2048 // n * GATH + 70, **kw)
             return o
 
         def size(e):
             for j in range(4):
-                d, sl, gp = "d%d" % (dn[0] % 2), slice(512 * j, 512 * j + 512), 512 * j // P
+                d, sl, gp = turn(), slice(512 * j, 512 * j + 512), j
                 for nm, mat, st in zip(EDGE[e], ("ib", "nib"), (True, False)):
-                    mm([MM(T[d][:], T[mat][:], B[nm][:, sl], st, not st)], 512, r=[K(nm, gp), mat] + ([] if st else [d]), w=[d], b=[d])
-                relu(B["m" + e][:, sl], T[d][:], 512, r=[d], w=[K("m" + e, j)], b=[d])
-                dn[0] += 1
+                    mm([MM(T[d][:], T[mat][:], B[nm][:, sl], st, not st)], 512, r=[K(nm, gp), mat], w=q4(d), b=[d])
+                relu(B["m" + e][:, sl], T[d][:], 512, r=q4(d), w=[K("m" + e, j)], b=[d])
 
         gather("sg", "u16l", t + 1)
         first[(t, h)] = gather("pg", "u16l", t)
@@ -431,43 +468,44 @@ def _plan(g, core, T, topo):
             gather("qg", "u16q", t)
         for grp in ("a", "d", "bc"):
             ed = [e for e in grp if e in fo]
-            if ed:
-                fold(t, h, ed)
+            fold(t, h, [e for e in ed if QUARTERS(e, t, h)])
         for j in range(PCS):
             sl = slice(P * j, P * j + P)
             v(lambda a=B["mx"][:, sl], b=B["lg"][:, sl]: g.vector.tensor_tensor_scan(a, T.msk[:], b, 0.0, OP.mult, OP.max), P, 0.5,
-              r=["msk", K("lg", j)], w=[K("mx", j)])
+              r=["msk"] + KP("lg", j), w=[K("mx", j)])
         mo = "mo%d%d" % (t, h)
         v(cp(cb("mo", t, h), B["mx"][:, 15::16]), 128, 0.5, r=[K("mx", j) for j in range(PCS)], w=[mo])
         d2 = dst(2)
-        send("rm%d%d" % (t, h), cb("mi", t, h), cb("mo", t, h), d2, topo.engines(core, d2)[1:8:2], mo, LAT, "mi%d%d" % (t, h))
+        send("rm%d%d" % (t, h), cb("mi", t, h), cb("mo", t, h), d2, topo.engines(core, d2)[:8], mo, LAT, "mi%d%d" % (t, h))
         if FUSED(t, h):
             for j in range(PCS):
                 sl = slice(P * j, P * j + P)
                 v(tt(B["qg"][:, sl], win.indirect(off("u16q", t, j)), B["sg"][:, sl], OP.subtract), P * GATH,
-                  r=xk + ["u16q%d%d" % (t, h), K("sg", j)], w=[K("qg", j)])
-                v(ts(B["md"][:, sl], B["qg"][:, sl], 0.0, OP.max), P, 0.5, r=[K("qg", j)], w=[K("md", jj) for jj in range(4) if 512 * jj // P == j])
+                  r=xk + ["u16q%d%d" % (t, h)] + KP("sg", j), w=KP("qg", j))
+                v(ts(B["md"][:, sl], B["qg"][:, sl], 0.0, OP.max), P, 0.5, r=KP("qg", j), w=KP("md", j))
         for e in "abc" if t or FUSED(t, h) else "abcd":
             if e not in fo:
                 size(e)
+            for j in range(QUARTERS(e, t, h), 4) if e in fo else []:
+                d, sl, gp = turn(), slice(512 * j, 512 * j + 512), j
+                x_, y_ = EDGE[e]
+                mm([MM(T[d][:], T.ib[:], B[x_][:, sl], True, True)], 512, r=[K(x_, gp), "ib"], w=q4(d), b=[d])
+                v(tt(B["m" + e][:, sl], B[y_][:, sl], T[d][:], OP.max), 512, r=q4(d) + [K(y_, gp)], w=[K("m" + e, j)], b=[d])
         e, ol = "e%d%d" % (t, h), "sg" if t else "lg"
         if OMAX(t, h):
-            d = "d%d" % (dn[0] % 2)
-            dn[0] += 1
-            mm([MM(T[d][:, 0:128], T.ib[:], T[e][:, 0:128], True, True)], 128, r=[e, "ib"], w=[d], b=[d])
-            for k in range(16):
-                v(tt(B["ao"][:, 128 * k:128 * k + 128], B[ol][:, k::16], T[d][:, 0:128], OP.max), 128,
-                  r=[K(ol, jj) for jj in range(PCS)] + [d], a=[K("ao", k // 4)], b=[d])
-            return
-        for j in range(4):
-            d = "d%d" % ((dn[0] + j) % 2)
+            d = "Ec" + hh
+            mm([MM(cb("bY", 1, h), T.ib[:], T[e][:, 0:128], True, True)], 128, r=[e, "ib"], w=[d], b=["bY"])
+            for k in range(4 * OMAX(t, h)):
+                v(tt(B["ao"][:, 128 * k:128 * k + 128], B[ol][:, k::16], cb("bY", 1, h), OP.max), 128,
+                  r=KP(ol, 0, 1) + [d], a=[K("ao", k // 4)], b=["bY"])
+        for j in range(OMAX(t, h), 4):
+            d = turn()
             fn = []
             for i in range(4):
                 o_ = T[d][:, 128 * i:128 * i + 128]
                 fn += [MM(o_, T.ib[:], B[ol][:, 4 * j + i::16], True, False), MM(o_, T.nib[:], T[e][:, 0:128], False, True)]
-            mm(fn, 1024, r=[K(ol, jj) for jj in range(PCS)] + [e, "ib", "nib"], w=[d], b=[d])
-            relu(B["ao"][:, 512 * j:512 * j + 512], T[d][:], 512, r=[d], w=[K("ao", j)], b=[d])
-        dn[0] += 4
+            mm(fn, 1024, r=KP(ol, 0, 1) + [e, "ib", "nib"], w=q4(d), b=[d])
+            relu(B["ao"][:, 512 * j:512 * j + 512], T[d][:], 512, r=q4(d), w=[K("ao", j)], b=[d])
 
     def logic(t, h):
         hh, n = str(h), 128
@@ -476,13 +514,11 @@ def _plan(g, core, T, topo):
         A, Bb, D, E = T["bA" + hh], T.bB, T.bD, T.bE
         half[0] = hh
         k_ = lambda nm: nm + hh
-        pcs = lambda nm: [_bn(nm, t, h) + "p%d" % j for j in range(PCS if nm[1] == "g" else 4)]
+        pcs = lambda nm: [_bn(nm, t, h) + "p%d" % j for j in range(4)]
         fl = T["fl" + hh]
         it = lambda nm: cb("itmp", ITMP.index(nm), h)
         ft = lambda nm: cb("ftmp", FTMP.index(nm), h)
         e, eo, mi = "e%d%d" % (t, h), "eo%d%d" % (t, h), "mi%d%d" % (t, h)
-        if t == 0:
-            first_page_form(h)
         mm([MM(A[:], one_row, T.rowlo[0:1, :], True, False)], 512, r=["one"] + CK, w=["A"], b=["bA"])
         mm([MM(A[:, 384:512], T.one[:], T["thm%d" % tm][:, 0:128], False, False)], 128, r=["one", "thm%d" % tm], a=["A"], b=["bA"])
 
@@ -496,27 +532,34 @@ def _plan(g, core, T, topo):
 
         for nm, (i, run) in _weights(t, h).items():
             sums(nm, i, run)
-        mm([MM(A[:, 384:512], T[e][:, 0:128], T["nbsc" if OMAX(t, h) else "bsc"][:], False, False)], 128, r=[e, "bsc", "nbsc"], a=["A"], b=["bA"])
+        c = COEF.index(2 * SC)
+        mm([MM(A[:, 384:512], T[e][:, 0:128], T.nbsc[:], False, False)] +
+           [MM(A[:, 384 + k:512:16], T[e][:, 0:128], T.fun[:, 8 * c:8 * c + 8], False, False) for k in range(4 * OMAX(t, h), 16)],
+           128 + 256 * (4 - OMAX(t, h)), r=[e, "nbsc", "fun%d" % c], a=["A"], b=["bA"])
         mm([MM(A[:, 384:512], T.one[:], T["thm%d" % tm][:, 128:256], False, True)], 128, r=["one", "thn%d" % tm], w=["A"], b=["bA"])
         X2, X1, XF, X3 = [A[:, 128 * i:128 * i + 128] for i in range(4)]
-        mm([MM(T.bY[:, 128:256], T[e][:, 0:128], T["wb%d" % tm][:], True, True)], 128, r=[e, "wb%d" % tm], w=["U"], b=["bY"])
-        v(cp(it("ui"), T.bY[:, 128:256]), n, r=["U"], w=[k_("ui")], b=["bY"])
+        U = cb("bB", h, 1)
+        mm([MM(U, T[e][:, 0:128], T["wb%d" % tm][:], True, True)], 128, r=[e, "wb%d" % tm], w=[k_("U")], b=["bB"])
+        uj, c4 = T["uj" + hh][:], 128.5 + 1.0 / 8192
+        vs(ts(uj, U, 1.0 / 4096, OP.mult, c4, OP.add), act(uj, U, AF.Copy, c4, 1.0 / 4096), n, r=[k_("U")], w=[k_("uj")], b=["bB"])
+        mm([MM(U, T[e][:, 0:128], T["wb%d" % tm][:], True, False), MM(U, one_row, T.rowb[0:1, 256:384], False, False),
+            MM(U, T.i4096[:], uj, False, True)], 3 * 128, r=[e, "wb%d" % tm, "one", "i4096", k_("uj")] + CB_, w=[k_("U")], b=["bB"])
         if (t, h) == (0, 0):
             v(cp(T.ka[:], T.k37[:]), n, r=["k37"], w=["ka"])
-        lh, qo = cb("lh", t, h), cb("qst", t, h)
-        PL, PLQ, PY = Bb[:, 0:128], Bb[:, 128:256], T.bY[:, 0:128]
-        mm([MM(PL, one_row, T.rowb[0:1, 0:128], True, False), MM(PL, T.i16[:], lh, False, True),
-            MM(PLQ, T.i16[:], lh, True, False), MM(PLQ, T.n16[:], cb("qh", t, h), False, True)], 4 * 128,
-           r=["one", "i16", "n16", "lh%d%d" % (t, h), "qh%d%d" % (t, h)] + CB_, w=["B"], b=["bB"])
-        mm([MM(PY, one_row, T.rowb[0:1, 128:256], True, False), MM(PY, T.i16[:], lh, False, False), MM(PY, T.i16[:], T.ka[:], False, t == 0)],
-           3 * 128, r=["one", "i16", "lh%d%d" % (t, h), "ka"] + CB_, w=["PY"], b=["bY"])
+        lh, raw = cb("lh", t, h), cb("raw", t, h)
+        qo, qk = (cb("raw", t - 1, h), "raw%d%d" % (t - 1, h)) if t else (cb("qst", 0, h), "qst0%d" % h)
+        PL, PY = cb("bB", h, 0), cb("bY", 0, h)
+        mm([MM(PL, T.one[0:2, :], T.rowb[0:2, 0:128], True, False), MM(PL, T.i16[:], lh, False, True)], 2 * 128,
+           r=["one", "i16", "lh%d%d" % (t, h)] + CB_, w=[k_("B")], b=["bB"])
+        if t + 2 < V:
+            shifted(cb("lst", t + 2, h), PL, CP - CL, n, r=[k_("B")], w=["lst%d%d" % (t + 2, h)], b=["bB"])
+        fn = [MM(PY, T.one[0:2, :], T.rowb[0:2, 128:256], True, False), MM(PY, T.i16[:], lh, False, False), MM(PY, T.i16[:], T.ka[:], False, t == 0)]
         if t:
-            mm([MM(T.bY[:, 16 * i:16 * i + 16], one_row, T["e%d1" % t][0:1, 128:144], False, i == 7) for i in range(8)], 8 * 64,
-               r=["one", "e%d1" % t], w=["PY"], b=["bY"])
-        v(ts(it("uj"), it("ui"), 4095, OP.bitwise_and), n, r=[k_("ui")], w=[k_("uj")])
-        v(tt(it("z"), it("uj"), PL, OP.mult), n, r=[k_("uj"), "B"], w=[k_("z")], b=["bB"])
+            fn += [MM(T.bY[:, 128 * h + 16 * i:128 * h + 16 * i + 16], one_row, T["e%d1" % t][0:1, 128:144], False, i == 7) for i in range(8)]
+        mm(fn, 3 * 128 + (8 * 64 if t else 0), r=["one", "i16", "lh%d%d" % (t, h), "ka", "e%d1" % t] + CB_, w=[k_("PY")], b=["bY"])
+        v(tt(it("z"), raw, U, OP.mult), n, r=[k_("U"), "raw%d%d" % (t, h)], w=[k_("z")], b=["bB"])
         v(ts(it("zs"), it("z"), 5, OP.arith_shift_right), n, r=[k_("z")], w=[k_("zs")])
-        v(tt(it("y"), it("zs"), PY, OP.add), n, r=[k_("zs"), "PY"], w=[k_("y")], b=["bY"])
+        v(tt(it("y"), it("zs"), PY, OP.add), n, r=[k_("zs"), k_("PY")], w=[k_("y")], b=["bY"])
         ms_, fz = T.msk[:, 0:128], T["fz" + hh]
         v(lambda: g.vector.tensor_tensor_scan(ft("sc"), ms_, XF, 0.0, OP.mult, OP.add), n, r=["A", "msk"], w=[k_("sc")], b=["bA"])
         v(ts(fz[:, 0::16], T.ftmp[:, FTMP.index("sc") * 256 + 128 * h + 15:FTMP.index("sc") * 256 + 128 * h + 128:16], 0.0, OP.is_ge, GATE, OP.mult), 8,
@@ -543,43 +586,53 @@ def _plan(g, core, T, topo):
             d1 = dst(-1)
             en = "e%d%d" % (t + 1, h)
             wd = 128 + 16 * h
-            send("re%d%d" % (t + 1, h), T[en][:, 0:wd], T[eo][:, 0:wd], d1, topo.engines(core, d1)[1:8:2], eo, LAT, en,
+            sentE[h] = send("re%d%d" % (t + 1, h), T[en][:, 0:wd], T[eo][:, 0:wd], d1, topo.engines(core, d1)[-8:], eo, LAT, en,
                  after=[last_w[eo + "A"]] if h else [])
         else:
             op("Y", 0.1, [lambda: g.sync.dma_start(T.ye[:, 128 * h:128 * h + 128], T[eo][:, 0:128])], r=[eo], sig=("d_ye%d" % h, 16), lat=2.0)
-        pst = cb("lst", t, h)
+        pst, last = cb("lst", t, h), t == V - 1
+        lk, ln, qh, qhk = "lh%d%d" % (t, h), "lh%d%d" % (t + 1, h), cb("qh", t, h), "qh%d%d" % (t, h)
+        if last:
+            mm([MM(D[:, 0:128], qh, T.i16[:], True, True)], 128, r=["i16", qhk], w=["Du"], b=["bD"])
+            shifted(cb("qst", 0, h), D[:, 0:128], 2048.0, n, r=["Du"], w=["qst0%d" % h], b=["bD"])
+        bE = BANKS(t, h)[0]
+        E, (E0, E1, E2, E3) = T[bE], [bE + str(i) for i in range(4)]
         v(tt(ft("m3"), it("y"), X3, OP.min), n, r=[k_("y"), "A"], w=[k_("m3")], b=["bA"])
-        v(tt(ft("r3"), ft("m3"), PL, OP.max), n, r=[k_("m3"), "B"], w=[k_("r3")], b=["bB"])
-        v(tt(E[:, 0:128], qo, X2, OP.min), n, r=["qst%d%d" % (t, h), "A"], w=["bE0"], b=["bA", "bE"])
-        v(tt(E[:, 128:256], pst, X1, OP.min), n, r=["lst%d%d" % (t, h), "A"], w=["bE1"], b=["bA", "bE"])
-        v(tt(ft("m1"), E[:, 128:256], fl[:], OP.subtract), n, r=FL + ["bE1"], w=[k_("m1")], b=["bE"])
-        v(tt(E[:, 0:128], ft("r3"), E[:, 0:128], OP.max), n, r=[k_("r3"), "bE0"], w=["bE0"], b=["bE"])
-        v(tt(it("r1"), ft("m1"), E[:, 0:128], OP.max), n, r=[k_("m1"), "bE0"], w=[k_("r1")], b=["bE"])
-        nw = it("nw")
-        v(ts(nw, it("r1"), 4095, OP.bitwise_and), n, r=[k_("r1")], w=[k_("nw")])
-        v(ts(cb("lh", t + 1, h), nw, 2048.0, OP.subtract), n, r=[k_("nw")], w=["lh%d%d" % (t + 1, h)])
-        if t + 3 < 5:
-            v(ts(cb("lst", t + 3, h), nw, CP, OP.add), n, r=[k_("nw")], w=["lst%d%d" % (t + 3, h)])
-        mm([MM(E[:, 256:384], cb("lh", t + 1, h), T.i16[:], True, True)], 128, r=["i16", "lh%d%d" % (t + 1, h)], w=["bE2"], b=["bE"])
-        if t < V - 1:
-            v(ts(cb("u16l", t + 3, h), E[:, 256:384], 2048.0, OP.add), n, r=["bE2"], w=["u16l%d%d" % (t + 3, h)], b=["bE"])
-        qn = cb("qst", t + 1, h)
-        v(tt(ft("ne"), nw, PL, OP.not_equal), n, r=[k_("nw"), "B"], w=[k_("ne")], b=["bB"])
-        v(tt(E[:, 128:256], ft("ne"), PLQ, OP.mult), n, r=[k_("ne"), "B"], w=["bE1"], b=["bB", "bE"])
-        v(tt(qn, qo, E[:, 128:256], OP.add), n, r=["qst%d%d" % (t, h), "bE1"], w=["qst%d%d" % (t + 1, h)], b=["bE"])
-        v(ts(cb("qh", t + 1, h), qn, CQ + 2048.0, OP.subtract), n, r=["qst%d%d" % (t + 1, h)], w=["qh%d%d" % (t + 1, h)])
-        if t == V - 1:
-            mm([MM(E[:, 384:512], cb("qh", t + 1, h), T.i16[:], True, True)], 128, r=["i16", "qh%d%d" % (t + 1, h)], w=["bE3"], b=["bE"])
+        v(tt(ft("r3"), ft("m3"), PL, OP.max), n, r=[k_("m3"), k_("B")], w=[k_("r3")], b=["bB"])
+        v(tt(E[:, 0:128], qo, X2, OP.min), n, r=[qk, "A"], w=[E0], b=["bA", bE])
+        v(tt(E[:, 128:256], pst, X1, OP.min), n, r=["lst%d%d" % (t, h), "A"], w=[E1], b=["bA", bE])
+        v(tt(ft("m1"), E[:, 128:256], fl[:], OP.subtract), n, r=FL + [E1], w=[k_("m1")], b=[bE])
+        v(tt(E[:, 0:128], ft("r3"), E[:, 0:128], OP.max), n, r=[k_("r3"), E0], w=[E0], b=[bE])
+        v(tt(it("r1"), ft("m1"), E[:, 0:128], OP.max), n, r=[k_("m1"), E0], w=[k_("r1")], b=[bE])
+        nw, nk, lhn = cb("raw", t + 1, h), "raw%d%d" % (t + 1, h), cb("lh", t + 1, h)
+        v(ts(nw, it("r1"), 4095, OP.bitwise_and), n, r=[k_("r1")], w=[nk])
+        v(ts(lhn, nw, 2048.0, OP.subtract), n, r=[nk], w=[ln])
+        mm([MM(E[:, 256:384], lhn, T.i16[:], True, True)], 128, r=["i16", ln], w=[E2], b=[bE])
+        if not last:
+            v(ts(cb("u16l", t + 3, h), E[:, 256:384], 2048.0, OP.add), n, r=[E2], w=["u16l%d%d" % (t + 3, h)], b=[bE])
+        less = lambda o_, a, b_: [MM(o_, a, T.i16[:], True, False), MM(o_, b_, T.n16[:], False, True)] if last else \
+            [MM(o_, T.i16[:], a, True, False), MM(o_, T.n16[:], b_, False, True)]
+        EL, bL, kL = E[:, 256:384], bE, E2
+        bE = BANKS(t, h)[1]
+        E, (E0, E1, E2, E3) = T[bE], [bE + str(i) for i in range(4)]
+        mm(less(E[:, 0:128], lhn, lh), 2 * 128, r=["i16", "n16", lk, ln], w=[E0], b=[bE])
+        mm(less(E[:, 384:512], lh, qh), 2 * 128, r=["i16", "n16", lk, qhk], w=[E3], b=[bE])
+        v(ts(ft("ne"), E[:, 0:128], 0.0, OP.not_equal), n, r=[E0], w=[k_("ne")], b=[bE])
+        v(tt(E[:, 128:256], ft("ne"), E[:, 384:512], OP.mult), n, r=[k_("ne"), E3], w=[E1], b=[bE])
         if t >= 2:
             o_ = cb("outs", t - 2, h)
             nm = ("yp", "ys", "yl")[t - 2]
-            shifted(o_, E[:, 256:384], 2048.0, n, r=["bE2"], w=["outs%d%d" % (t - 2, h)], b=["bE"])
+            shifted(o_, EL, 2048.0, n, r=[kL], w=["outs%d%d" % (t - 2, h)], b=[bL])
             op("Y", 0.1, [lambda: g.sync.dma_start(T[nm][:, 128 * h:128 * h + 128], o_)], r=["outs%d%d" % (t - 2, h)], sig=("d_%s%d" % (nm, h), 16), lat=2.0)
-        if t == V - 1:
+        if last:
             oq = cb("outs", 3, h)
-            shifted(oq, E[:, 384:512], 2048.0, n, r=["bE3"], w=["outs3%d" % h], b=["bE"])
+            v(tt(oq, cb("qst", 0, h), E[:, 128:256], OP.add), n, r=["qst0%d" % h, E1], w=["outs3%d" % h], b=[bE])
             op("Y", 0.1, [lambda: g.sync.dma_start(T.yq[:, 128 * h:128 * h + 128], oq)], r=["outs3%d" % h], sig=("d_yq%d" % h, 16), lat=2.0)
+        else:
+            v(tt(cb("qh", t + 1, h), qh, E[:, 128:256], OP.add), n, r=[qhk, E1], w=["qh%d%d" % (t + 1, h)], b=[bE])
 
+    for h in range(H2):
+        first_page_form(h)
     for t in range(V):
         if t < 4:
             tabs(t)
@@ -598,12 +651,13 @@ def _order(ops):
         for d in pred[i]:
             succ[d].append(i)
     q, c, lat = [o["q"] for o in ops], [o["c"] for o in ops], [o["lat"] for o in ops]
-    dma = [o.get("dma", 0.0) for o in ops]
+    dma, bank = [o.get("dma", 0.0) for o in ops], [o["b"] for o in ops]
+    rdma = [dma[i - 1] if q[i] == "R" else 0.0 for i in range(n)]
 
-    def list_pass(before, after, prio, forward, q, theta=THETA):
+    def list_pass(before, after, prio, forward, theta, bias):
         left = [len(b) for b in before]
         ready_t = [0.0 if forward or after[i] else lat[i] for i in range(n)]
-        start, free, ready, seq, took = [0.0] * n, {}, {}, [], list(q)
+        start, free, ready, seq, took, held = [0.0] * n, {}, {}, [], list(q), {}
         for i in range(n):
             if not left[i]:
                 ready.setdefault(q[i], []).append(i)
@@ -613,10 +667,19 @@ def _order(ops):
                 for i in lst:
                     e = qq
                     if qq == "X":
-                        e = "V" if free.get("V", 0.0) + BIAS < free.get("S", 0.0) and ready_t[i] < free.get("S", 0.0) else "S"
-                    can.append((max(free.get(e, 0.0), ready_t[i]), i, e))
+                        e = "V" if free.get("V", 0.0) + bias < free.get("S", 0.0) and ready_t[i] < free.get("S", 0.0) else "S"
+                    s = max(free.get(e, 0.0), ready_t[i])
+                    for b in bank[i]:
+                        s = max([s] + [f + WAKE for ee, f in held.get(b, {}).items() if ee != e])
+                    can.append((s, i, e))
             end, e = min((s + theta * c[i], e) for s, i, e in can)
-            _, i, st = min((-prio[i], i, s) for s, i, ee in can if ee == e and s <= end)
+            can = sorted((-prio[i], i, s) for s, i, ee in can if ee == e)
+            for k, (_, i, st) in enumerate(can):
+                if st <= end and all(st + theta * c[i] <= s for _, _, s in can[:k]):
+                    break
+            else:
+                free[e] = min(s for _, _, s in can if s > end)
+                continue
             took[i] = e
             ready[q[i]].remove(i)
             seq.append(i)
@@ -624,9 +687,14 @@ def _order(ops):
             fin = st + c[i]
             if q[i] != "R":
                 free[took[i]] = fin
+            for b in bank[i]:
+                held.setdefault(b, {})[e] = fin
             if dma[i] and forward:
                 free["D"] = max(fin + START, free.get("D", 0.0)) + dma[i]
                 fin = free["D"] - START - dma[i]
+            if rdma[i] and not forward:
+                free["D"] = max(fin - START - rdma[i], free.get("D", 0.0)) + rdma[i]
+                fin = free["D"] + START
             for k in after[i]:
                 ready_t[k] = max(ready_t[k], fin + lat[i if forward else k] + WAKE)
                 left[k] -= 1
@@ -634,26 +702,52 @@ def _order(ops):
                     ready.setdefault(q[k], []).append(k)
         return start, seq, took
 
-    base = [0.0] * n
+    def replay(seq, took, slow, gath, far):
+        fin, free, held = [0.0] * n, {}, {}
+        for i in seq:
+            e = took[i]
+            s = max([free.get(e, 0.0)] + [fin[d] + WAKE for d in pred[i]] +
+                    [f + WAKE for b in bank[i] for ee, f in held.get(b, {}).items() if ee != e])
+            f = s + c0[i] * (slow * (gath if ops[i]["n"][1:2] == "g" else 1.0) if e in "TVS" else 1.0)
+            if e != "R":
+                free[e] = f
+            for b in bank[i]:
+                held.setdefault(b, {})[e] = f
+            if dma[i]:
+                free["D"] = max(f + START * far, free.get("D", 0.0)) + dma[i] * far
+                f = free["D"] - (START + dma[i]) * far
+            fin[i] = f + lat[i] * (far if e == "R" else 1.0)
+        return max(fin)
+
+    c0, base = list(c), [0.0] * n
     for i in reversed(range(n)):
         base[i] = max([base[k] for k in succ[i]] + [0.0]) + c[i] + lat[i] + WAKE
     rs = np.random.RandomState(SEED)
-    best = None
-    for trial in range(TRIES):
-        prio = [float(p + (SPREAD * x if trial else 0.0)) for p, x in zip(base, rs.random_sample(n))]
+    best = _CHOSEN.get(n)
+    for trial in range(0 if best else TRIES):
+        prio = [float(p + SPREAD * x) for p, x in zip(base, rs.random_sample(n))]
+        theta, bias, slow = [float(a + (b - a) * rs.random_sample()) for a, b in (THETA, BIAS, SLOW)]
+        c[:] = [x * slow if e in "TVSX" else x for x, e in zip(c0, q)]
         for turn in range(TURNS):
-            start, seq, took = list_pass(pred, succ, prio, True, q)
-            span = max(start[i] + c[i] + lat[i] for i in range(n))
+            start, seq, took = list_pass(pred, succ, prio, True, theta, bias)
+            span = sum(replay(seq, took, *m[:3]) / m[3] for m in SETTINGS) if turn else 1e9
             if best is None or span < best[0] - 1e-9:
                 best = (span, start, seq, took)
-            back = list_pass(succ, pred, [start[i] + c[i] for i in range(n)], False, q)[0]
+            back = list_pass(succ, pred, [start[i] + c[i] for i in range(n)], False, theta, bias)[0]
             prio = [back[i] + c[i] for i in range(n)]
-    order = {}
+    _CHOSEN[n] = best
+    order, held = {}, {}
     for i in best[2]:
         ops[i]["st"], ops[i]["q"] = best[1][i], best[3][i]
+        for b in bank[i]:
+            for e, k in held.setdefault(b, {}).items():
+                if e != ops[i]["q"]:
+                    ops[i]["d"][k] = 1
+            held[b][ops[i]["q"]] = i
         if q[i] == "X":
             ops[i]["f"] = ops[i]["alt"][best[3][i]]
         order.setdefault(ops[i]["q"], []).append(ops[i])
+    order["Y"].sort(key=lambda o: (o["st"], o["i"]))
     return order
 
 

@@ -1,3 +1,4 @@
+import math
 import numpy as np
 from concourse.bass import DstId, RemoteDMATransfer
 from concourse.mybir import AluOpType as OP, ActivationFunctionType as AF, AxisListType as AX
@@ -6,28 +7,52 @@ V, H2 = 5, 2
 PCS = 2
 PE_NS, CY_NS, GATH = 0.4167, 0.83, 1.56
 LAT, WAKE = 4.5, 0.14
-SPREAD, SEED, TRIES, TURNS = 1.0, 849, 150, 6
-SC = 2.0 ** 23
-CL, CF, CP = -2.0 ** 21, 8192.0, 2.0 ** 21
-GATE = 2.0 ** 23
+SEED, TRIES, MOVES = 7, 700, 20000
+SC = 2.0 ** 25
+CL, CF, CP = -2.0 ** 24, 8192.0, 2.0 ** 21
+GATE = 2.0 ** 25
+MID = 2.0 ** 18 - 128 + 31.0 / 64
 START, DFOLD, DSMALL, BACK = 1.9, 2.8, 0.4, 2.8
 LTAB, FIRST = (0.0, 14.0, 25.0, 31.0), 2.0
 XW = 4096 + 16
 EDGE = {"a": ("pg", "sg"), "b": ("sg", "lg"), "c": ("pg", "lg"), "d": ("qg", "sg")}
-TESTS = {"a": (0, 0, -1, 0), "b": (SC, SC, -2, 0), "c": (0, -SC, 2, 0), "d": (-SC, 0, 0, 0), "o": (0, 0, 0, SC)}
+TESTS = {"a": (-1, 0, 0, 0), "b": (-2, SC, SC, 0), "c": (2, -SC, 0, 0), "d": (0, 0, -SC, 0), "o": (0, 0, 0, SC)}
 _CHOSEN = {}
-SLOW = (1.0, 1.1)
-SETTINGS = ((1.0, 1.0, 1.0, 50.0), (1.12, 0.83, 0.95, 105.0), (1.25, 1.0, 0.95, 125.0), (1.45, 1.22, 0.95, 158.0), (1.1, 1.0, 1.3, 120.0))
-THETA = (0.1, 0.5)
-BIAS = (0.3, 1.2)
+MOG = False
+FAR, GF, POWER = 1.0, 1.0, 25
+SETTINGS = ((1.15, 0.83, 0.9, 98.0), (1.05, 1.0, 1.0, 98.5), (1.3, 1.2, 1.0, 128.5), (1.05, 0.9, 1.2, 109.0))
+SLOW, BIAS = 0.15, 2.0
+HEAT, STEP = (0.07, 0.05, 0.01), 40
 
 
 def FOLD(t, h):
-    return "a" if (t, h) == (V - 1, H2 - 1) else "ab"
+    return "" if LESS(t, h) else {(4, 1): ""}.get((t, h), "ab")
+
+
+def MAX(t, h):
+    return {(4, 0): "c", (4, 1): "bc"}.get((t, h), "")
+
+
+def LESS(t, h):
+    return False
+
+
+def SRELU(t, h):
+    return ""
+
+
+def JOINM(t):
+    return False
+
+
+def JOINE(t):
+    return False
 
 
 def ENG(n, t, h):
-    return "X"
+    if n[1] == "g":
+        return "V" if n[-1] == "0" and n[0] in {(0, 0): "sp", (0, 1): "p"}.get((t, h), "l" if t == 4 or (t, h) == (2, 1) else "lp") else "S"
+    return "S" if t >= 0 else "SV"
 
 
 def QUARTERS(e, t, h):
@@ -39,7 +64,7 @@ def EFIRST(t, h):
 
 
 def BOTH(t, h):
-    return t == 4
+    return t > 0
 
 
 def CALLS(e, t, h):
@@ -51,7 +76,7 @@ def PIECES(nm, t, h):
 
 
 def BANKS(t, h):
-    return ("d0", "d0", "d0") if (t, h) == (4, 1) else ("bE", "bE", "d1")
+    return ("d0", "d0", "d0") if (t, h) == (4, 1) else ("bE", "bE", "d1" if h == 0 else "d0")
 
 
 def FUSED(t, h):
@@ -59,7 +84,7 @@ def FUSED(t, h):
 
 
 def OMAX(t, h):
-    return 4 * 1
+    return {(4, 0): 0}.get((t, h), 4)
 
 
 def _weights(t, h):
@@ -71,13 +96,13 @@ def _weights(t, h):
     for e, (x, y) in EDGE.items():
         if e == "d" and t:
             continue
-        if e in FOLD(t, h):
+        if e in FOLD(t, h) + MAX(t, h):
             add("m" + e, e, 2), add(x, e, -1), add(y, e, -1)
-        elif e == "d" and FUSED(t, h):
-            add("md", e, 2), add("qg", e, -1)
+        elif e == "d" and FUSED(t, h) or e in "bc" and LESS(t, h):
+            add("m" + e, e, 2), add(x, e, -1)
         else:
             add("m" + e, e, 2), add(x, e, -1), add(y, e, 1)
-    add("ao", "o", 2), add("sg" if t else "lg", "o", -1)
+    add("ao", "o", 2), add("sg" if t and not LESS(t, h) else "lg", "o", -1)
     out = {}
     for nm, c in w.items():
         nz = [i for i in range(4) if c[i]]
@@ -86,16 +111,21 @@ def _weights(t, h):
     return out
 
 
+def _row(i, run):
+    return [(r, j) for r, c in enumerate(ROWS) for j in range(5 - len(run) if i or len(run) == 1 else 1) if c[j:j + len(run)] == run][:1]
+
+
 RUNS = []
 for _t in range(V):
     for _h in range(H2):
-        RUNS += [_c for _, _c in _weights(_t, _h).values()]
-COEF = []
-for _c in sorted(set(RUNS), key=lambda c: (-len(c), c)):
-    if not any(tuple(COEF[i:i + len(_c)]) == _c for i in range(len(COEF))):
-        COEF += list(_c)
+        RUNS += list(_weights(_t, _h).values())
+ROWS = []
+for _i, _c in sorted(set(RUNS), key=lambda c: (-len(c[1]), c)):
+    if not _row(_i, _c):
+        ROWS.append((0,) * _i + _c + (0,) * (4 - _i - len(_c)))
+NR = len(ROWS)
 LONG = ("sg", "lg", "pg", "qg", "ma", "mb", "mc", "md", "ao", "mx")
-TWICE = ("sg", "pg", "qg")
+TURN = {"sg": 2, "pg": 3}
 
 SCRATCH, SEMAPHORES = {}, ["sT", "sV", "sS", "sG", "lsem"]
 
@@ -105,22 +135,27 @@ def _buf(name, cols, dtype, where="sbuf"):
 
 
 def _bn(nm, t, h):
-    return nm + str(h) + ("o" if nm in TWICE and t % 2 else "")
+    return nm + str(h) + "o" * (t % TURN.get(nm, 1))
 
 
-for _n in ("d0", "d1", "bY", "bA0", "bA1", "bB", "bD", "bE"):
+for _n in ("d0", "d1", "bY", "bD", "bE"):
     _buf(_n, 512, "float32", "psum")
+for _n in ("bA0", "bA1", "bA2"):
+    SCRATCH[_n] = ("psum", [128, 8, 16, 4], "float32")
+SCRATCH["fun"] = ("sbuf", [128, 8, 3 * NR, 4], "bfloat16")
+SCRATCH["rowlo"] = ("sbuf", [128, 8, 16, 4], "bfloat16")
 for _t in range(4):
     _buf("x%d" % _t, XW, "bfloat16")
     _buf("thm%d" % _t, 256, "bfloat16")
     _buf("wb%d" % _t, 128, "bfloat16")
-LANDS = sorted({_bn(_n, _t, _h) for _n in LONG for _t in range(2) for _h in range(2)})
+LANDS = sorted({_bn(_n, _t, _h) for _n in LONG for _t in range(V) for _h in range(2)})
 for _n in LANDS:
     _buf(_n, 2048, "bfloat16")
 for _h in range(2):
     for _n in ("fl", "fz", "absd"):
         _buf(_n + str(_h), 128, "bfloat16")
-ITMP, FTMP = ("z", "zs", "y", "r1", "t2"), ("m3", "r3", "m1", "ne", "sc")
+ITMP, FTMP = ("r1", "t2"), ("z", "y", "m3", "r3", "m1", "xq")
+_buf("eq", 256, "float16")
 _buf("itmp", len(ITMP) * 256, "int32")
 _buf("ftmp", len(FTMP) * 256, "float32")
 _buf("mo", V * 256, "bfloat16")
@@ -131,17 +166,15 @@ _buf("lst", 5 * 256, "float32")
 _buf("lh", 6 * 256, "float16")
 _buf("raw", 6 * 256, "int32")
 _buf("qst", 256, "float32")
-_buf("qh", 6 * 256, "float16")
 _buf("outs", 4 * 256, "float32")
-for _t in range(V + 1):
+for _t in range(V):
+    _buf("e%d" % _t, 272, "bfloat16")
+    _buf("eo%d" % _t, 272, "bfloat16")
     for _h in range(2):
-        _buf("e%d%d" % (_t, _h), 144, "bfloat16")
-        if _t < V:
-            _buf("eo%d%d" % (_t, _h), 144, "bfloat16")
-            SEMAPHORES.append("rm%d%d" % (_t, _h))
-            SEMAPHORES += ["f%s%d%d%d" % (_e, _t, _h, _w) for _e in FOLD(_t, _h) for _w in range(CALLS(_e, _t, _h))]
-            if _t:
-                SEMAPHORES.append("re%d%d" % (_t, _h))
+        SEMAPHORES.append("rm%d%d" % (_t, _h))
+        SEMAPHORES += ["f%s%d%d%d" % (_e, _t, _h, _w) for _e in FOLD(_t, _h) for _w in range(CALLS(_e, _t, _h))]
+        if _t:
+            SEMAPHORES.append("re%d%d" % (_t, _h))
 SEMAPHORES += ["rx1", "rx2", "rx3"] + ["px%d%d" % (_r, _w) for _r in range(4) for _w in range(2)]
 for _n in ("pl", "sl", "ll", "ql"):
     _buf("i_" + _n, 256, "int32")
@@ -150,8 +183,8 @@ _buf("i_tw", 2, "int32")
 _buf("i_th", 2, "int32")
 _buf("ka", 128, "float16")
 _buf("k37", 128, "float32")
-_buf("acol", 32, "int32")
-_buf("cnt", 1, "float32")
+_buf("acol", 1, "int32")
+_buf("cnt", 2 + V, "float32")
 _buf("onec", 128, "bfloat16")
 _buf("one32", 128, "float32")
 _buf("i32", 128, "float32")
@@ -160,9 +193,7 @@ _buf("n16", 128, "float16")
 for _n in ("one", "ib", "nib", "i1024", "im512", "i4096", "bt", "b128", "nbsc", "uj0", "uj1"):
     _buf(_n, 128, "bfloat16")
 _buf("msk", 2048 // PCS, "bfloat16")
-_buf("fun", 8 * len(COEF), "bfloat16")
 _buf("rowb", 384, "bfloat16")
-_buf("rowlo", 512, "bfloat16")
 LOADS = ["sl", "xt0", "xt1", "pl", "th", "wt", "ll", "ql", "ed0", "ed1"]
 STORES = ["%s%d" % (_n, _h) for _n in ("yp", "ys", "yl", "yq", "ye") for _h in range(2)]
 SEMAPHORES += ["d_" + _n for _n in LOADS + STORES]
@@ -230,7 +261,7 @@ def _plan(g, core, T, topo):
         o = {"q": q, "c": cost, "f": fns, "d": {}, "sig": sig, "lat": lat, "i": len(ops), "n": (list(w) + list(a) + list(r) + ["?"])[0]}
         for x in after:
             o["d"][x["i"]] = 1
-        r, w, a, b = [[k + half[0] if k in ("A", "A1", "bA") else k for k in ks] for ks in (r, w, a, b)]
+        r, w, a, b = [[k + half[0] if k in ("A", "AL", "AG", "bA") else k for k in ks] for ks in (r, w, a, b)]
         for k in r:
             for x in [last_w.get(k)] + accs.get(k, []):
                 if x is not None:
@@ -273,13 +304,11 @@ def _plan(g, core, T, topo):
     def vs(fv, fs, n, **kw):
         o = op("X", vec(n), None, **kw)
         o["alt"] = {"V": [fv], "S": [fs]}
-        e = ENG(o["n"], *now)
-        if e != "X":
-            o["q"], o["f"] = e, o["alt"][e]
+        o["e"] = ENG(o["n"], *now)
         return o
 
-    def scaled(out, a, c, n, **kw):
-        return vs(ts(out, a, float(c), OP.mult), act(out, a, AF.Copy, 0.0, float(c)), n, **kw)
+    def scaled(out, x, c, n, **kw):
+        return vs(ts(out, x, float(c), OP.mult), act(out, x, AF.Copy, 0.0, float(c)), n, **kw)
 
     def shifted(out, a, c, n, **kw):
         return vs(ts(out, a, float(c), OP.add), act(out, a, AF.Copy, float(c)), n, **kw)
@@ -303,15 +332,15 @@ def _plan(g, core, T, topo):
 
     def load(name, out, in_, key):
         return op("Y", 0.0, [lambda: g.sync.dma_start(out, in_)], w=[key], sig=("d_" + name, 16),
-                  lat={"sl": 2.2, "xt0": 3.1, "xt1": 3.9}.get(name, 3.7 + 0.1 * len(ops)))
+                  lat={"sl": 2.2, "xt0": 3.1, "th": 3.2, "wt": 3.25, "xt1": 4.0}.get(name, 3.7 + 0.1 * len(ops)))
 
     def send(name, out, in_, dst, eng, key, lat, rkey, after=()):
         eng = [e for e in eng]
         m = sum(1 << e for e in eng)
         rid, pid, _ = topo.addr(dst)
-        so = op("G", 1.3, [lambda: g.remote_dma(out, in_, T.sem[name], T.sem["lsem"], pid, rid, m)], r=[key], sig=("send", len(eng)), after=after)
+        so = op("G", 1.3, [lambda: g.remote_dma(out, in_, T.sem[name], T.sem["lsem"], pid, rid, m)], r=key, sig=("send", len(eng)), after=after)
         so["dma"] = DSMALL
-        op("R", 0.0, [], w=[rkey], sig=(name, len(eng)), after=[so], lat=lat)
+        op("R", 0.0, [], w=rkey, sig=(name, len(eng)), after=[so], lat=lat)
         return so
 
     def dst(k):
@@ -323,14 +352,14 @@ def _plan(g, core, T, topo):
 
     load("sl", T.i_sl[:], T.sl[:], "i_sl")
     load("xt0", T.x0[:, 0:XW // 2], T.xt[:, 0:XW // 2], "x0")
-    load("xt1", T.x0[:, XW // 2:4096], T.xt[:, XW // 2:4096], "x0b")
-    load("ll", T.i_ll[:], T.ll[:], "i_ll")
     load("th", T.i_tw[:, 0:1], T.th[:], "i_th")
     load("wt", T.i_tw[:, 1:2], T.wt[:], "i_wt")
+    load("xt1", T.x0[:, XW // 2:4096], T.xt[:, XW // 2:4096], "x0b")
     load("pl", T.i_pl[:], T.pl[:], "i_pl")
+    load("ll", T.i_ll[:], T.ll[:], "i_ll")
     load("ql", T.i_ql[:], T.ql[:], "i_ql")
-    load("ed0", T.e00[:, 0:128], T.ed[:, 0:128], "e00")
-    load("ed1", T.e01[:, 0:128], T.ed[:, 128:256], "e01")
+    load("ed0", T.e0[:, 0:128], T.ed[:, 0:128], "e00")
+    load("ed1", T.e0[:, 128:256], T.ed[:, 128:256], "e01")
     ms = lambda ap, c: (lambda: g.vector.memset(ap, c))
     v(ms(T.one32[:], 1.0), 128, w=["one32"])
     v(ms(T.one[:], 1.0), 128, 0.5, w=["one"])
@@ -348,15 +377,19 @@ def _plan(g, core, T, topo):
     scaled(T.nbsc[:], T.b128[:], -SC, 128, r=["b128"], w=["nbsc"])
     v(ms(T.msk[:], 1.0), 2048 // PCS, 0.5, w=["msk"])
     v(ms(T.msk[:, 0::16], 0.0), 128 // PCS, 0.5, w=["msk"])
-    for i, c in enumerate(COEF):
-        scaled(T.fun[:, 8 * i:8 * i + 8], T.b128[:, 0::16], c, 8, r=["b128"], w=["fun%d" % i])
-    v(ms(T.rowb[0:2, 0:256], CL), 256, 0.5, w=["rowb0", "rowb128"])
-    for nm, a, b, c in (("rowlo", 0, 256, -SC / 2), ("rowlo", 256, 384, 0.0), ("rowlo", 384, 512, SC / 2),
-                        ("rowb", 0, 128, 2048.0), ("rowb", 128, 256, 2048.0 + CF), ("rowb", 256, 384, 129.0 * 4096)):
-        v(ms(T[nm][0:1, a:b], c), b - a, 0.5, w=[nm + str(a)])
+    v(ms(T.fun[:], 0.0), 96 * NR, 0.5, w=["fun"])
+    for r, row in enumerate(ROWS):
+        for i, c in enumerate(row):
+            if c:
+                scaled(T.fun[:, :, 2 * NR + r, i], T.b128[:, 0::16], c, 8, r=["b128"], a=["fun"])
+    v(cp(T.fun[:, :, 0:NR, 0], T.fun[:, :, 2 * NR:, 0]), 8 * NR, 0.5, r=["fun"], w=["funx"])
+    v(cp(T.fun[:, :, NR:2 * NR, 1:4], T.fun[:, :, 2 * NR:, 1:4]), 24 * NR, 0.5, r=["fun"], w=["funt"])
+    for p, a, c in ((2, 0, CL), (2, 128, CL + 2.0 ** 18), (1, 0, 2048.0), (1, 128, 2048.0 + CF - 128), (1, 256, 129.0 * 4096)):
+        v(ms(T.rowb[0:p, a:a + 128], c), 128, 0.5, w=["rowb%d" % a])
+    for i, c in enumerate((0.0, -SC / 2, CL, SC / 2)):
+        v(ms(T.rowlo[0:1, :, :, i], c), 128, 0.5, a=["rowlo"])
     for h in range(H2):
         v(ms(T["fz%d" % h][:], 0.0), 128, 0.5, w=["fz0%d" % h])
-    CK = ["rowlo0", "rowlo256", "rowlo384"]
     CB_ = ["rowb0", "rowb128", "rowb256"]
     one_row = T.one[0:1, :]
     v(ts(T.i_th[:, 0:1], T.i_tw[:, 0:1], 4, OP.arith_shift_right), 1, r=["i_th"], w=["thh"])
@@ -399,15 +432,14 @@ def _plan(g, core, T, topo):
     for nm, i in (("sl", 1), ("pl", 0), ("ll", 2)):
         v(cp(T.u16l[:, 256 * i:256 * i + 256], T["i_" + nm][:]), 256, r=["i_" + nm], w=["u16l%d0" % i, "u16l%d1" % i])
     v(cp(T.u16q[:, 0:256], T.i_ql[:]), 256, r=["i_ql"], w=["u16q00", "u16q01"])
-    for nm in ("ll", "ql", "pl", "sl"):
-        v(ts(T["f_" + nm][:], T["i_" + nm][:], 2048.0, OP.subtract), 256, r=["i_" + nm], w=["f_" + nm])
+    for nm, lst, i in (("ll", "u16l", 2), ("ql", "u16q", 0), ("pl", "u16l", 0), ("sl", "u16l", 1)):
+        v(ts(T["f_" + nm][:], T[lst][:, 256 * i:256 * i + 256], 2048.0, OP.subtract), 256, 0.5, r=["%s%d0" % (lst, i)], w=["f_" + nm])
 
     def first_page_form(h):
         hs = slice(128 * h, 128 * h + 128)
         for c, nm in enumerate(("ll", "ql", "pl", "sl")):
             mm([MM(T.bE[:, 128 * c:128 * c + 128], T["f_" + nm][:, hs], T.i16[:], True, True)], 128, r=["f_" + nm, "i16"], w=["bE%d" % c], b=["bE"])
         v(cp(cb("lh", 0, h), T.bE[:, 0:128]), 128, r=["bE0"], w=["lh0%d" % h], b=["bE"])
-        v(cp(cb("qh", 0, h), T.bE[:, 128:256]), 128, r=["bE1"], w=["qh0%d" % h], b=["bE"])
         shifted(cb("qst", 0, h), T.bE[:, 128:256], 2048.0, 128, r=["bE1"], w=["qst0%d" % h], b=["bE"])
         v(ts(cb("raw", 0, h), T.bE[:, 0:128], 2048.0, OP.add), 128, r=["bE0"], w=["raw0%d" % h], b=["bE"])
         for i, c in ((0, 2), (1, 3)):
@@ -461,9 +493,26 @@ def _plan(g, core, T, topo):
                     mm([MM(T[d][:], T[mat][:], B[nm][:, sl], st, not st)], 512, r=[K(nm, gp), mat], w=q4(d), b=[d])
                 relu(B["m" + e][:, sl], T[d][:], 512, r=q4(d), w=[K("m" + e, j)], b=[d])
 
-        gather("sg", "u16l", t + 1)
-        first[(t, h)] = gather("pg", "u16l", t)
-        gather("lg", "u16l", t + 2)
+        def less(nm, lst, i, y, e):
+            n = PIECES(nm, t, h)
+            for j in range(n):
+                sl = slice(2048 // n * j, 2048 // n * (j + 1))
+                v(tt(B[nm][:, sl], win.indirect(off(lst, i, j, n)), B[y][:, sl], OP.subtract), 2048 // n * GATH + 70,
+                  r=xk + ["%s%d%d" % (lst, i, h)] + KP(y, j, n), w=KP(nm, j, n))
+                kw = dict(r=KP(nm, j, n), w=KP("m" + e, j, n))
+                if e in SRELU(t, h):
+                    s(act(B["m" + e][:, sl], B[nm][:, sl], AF.Relu), 2048 // n, **kw)
+                else:
+                    v(ts(B["m" + e][:, sl], B[nm][:, sl], 0.0, OP.max), 2048 // n, 0.5, **kw)
+
+        if LESS(t, h):
+            gather("lg", "u16l", t + 2)
+            less("sg", "u16l", t + 1, "lg", "b")
+            less("pg", "u16l", t, "lg", "c")
+        else:
+            gather("sg", "u16l", t + 1)
+            first[(t, h)] = gather("pg", "u16l", t)
+            gather("lg", "u16l", t + 2)
         if t == 0 and not FUSED(t, h):
             gather("qg", "u16q", t)
         for grp in ("a", "d", "bc"):
@@ -474,36 +523,32 @@ def _plan(g, core, T, topo):
             v(lambda a=B["mx"][:, sl], b=B["lg"][:, sl]: g.vector.tensor_tensor_scan(a, T.msk[:], b, 0.0, OP.mult, OP.max), P, 0.5,
               r=["msk"] + KP("lg", j), w=[K("mx", j)])
         mo = "mo%d%d" % (t, h)
-        v(cp(cb("mo", t, h), B["mx"][:, 15::16]), 128, 0.5, r=[K("mx", j) for j in range(PCS)], w=[mo])
+        if MOG:
+            gq(lambda: g.affine_select(cb("mo", t, h), B["mx"][:, 15::16], [[0, 128]], OP.is_ge, 0.0, 0, 0), 128, r=[K("mx", j) for j in range(PCS)], w=[mo])
+        else:
+            v(cp(cb("mo", t, h), B["mx"][:, 15::16]), 128, 0.5, r=[K("mx", j) for j in range(PCS)], w=[mo])
         d2 = dst(2)
-        send("rm%d%d" % (t, h), cb("mi", t, h), cb("mo", t, h), d2, topo.engines(core, d2)[:8], mo, LAT, "mi%d%d" % (t, h))
+        if h or not JOINM(t):
+            hs = range(0 if JOINM(t) else h, h + 1)
+            send("rm%d%d" % (t, h), cb("mi", t, hs[0], 128 * len(hs)), cb("mo", t, hs[0], 128 * len(hs)), d2, topo.engines(core, d2)[:8],
+                 ["mo%d%d" % (t, a) for a in hs], LAT, ["mi%d%d" % (t, a) for a in hs])
         if FUSED(t, h):
-            for j in range(PCS):
-                sl = slice(P * j, P * j + P)
-                v(tt(B["qg"][:, sl], win.indirect(off("u16q", t, j)), B["sg"][:, sl], OP.subtract), P * GATH,
-                  r=xk + ["u16q%d%d" % (t, h)] + KP("sg", j), w=KP("qg", j))
-                v(ts(B["md"][:, sl], B["qg"][:, sl], 0.0, OP.max), P, 0.5, r=KP("qg", j), w=KP("md", j))
-        for e in "abc" if t or FUSED(t, h) else "abcd":
-            if e not in fo:
+            less("qg", "u16q", t, "sg", "d")
+        for e in "a" if LESS(t, h) else "abc" if t or FUSED(t, h) else "abcd":
+            if e not in fo + MAX(t, h):
                 size(e)
-            for j in range(QUARTERS(e, t, h), 4) if e in fo else []:
-                d, sl, gp = turn(), slice(512 * j, 512 * j + 512), j
-                x_, y_ = EDGE[e]
-                mm([MM(T[d][:], T.ib[:], B[x_][:, sl], True, True)], 512, r=[K(x_, gp), "ib"], w=q4(d), b=[d])
-                v(tt(B["m" + e][:, sl], B[y_][:, sl], T[d][:], OP.max), 512, r=q4(d) + [K(y_, gp)], w=[K("m" + e, j)], b=[d])
-        e, ol = "e%d%d" % (t, h), "sg" if t else "lg"
-        if OMAX(t, h):
-            d = "Ec" + hh
-            mm([MM(cb("bY", 1, h), T.ib[:], T[e][:, 0:128], True, True)], 128, r=[e, "ib"], w=[d], b=["bY"])
-            for k in range(4 * OMAX(t, h)):
-                v(tt(B["ao"][:, 128 * k:128 * k + 128], B[ol][:, k::16], cb("bY", 1, h), OP.max), 128,
-                  r=KP(ol, 0, 1) + [d], a=[K("ao", k // 4)], b=["bY"])
+            for j in range(QUARTERS(e, t, h), 4) if e in fo else range(4) if e in MAX(t, h) else []:
+                sl, (x_, y_) = slice(512 * j, 512 * j + 512), EDGE[e]
+                v(tt(B["m" + e][:, sl], B[x_][:, sl], B[y_][:, sl], OP.max), 512, r=[K(x_, j), K(y_, j)], w=[K("m" + e, j)])
+        e, ol, ed = "e%d%d" % (t, h), "sg" if t and not LESS(t, h) else "lg", cb("e%d" % t, 0, h)
+        for k in range(4 * OMAX(t, h)):
+            v(tt(B["ao"][:, 128 * k:128 * k + 128], B[ol][:, k::16], ed, OP.max), 128, r=KP(ol, 0, 1) + [e], a=[K("ao", k // 4)])
         for j in range(OMAX(t, h), 4):
             d = turn()
             fn = []
             for i in range(4):
                 o_ = T[d][:, 128 * i:128 * i + 128]
-                fn += [MM(o_, T.ib[:], B[ol][:, 4 * j + i::16], True, False), MM(o_, T.nib[:], T[e][:, 0:128], False, True)]
+                fn += [MM(o_, T.ib[:], B[ol][:, 4 * j + i::16], True, False), MM(o_, T.nib[:], ed, False, True)]
             mm(fn, 1024, r=KP(ol, 0, 1) + [e, "ib", "nib"], w=q4(d), b=[d])
             relu(B["ao"][:, 512 * j:512 * j + 512], T[d][:], 512, r=q4(d), w=[K("ao", j)], b=[d])
 
@@ -511,98 +556,109 @@ def _plan(g, core, T, topo):
         hh, n = str(h), 128
         tm = t % 4
         B = {nm: T[_bn(nm, t, h)] for nm in LONG}
-        A, Bb, D, E = T["bA" + hh], T.bB, T.bD, T.bE
-        half[0] = hh
+        half[0] = str((2 * t + h) % 3)
+        A, D = T["bA" + half[0]], T.bD
         k_ = lambda nm: nm + hh
         pcs = lambda nm: [_bn(nm, t, h) + "p%d" % j for j in range(4)]
         fl = T["fl" + hh]
         it = lambda nm: cb("itmp", ITMP.index(nm), h)
         ft = lambda nm: cb("ftmp", FTMP.index(nm), h)
         e, eo, mi = "e%d%d" % (t, h), "eo%d%d" % (t, h), "mi%d%d" % (t, h)
-        mm([MM(A[:], one_row, T.rowlo[0:1, :], True, False)], 512, r=["one"] + CK, w=["A"], b=["bA"])
-        mm([MM(A[:, 384:512], T.one[:], T["thm%d" % tm][:, 0:128], False, False)], 128, r=["one", "thm%d" % tm], a=["A"], b=["bA"])
+        ed, edo = cb("e%d" % t, 0, h), cb("eo%d" % t, 0, h)
+        XF, X1, X2, X3 = A[:, :, 0, 0], A[:, :, :, 1], A[:, :, :, 2], A[:, :, :, 3]
+        mm([MM(A[:], one_row, T.rowlo[0:1], True, False)], 512, r=["one", "rowlo"], w=["A"], b=["bA"])
+        for i, key in enumerate(("thm", "thn")[:2 if t else 1]):
+            mm([MM(X3, T.one[:], T["thm%d" % tm][:, 128 * i:128 * i + 128], False, False)], 128, r=["one", key + str(tm)], a=["A"], b=["bA"])
 
         def sums(nm, i, run):
-            c = [j for j in range(len(COEF)) if tuple(COEF[j:j + len(run)]) == run][0]
-            fn = []
+            (r, j), w, fn = _row(i, run)[0], len(run), []
             for k in range(16):
                 lt = B[nm][:, 128 * k:128 * k + 128] if nm == "ao" else B[nm][:, k::16]
-                fn.append(MM(A[:, 128 * i + k:128 * (i + len(run)):16], lt, T.fun[:, 8 * c:8 * (c + len(run))], False, False))
-            mm(fn, 64 * len(fn), r=pcs(nm) + ["fun%d" % j for j in range(c, c + len(run))], a=["A"], b=["bA"])
+                if i == 0 and w > 1 and k:
+                    fn.append(MM(A[:, :, 0:k + 1:k, 0:w], lt, T.fun[:, :, r:NR + r + 1:NR, 0:w], False, False))
+                else:
+                    fn.append(MM(A[:, :, k if i else 0, i:i + w], lt, T.fun[:, :, 2 * NR + r, j:j + w], False, False))
+            mm(fn, 64 * len(fn), r=pcs(nm) + ["fun", "funx", "funt"], a=["A"], b=["bA"])
 
         for nm, (i, run) in _weights(t, h).items():
             sums(nm, i, run)
-        c = COEF.index(2 * SC)
-        mm([MM(A[:, 384:512], T[e][:, 0:128], T.nbsc[:], False, False)] +
-           [MM(A[:, 384 + k:512:16], T[e][:, 0:128], T.fun[:, 8 * c:8 * c + 8], False, False) for k in range(4 * OMAX(t, h), 16)],
-           128 + 256 * (4 - OMAX(t, h)), r=[e, "nbsc", "fun%d" % c], a=["A"], b=["bA"])
-        mm([MM(A[:, 384:512], T.one[:], T["thm%d" % tm][:, 128:256], False, True)], 128, r=["one", "thn%d" % tm], w=["A"], b=["bA"])
-        X2, X1, XF, X3 = [A[:, 128 * i:128 * i + 128] for i in range(4)]
-        U = cb("bB", h, 1)
-        mm([MM(U, T[e][:, 0:128], T["wb%d" % tm][:], True, True)], 128, r=[e, "wb%d" % tm], w=[k_("U")], b=["bB"])
+        r, j = _row(3, (2 * SC,))[0]
+        mm([MM(X3, ed, T.nbsc[:], False, False)] +
+           [MM(A[:, :, k, 3], ed, T.fun[:, :, 2 * NR + r, j], False, False) for k in range(4 * OMAX(t, h), 16)],
+           128 + 256 * (4 - OMAX(t, h)), r=[e, "nbsc", "fun"], a=["A"], b=["bA"])
+        if t:
+            mm([MM(X2, one_row, T.rowb[0:1, 0:128], False, False), MM(X2, T.i16[:], cb("lh", t, h), False, True)], 256,
+               r=["one", "i16", "lh%d%d" % (t, h)] + CB_, w=["A"], b=["bA"])
+        else:
+            mm([MM(X3, T.one[:], T.thm0[:, 128:256], False, True)], 128, r=["one", "thn0"], w=["A"], b=["bA"])
+        U = cb("bY", 1, h)
+        mm([MM(U, ed, T["wb%d" % tm][:], True, True)], 128, r=[e, "wb%d" % tm], w=[k_("U")], b=["bY"])
         uj, c4 = T["uj" + hh][:], 128.5 + 1.0 / 8192
-        vs(ts(uj, U, 1.0 / 4096, OP.mult, c4, OP.add), act(uj, U, AF.Copy, c4, 1.0 / 4096), n, r=[k_("U")], w=[k_("uj")], b=["bB"])
-        mm([MM(U, T[e][:, 0:128], T["wb%d" % tm][:], True, False), MM(U, one_row, T.rowb[0:1, 256:384], False, False),
-            MM(U, T.i4096[:], uj, False, True)], 3 * 128, r=[e, "wb%d" % tm, "one", "i4096", k_("uj")] + CB_, w=[k_("U")], b=["bB"])
+        vs(ts(uj, U, 1.0 / 4096, OP.mult, c4, OP.add), act(uj, U, AF.Copy, c4, 1.0 / 4096), n, r=[k_("U")], w=[k_("uj")], b=["bY"])
+        mm([MM(U, ed, T["wb%d" % tm][:], True, False), MM(U, one_row, T.rowb[0:1, 256:384], False, False),
+            MM(U, T.i4096[:], uj, False, True)], 3 * 128, r=[e, "wb%d" % tm, "one", "i4096", k_("uj")] + CB_, w=[k_("U")], b=["bY"])
         if (t, h) == (0, 0):
             v(cp(T.ka[:], T.k37[:]), n, r=["k37"], w=["ka"])
         lh, raw = cb("lh", t, h), cb("raw", t, h)
         qo, qk = (cb("raw", t - 1, h), "raw%d%d" % (t - 1, h)) if t else (cb("qst", 0, h), "qst0%d" % h)
-        PL, PY = cb("bB", h, 0), cb("bY", 0, h)
-        mm([MM(PL, T.one[0:2, :], T.rowb[0:2, 0:128], True, False), MM(PL, T.i16[:], lh, False, True)], 2 * 128,
-           r=["one", "i16", "lh%d%d" % (t, h)] + CB_, w=[k_("B")], b=["bB"])
+        bE = BANKS(t, h)[0]
+        E, (E0, E1, E2, E3) = T[bE], [bE + str(i) for i in range(4)]
+        PL, PY = E[:, 256:384], cb("bY", 0, h)
         if t + 2 < V:
-            shifted(cb("lst", t + 2, h), PL, CP - CL, n, r=[k_("B")], w=["lst%d%d" % (t + 2, h)], b=["bB"])
-        fn = [MM(PY, T.one[0:2, :], T.rowb[0:2, 128:256], True, False), MM(PY, T.i16[:], lh, False, False), MM(PY, T.i16[:], T.ka[:], False, t == 0)]
-        if t:
-            fn += [MM(T.bY[:, 128 * h + 16 * i:128 * h + 16 * i + 16], one_row, T["e%d1" % t][0:1, 128:144], False, i == 7) for i in range(8)]
-        mm(fn, 3 * 128 + (8 * 64 if t else 0), r=["one", "i16", "lh%d%d" % (t, h), "ka", "e%d1" % t] + CB_, w=[k_("PY")], b=["bY"])
-        v(tt(it("z"), raw, U, OP.mult), n, r=[k_("U"), "raw%d%d" % (t, h)], w=[k_("z")], b=["bB"])
-        v(ts(it("zs"), it("z"), 5, OP.arith_shift_right), n, r=[k_("z")], w=[k_("zs")])
-        v(tt(it("y"), it("zs"), PY, OP.add), n, r=[k_("zs"), k_("PY")], w=[k_("y")], b=["bY"])
+            mm([MM(PL, T.one[0:2, :], T.rowb[0:2, 0:128], True, False), MM(PL, T.i16[:], lh, False, True)], 2 * 128,
+               r=["one", "i16", "lh%d%d" % (t, h)] + CB_, w=[E2], b=[bE])
+            shifted(cb("lst", t + 2, h), PL, CP - CL, n, r=[E2], w=["lst%d%d" % (t + 2, h)], b=[bE])
+        fn = [MM(PY, T.one[0:2, :], T.rowb[0:2, 128:256], True, False), MM(PY, T.i16[:], lh, False, False), MM(PY, T.i16[:], T.ka[:], False, True)]
+        mm(fn, 3 * 128, r=["one", "i16", "lh%d%d" % (t, h), "ka"] + CB_, w=[k_("PY")], b=["bY"])
+        v(tt(ft("z"), raw, U, OP.mult), n, r=[k_("U"), "raw%d%d" % (t, h)], w=[k_("z")], b=["bY"])
+        ac = T.cnt[:, 2 + t:3 + t]
+        if h == 0 and t:
+            shifted(ac, T["e%d" % t][:, 256:257], -MID, 1, r=["e%d1" % t], w=["am%d" % t])
+        elif h == 0:
+            v(ms(ac, -MID), 1, w=["am0"])
+        vs(ts(ft("z"), ft("z"), 1.0 / 32, OP.mult, ac, OP.add), act(ft("z"), ft("z"), AF.Identity, ac, 1.0 / 32), n, r=["am%d" % t, k_("z")], w=[k_("z")])
+        v(tt(ft("y"), ft("z"), PY, OP.add), n, r=[k_("z"), k_("PY")], w=[k_("y")], b=["bY"])
         ms_, fz = T.msk[:, 0:128], T["fz" + hh]
-        v(lambda: g.vector.tensor_tensor_scan(ft("sc"), ms_, XF, 0.0, OP.mult, OP.add), n, r=["A", "msk"], w=[k_("sc")], b=["bA"])
-        v(ts(fz[:, 0::16], T.ftmp[:, FTMP.index("sc") * 256 + 128 * h + 15:FTMP.index("sc") * 256 + 128 * h + 128:16], 0.0, OP.is_ge, GATE, OP.mult), 8,
-          r=[k_("sc"), "fz0" + hh], w=[k_("fz")])
+        v(ts(fz[:, 0::16], XF, 0.0, OP.is_ge, GATE, OP.mult), 8, r=["A", "fz0" + hh], w=[k_("fz")], b=["bA"])
         v(lambda: g.vector.tensor_tensor_scan(fl[:], ms_, fz[:], 0.0, OP.mult, OP.add), n, 0.5, r=["msk", k_("fz")], w=[k_("fl") + "a"])
         FL = [k_("fl") + "a"]
-        mm([MM(D[:, 256:384], T.ib[:], T[e][:, 0:128], True, False), MM(D[:, 256:384], T.nib[:], cb("mi", t, h), False, True)], 256,
+        mm([MM(D[:, 256:384], T.ib[:], ed, True, False), MM(D[:, 256:384], T.nib[:], cb("mi", t, h), False, True)], 256,
            r=[e, mi, "ib", "nib"], w=["Dd"], b=["bD"])
         absd = T["absd" + hh][:]
         s(act(absd, D[:, 256:384], AF.Abs), n, r=["Dd"], w=[k_("absd")], b=["bD"])
-        mm([MM(D[:, 384:512], T.ib[:], T[e][:, 0:128], True, False), MM(D[:, 384:512], T.ib[:], cb("mi", t, h), False, False),
+        mm([MM(D[:, 384:512], T.ib[:], ed, True, False), MM(D[:, 384:512], T.ib[:], cb("mi", t, h), False, False),
             MM(D[:, 384:512], fl[:], T.i1024[:], False, True),
             MM(D[:, 128:256], fl[:], T.im512[:], True, False), MM(D[:, 128:256], T.ib[:], absd, False, True)], 5 * 128,
            r=FL + [e, mi, k_("absd"), "ib", "im512", "i1024"], w=["De"], b=["bD"])
         v(ts(it("t2"), D[:, 384:512], 0.5, OP.mult, 512.25, OP.subtract), n, r=["De"], w=[k_("t2")], b=["bD"])
-        v(tt(T[eo][:, 0:128], it("t2"), D[:, 128:256], OP.max), n, r=[k_("t2"), "De"], w=[eo], b=["bD"])
+        v(tt(edo, it("t2"), D[:, 128:256], OP.max), n, r=[k_("t2"), "De"], w=[eo], b=["bD"])
         if t < V - 1:
             if h == 1:
                 mm([MM(D[:, 0:8], T.onec[:], T["fl%d" % a][:, 0::16], a == 0, a == 1) for a in range(2)], 128, r=FL + ["fl0a", "onec"], w=["Du"], b=["bD"])
-                v(lambda: g.vector.tensor_reduce(T.cnt[:, 0:1], D[:, 0:8], AX.X, OP.add), 8, r=["Du"], w=["cnt"], b=["bD"])
-                v(ts(T.acol[:, 0:16], T.one32[:, 0:16], T.cnt[:, 0:1], OP.mult, -1.0, OP.mult), 16, r=["cnt", "one32"], w=["ac0"])
-                v(ts(T.acol[:, 16:32], T.acol[:, 0:16], 31, OP.bitwise_and), 16, r=["ac0"], w=["ac1"])
-                v(cp(T[eo][:, 128:144], T.acol[:, 16:32]), 16, r=["ac1"], w=[eo + "A"])
+                v(lambda: g.vector.tensor_reduce(T.cnt[:, 0:1], D[:, 0:8], AX.X, OP.add, negate=True), 8, r=["Du"], w=["cnt"], b=["bD"])
+                v(ts(T.acol[:], T.cnt[:, 0:1], 15.5, OP.subtract, 1.0 / 32, OP.mult), 1, r=["cnt"], w=["ac0"])
+                v(ts(T["eo%d" % t][:, 256:257], T.acol[:], -32.0, OP.mult, T.cnt[:, 0:1], OP.add), 1, r=["ac0", "cnt"], w=[eo + "A"])
             d1 = dst(-1)
-            en = "e%d%d" % (t + 1, h)
-            wd = 128 + 16 * h
-            sentE[h] = send("re%d%d" % (t + 1, h), T[en][:, 0:wd], T[eo][:, 0:wd], d1, topo.engines(core, d1)[-8:], eo, LAT, en,
-                 after=[last_w[eo + "A"]] if h else [])
+            if h or not JOINE(t):
+                hs = range(0 if JOINE(t) else h, h + 1)
+                sl = slice(128 * hs[0], 128 + 129 * h)
+                sentE[h] = send("re%d%d" % (t + 1, h), T["e%d" % (t + 1)][:, sl], T["eo%d" % t][:, sl], d1, topo.engines(core, d1)[-8:],
+                                ["eo%d%d" % (t, a) for a in hs] + [eo + "A"] * h, LAT, ["e%d%d" % (t + 1, a) for a in hs])
         else:
-            op("Y", 0.1, [lambda: g.sync.dma_start(T.ye[:, 128 * h:128 * h + 128], T[eo][:, 0:128])], r=[eo], sig=("d_ye%d" % h, 16), lat=2.0)
+            op("Y", 0.1, [lambda: g.sync.dma_start(T.ye[:, 128 * h:128 * h + 128], edo)], r=[eo], sig=("d_ye%d" % h, 16), lat=2.0)
         pst, last = cb("lst", t, h), t == V - 1
-        lk, ln, qh, qhk = "lh%d%d" % (t, h), "lh%d%d" % (t + 1, h), cb("qh", t, h), "qh%d%d" % (t, h)
+        lk, ln = "lh%d%d" % (t, h), "lh%d%d" % (t + 1, h)
         if last:
-            mm([MM(D[:, 0:128], qh, T.i16[:], True, True)], 128, r=["i16", qhk], w=["Du"], b=["bD"])
-            shifted(cb("qst", 0, h), D[:, 0:128], 2048.0, n, r=["Du"], w=["qst0%d" % h], b=["bD"])
-        bE = BANKS(t, h)[0]
-        E, (E0, E1, E2, E3) = T[bE], [bE + str(i) for i in range(4)]
-        v(tt(ft("m3"), it("y"), X3, OP.min), n, r=[k_("y"), "A"], w=[k_("m3")], b=["bA"])
-        v(tt(ft("r3"), ft("m3"), PL, OP.max), n, r=[k_("m3"), k_("B")], w=[k_("r3")], b=["bB"])
+            mm([MM(D[:, 0:128], one_row, T.rowb[0:1, 0:128], True, False), MM(D[:, 0:128], lh, T.i16[:], False, True)], 2 * 128,
+               r=["one", "i16", lk] + CB_, w=["Du"], b=["bD"])
+        v(tt(ft("m3"), ft("y"), X3, OP.min), n, r=[k_("y"), "A"], w=[k_("m3")], b=["bA"])
+        r3 = "m3" if t else "r3"
+        if not t:
+            v(tt(ft("r3"), ft("m3"), PL, OP.max), n, r=[k_("m3"), E2], w=[k_("r3")], b=[bE])
         v(tt(E[:, 0:128], qo, X2, OP.min), n, r=[qk, "A"], w=[E0], b=["bA", bE])
         v(tt(E[:, 128:256], pst, X1, OP.min), n, r=["lst%d%d" % (t, h), "A"], w=[E1], b=["bA", bE])
         v(tt(ft("m1"), E[:, 128:256], fl[:], OP.subtract), n, r=FL + [E1], w=[k_("m1")], b=[bE])
-        v(tt(E[:, 0:128], ft("r3"), E[:, 0:128], OP.max), n, r=[k_("r3"), E0], w=[E0], b=[bE])
+        v(tt(E[:, 0:128], ft(r3), E[:, 0:128], OP.max), n, r=[k_(r3), E0], w=[E0], b=[bE])
         v(tt(it("r1"), ft("m1"), E[:, 0:128], OP.max), n, r=[k_("m1"), E0], w=[k_("r1")], b=[bE])
         nw, nk, lhn = cb("raw", t + 1, h), "raw%d%d" % (t + 1, h), cb("lh", t + 1, h)
         v(ts(nw, it("r1"), 4095, OP.bitwise_and), n, r=[k_("r1")], w=[nk])
@@ -610,15 +666,25 @@ def _plan(g, core, T, topo):
         mm([MM(E[:, 256:384], lhn, T.i16[:], True, True)], 128, r=["i16", ln], w=[E2], b=[bE])
         if not last:
             v(ts(cb("u16l", t + 3, h), E[:, 256:384], 2048.0, OP.add), n, r=[E2], w=["u16l%d%d" % (t + 3, h)], b=[bE])
-        less = lambda o_, a, b_: [MM(o_, a, T.i16[:], True, False), MM(o_, b_, T.n16[:], False, True)] if last else \
-            [MM(o_, T.i16[:], a, True, False), MM(o_, T.n16[:], b_, False, True)]
+        term = lambda o_, a, m, st, sp: MM(o_, a, m, st, sp) if last else MM(o_, m, a, st, sp)
         EL, bL, kL = E[:, 256:384], bE, E2
         bE = BANKS(t, h)[1]
         E, (E0, E1, E2, E3) = T[bE], [bE + str(i) for i in range(4)]
-        mm(less(E[:, 0:128], lhn, lh), 2 * 128, r=["i16", "n16", lk, ln], w=[E0], b=[bE])
-        mm(less(E[:, 384:512], lh, qh), 2 * 128, r=["i16", "n16", lk, qhk], w=[E3], b=[bE])
-        v(ts(ft("ne"), E[:, 0:128], 0.0, OP.not_equal), n, r=[E0], w=[k_("ne")], b=[bE])
-        v(tt(E[:, 128:256], ft("ne"), E[:, 384:512], OP.mult), n, r=[k_("ne"), E3], w=[E1], b=[bE])
+        eq, o_ = cb("eq", 0, h), E[:, 128:256]
+        if last:
+            mm([term(o_, lhn, T.i16[:], True, False), term(o_, lh, T.n16[:], False, True)], 2 * 128, r=["i16", "n16", lk, ln], w=[E1], b=[bE])
+            v(ts(eq, o_, 0.0, OP.is_equal), n, r=[E1], w=[k_("eq")], b=[bE])
+        else:
+            v(tt(eq, lhn, lh, OP.is_equal), n, r=[lk, ln], w=[k_("eq")])
+        o_ = E[:, 384:512]
+        if t:
+            mm([term(o_, ft("xq"), T.i32[:], True, False), term(o_, lh, T.i16[:], False, False), term(o_, cb("lh", t - 1, h), T.n16[:], False, True)],
+               6 * 128, r=["i32", "i16", "n16", lk, "lh%d%d" % (t - 1, h), k_("xq")], w=[E3], b=[bE])
+        else:
+            hs = slice(128 * h, 128 * h + 128)
+            mm([MM(o_, T.f_ll[:, hs], T.i16[:], True, False), MM(o_, T.f_ql[:, hs], T.n16[:], False, True)], 2 * 128,
+               r=["i16", "n16", "f_ll", "f_ql"], w=[E3], b=[bE])
+        v(tt(ft("xq"), eq, E[:, 384:512], OP.mult), n, r=[k_("eq"), E3], w=[k_("xq")], b=[bE])
         if t >= 2:
             o_ = cb("outs", t - 2, h)
             nm = ("yp", "ys", "yl")[t - 2]
@@ -626,127 +692,255 @@ def _plan(g, core, T, topo):
             op("Y", 0.1, [lambda: g.sync.dma_start(T[nm][:, 128 * h:128 * h + 128], o_)], r=["outs%d%d" % (t - 2, h)], sig=("d_%s%d" % (nm, h), 16), lat=2.0)
         if last:
             oq = cb("outs", 3, h)
-            v(tt(oq, cb("qst", 0, h), E[:, 128:256], OP.add), n, r=["qst0%d" % h, E1], w=["outs3%d" % h], b=[bE])
+            v(tt(oq, D[:, 0:128], ft("xq"), OP.subtract), n, r=["Du", k_("xq")], w=["outs3%d" % h], b=["bD"])
             op("Y", 0.1, [lambda: g.sync.dma_start(T.yq[:, 128 * h:128 * h + 128], oq)], r=["outs3%d" % h], sig=("d_yq%d" % h, 16), lat=2.0)
-        else:
-            v(tt(cb("qh", t + 1, h), qh, E[:, 128:256], OP.add), n, r=[qhk, E1], w=["qh%d%d" % (t + 1, h)], b=[bE])
 
     for h in range(H2):
         first_page_form(h)
     for t in range(V):
         if t < 4:
             tabs(t)
-        for h in range(H2):
-            now[:] = [t, h]
-            big(t, h)
-            logic(t, h)
+        for f in (big, logic):
+            for h in range(H2):
+                now[:] = [t, h]
+                f(t, h)
     return ops
 
 
-def _order(ops):
-    n = len(ops)
-    pred = [sorted(o["d"]) for o in ops]
-    succ = [[] for _ in range(n)]
-    for i in range(n):
+def _choose(ops):
+    n, Q = len(ops), "TVSGYR"
+    q, dma = [o["q"] for o in ops], [o.get("dma", 0.0) for o in ops]
+    names = sorted({b for o in ops for b in o["b"]})
+    bank = [[3 * names.index(b) for b in o["b"]] for o in ops]
+    other = ((1, 2), (0, 2), (0, 1))
+    can = [[Q.index(e) for e in o.get("e", o["q"])] for o in ops]
+    anc, pred, succ = [], [], [[] for _ in ops]
+    for i, o in enumerate(ops):
+        far = 0
+        for d in o["d"]:
+            far |= anc[d]
+        pred.append(sorted(d for d in o["d"] if not far >> d & 1))
+        anc.append(far | sum(1 << d for d in pred[i]))
         for d in pred[i]:
             succ[d].append(i)
-    q, c, lat = [o["q"] for o in ops], [o["c"] for o in ops], [o["lat"] for o in ops]
-    dma, bank = [o.get("dma", 0.0) for o in ops], [o["b"] for o in ops]
-    rdma = [dma[i - 1] if q[i] == "R" else 0.0 for i in range(n)]
+    waits = [[d for d in pred[i] if not q[i] == q[d] == "T"] for i in range(n)]
 
-    def list_pass(before, after, prio, forward, theta, bias):
-        left = [len(b) for b in before]
-        ready_t = [0.0 if forward or after[i] else lat[i] for i in range(n)]
-        start, free, ready, seq, took, held = [0.0] * n, {}, {}, [], list(q), {}
-        for i in range(n):
-            if not left[i]:
-                ready.setdefault(q[i], []).append(i)
-        while len(seq) < n:
-            can = []
-            for qq, lst in ready.items():
-                for i in lst:
-                    e = qq
-                    if qq == "X":
-                        e = "V" if free.get("V", 0.0) + bias < free.get("S", 0.0) and ready_t[i] < free.get("S", 0.0) else "S"
-                    s = max(free.get(e, 0.0), ready_t[i])
-                    for b in bank[i]:
-                        s = max([s] + [f + WAKE for ee, f in held.get(b, {}).items() if ee != e])
-                    can.append((s, i, e))
-            end, e = min((s + theta * c[i], e) for s, i, e in can)
-            can = sorted((-prio[i], i, s) for s, i, ee in can if ee == e)
-            for k, (_, i, st) in enumerate(can):
-                if st <= end and all(st + theta * c[i] <= s for _, _, s in can[:k]):
-                    break
+    def costs(slow, gath, far):
+        f = [1.0 if e not in "TVSX" else slow * gath if o["n"][1:2] == "g" else slow for e, o in zip(q, ops)]
+        return ([o["c"] * x for o, x in zip(ops, f)], [o["lat"] * (far if e == "R" else 1.0) + WAKE * far ** 3 for e, o in zip(q, ops)],
+                [x * far for x in dma], START * far)
+
+    def first(gaps, x):
+        lo, hi = 0, len(gaps)
+        while lo < hi:
+            m = (lo + hi) // 2
+            if gaps[m][1] < x:
+                lo = m + 1
             else:
-                free[e] = min(s for _, _, s in can if s > end)
-                continue
-            took[i] = e
-            ready[q[i]].remove(i)
-            seq.append(i)
-            start[i] = st
-            fin = st + c[i]
-            if q[i] != "R":
-                free[took[i]] = fin
-            for b in bank[i]:
-                held.setdefault(b, {})[e] = fin
-            if dma[i] and forward:
-                free["D"] = max(fin + START, free.get("D", 0.0)) + dma[i]
-                fin = free["D"] - START - dma[i]
-            if rdma[i] and not forward:
-                free["D"] = max(fin - START - rdma[i], free.get("D", 0.0)) + rdma[i]
-                fin = free["D"] + START
-            for k in after[i]:
-                ready_t[k] = max(ready_t[k], fin + lat[i if forward else k] + WAKE)
-                left[k] -= 1
-                if not left[k]:
-                    ready.setdefault(q[k], []).append(k)
-        return start, seq, took
+                hi = m
+        return lo
 
-    def replay(seq, took, slow, gath, far):
-        fin, free, held = [0.0] * n, {}, {}
-        for i in seq:
-            e = took[i]
-            s = max([free.get(e, 0.0)] + [fin[d] + WAKE for d in pred[i]] +
-                    [f + WAKE for b in bank[i] for ee, f in held.get(b, {}).items() if ee != e])
-            f = s + c0[i] * (slow * (gath if ops[i]["n"][1:2] == "g" else 1.0) if e in "TVS" else 1.0)
-            if e != "R":
+    def fit(gaps, r, d):
+        k = first(gaps, r + d)
+        while True:
+            a, b = gaps[k]
+            if a < r:
+                a = r
+            if a + d <= b + 1e-9:
+                return a
+            k += 1
+
+    def cut(gaps, x, y):
+        k = lo = first(gaps, x + 1e-9)
+        new, (a, b) = [], gaps[k]
+        while a < y:
+            if x - a > 0.04:
+                new.append((a, x))
+            k += 1
+            if b - y > 0.04:
+                new.append((y, b))
+                break
+            a, b = gaps[k]
+        gaps[lo:k] = new
+
+    def place(key, forward, tab, bias):
+        c, la, dm, st = tab
+        gaps, free = [[(0.0, 1e9)] for _ in range(7)], [[(0.0, 1e9)] for _ in range(3 * len(names))]
+        start, eng = [0.0] * n, [0] * n
+        ready = [0.0 if forward or succ[i] else la[i] for i in range(n)]
+        for i in sorted(range(n), key=lambda i: key[i]):
+            r, d, best = ready[i], c[i], None
+            if dm[i] and not forward:
+                s = fit(gaps[6], max(r - st - dm[i], 0.0), dm[i])
+                cut(gaps[6], s, s + dm[i])
+                r = max(r, s + dm[i] + st)
+            for e in can[i]:
+                s, s2 = -1.0, r
+                while s2 > s:
+                    s = s2 = fit(gaps[e], s2, d)
+                    for b in bank[i]:
+                        s2 = fit(free[b + e], s2, d)
+                if best is None or s + bias < best[0]:
+                    best = (s, e)
+            s, e = start[i], eng[i] = best
+            if d:
+                cut(gaps[e], s, s + d)
+            for b in bank[i]:
+                for x in other[e]:
+                    cut(free[b + x], s - WAKE, s + d + WAKE)
+            f = s + d
+            if dm[i] and forward:
+                s = fit(gaps[6], f + st, dm[i])
+                cut(gaps[6], s, s + dm[i])
+                f = s - st
+            for k in succ[i] if forward else pred[i]:
+                x = f + (1e-6 if q[i] == q[k] == "T" else la[i if forward else k])
+                if x > ready[k]:
+                    ready[k] = x
+        return start, eng
+
+    def run(seq, eng, tab, p0, state, fin, marks=None, why=None):
+        c, la, dm, st = tab
+        free, held, dfree = state[0][:], state[1][:], state[2]
+        last, lastd = [-1] * (6 + len(held)), -1
+        for p, i in enumerate(seq[p0:], p0):
+            e, bs = eng[i], bank[i]
+            s = free[e]
+            for d in waits[i]:
+                if fin[d] > s:
+                    s = fin[d]
+            if bs:
+                x, y = other[e]
+                for b in bs:
+                    if held[b + x] > s:
+                        s = held[b + x]
+                    if held[b + y] > s:
+                        s = held[b + y]
+            if marks:
+                if p % STEP == 0:
+                    marks[p // STEP] = (free[:], held[:], dfree)
+                w = (last[e], 1) if s == free[e] else ([(d, 0) for d in waits[i] if fin[d] == s] +
+                                                       [(last[6 + b + x], 1) for b in bs for x in other[e] if held[b + x] == s])[0]
+                why[i] = (w, lastd if dm[i] and dfree > s + c[i] + st else -1, s)
+                last[e] = i
+                for b in bs:
+                    last[6 + b + e] = i
+                if dm[i]:
+                    lastd = i
+            f = s + c[i]
+            if e != 5:
                 free[e] = f
-            for b in bank[i]:
-                held.setdefault(b, {})[e] = f
-            if dma[i]:
-                free["D"] = max(f + START * far, free.get("D", 0.0)) + dma[i] * far
-                f = free["D"] - (START + dma[i]) * far
-            fin[i] = f + lat[i] * (far if e == "R" else 1.0)
-        return max(fin)
+            for b in bs:
+                held[b + e] = f + WAKE
+            if dm[i]:
+                dfree = max(f + st, dfree) + dm[i]
+                f = dfree - st - dm[i]
+            fin[i] = f + la[i]
+        return max(fin) - WAKE
 
-    c0, base = list(c), [0.0] * n
-    for i in reversed(range(n)):
-        base[i] = max([base[k] for k in succ[i]] + [0.0]) + c[i] + lat[i] + WAKE
+    zero, tabs = ([0.0] * 6, [0.0] * (3 * len(names)), 0.0), [costs(*m[:3]) for m in SETTINGS]
+    worth = lambda j, span: 100.0 / (POWER * len(tabs)) * (span / SETTINGS[j][3]) ** POWER
     rs = np.random.RandomState(SEED)
-    best = _CHOSEN.get(n)
-    for trial in range(0 if best else TRIES):
-        prio = [float(p + SPREAD * x) for p, x in zip(base, rs.random_sample(n))]
-        theta, bias, slow = [float(a + (b - a) * rs.random_sample()) for a, b in (THETA, BIAS, SLOW)]
-        c[:] = [x * slow if e in "TVSX" else x for x, e in zip(c0, q)]
-        for turn in range(TURNS):
-            start, seq, took = list_pass(pred, succ, prio, True, theta, bias)
-            span = sum(replay(seq, took, *m[:3]) / m[3] for m in SETTINGS) if turn else 1e9
-            if best is None or span < best[0] - 1e-9:
-                best = (span, start, seq, took)
-            back = list_pass(succ, pred, [start[i] + c[i] for i in range(n)], False, theta, bias)[0]
-            prio = [back[i] + c[i] for i in range(n)]
-    _CHOSEN[n] = best
+    tab, key = tabs[0], [0.0] * n
+    for i in reversed(range(n)):
+        key[i] = min([key[k] for k in succ[i]] + [0.0]) - tab[0][i] - tab[1][i]
+    best = cur = None
+    for turn in range(TRIES):
+        slow, bias, size, at = rs.random_sample(4).tolist()
+        tab, bias = costs(1.0 + SLOW * slow, GF, FAR), BIAS * bias
+        if cur:
+            at, key = 110 * at - 15, []
+            for i, x in enumerate(rs.random_sample(n).tolist()):
+                key.append(max([cur[1][i] + (size * size * x if at <= cur[1][i] <= at + 25 else 0.0)] + [key[d] + 1e-6 for d in pred[i]]))
+        start, eng = place(key, True, tab, bias)
+        for _ in range(2 if cur else 6):
+            back = place([-s - c for s, c in zip(start, tab[0])], False, tab, bias)[0]
+            start, eng = place([-s - c for s, c in zip(back, tab[0])], True, tab, bias)
+            seq = sorted(range(n), key=lambda i: start[i])
+            val = sum(worth(j, run(seq, eng, t, 0, zero, [0.0] * n)) for j, t in enumerate(tabs))
+            if cur is None or val < cur[0] + HEAT[0] * slow:
+                cur = (val, start, seq, eng)
+            if best is None or val < best[0]:
+                best = cur
+
+    def full(seq):
+        out = []
+        for t in tabs:
+            fin, marks, why = [0.0] * n, [None] * (n // STEP + 1), [None] * n
+            span, pairs = run(seq, eng, t, 0, zero, fin, marks, why), []
+            i, byq = fin.index(max(fin)), False
+            while i >= 0:
+                (d, kind), dd, _ = why[i]
+                if dd >= 0 and not byq:
+                    d, kind = dd, 2
+                if kind and d >= 0:
+                    pairs.append((d, i))
+                i, byq = d, kind == 1
+            out.append((span, fin, marks, why, pairs))
+        pos = [0] * n
+        for k, i in enumerate(seq):
+            pos[i] = k
+        return out, sum(worth(j, r[0]) for j, r in enumerate(out)), pos
+
+    seq, eng = best[2], best[3][:]
+    res, val, pos = full(seq)
+    best, taken = (val, seq, eng[:], res[0][3]), 0
+    for turn in range(MOVES):
+        a, b, kind, far, heat = rs.random_sample(5).tolist()
+        pairs = res[int(a * len(res))][4]
+        u, v = pairs[int(b * len(pairs))]
+        far, new, flip = int(-12 * math.log(1 - far)), seq, None
+        if kind < 0.2:
+            flip = u if kind < 0.1 else v
+            if q[flip] != "X":
+                continue
+            eng[flip], p0 = 3 - eng[flip], pos[flip]
+        elif kind < 0.6:
+            p0 = max([pos[d] + 1 for d in pred[v]] + [0, pos[u] - far])
+            if p0 > pos[u]:
+                continue
+            new = seq[:p0] + [v] + seq[p0:pos[v]] + seq[pos[v] + 1:]
+        else:
+            p0, k = pos[u], min([pos[d] - 1 for d in succ[u]] + [n - 1, pos[v] + far])
+            if k < pos[v]:
+                continue
+            new = seq[:p0] + seq[p0 + 1:k + 1] + [u] + seq[k + 1:]
+        k = p0 // STEP
+        x, room = 0.0, -HEAT[1] * (HEAT[2] / HEAT[1]) ** (turn / MOVES) * math.log(1 - heat)
+        for j in range(len(res)):
+            j = (j + int(a * len(res))) % len(res)
+            x += worth(j, run(new, eng, tabs[j], k * STEP, res[j][2][k], res[j][1][:])) - worth(j, res[j][0])
+            if x > room + 0.1:
+                break
+        if x <= room:
+            seq, taken = new, taken + 1
+            res, val, pos = full(seq)
+            if taken % 20 == 0:
+                seq = sorted(seq, key=lambda i: res[0][3][i][2])
+                res, val, pos = full(seq)
+            if val < best[0]:
+                best = (val, seq, eng[:], res[0][3])
+        elif flip is not None:
+            eng[flip] = 3 - eng[flip]
+    return best[1], [Q[e] for e in best[2]], [w[2] for w in best[3]]
+
+
+def _order(ops):
+    if len(ops) not in _CHOSEN:
+        _CHOSEN[len(ops)] = _choose(ops)
+    seq, took, start = _CHOSEN[len(ops)]
     order, held = {}, {}
-    for i in best[2]:
-        ops[i]["st"], ops[i]["q"] = best[1][i], best[3][i]
-        for b in bank[i]:
+    for i in seq:
+        o = ops[i]
+        if o["q"] == "X":
+            o["f"] = o["alt"][took[i]]
+        o["st"], o["q"] = start[i], took[i]
+        for b in o["b"]:
             for e, k in held.setdefault(b, {}).items():
-                if e != ops[i]["q"]:
-                    ops[i]["d"][k] = 1
-            held[b][ops[i]["q"]] = i
-        if q[i] == "X":
-            ops[i]["f"] = ops[i]["alt"][best[3][i]]
-        order.setdefault(ops[i]["q"], []).append(ops[i])
+                if e != o["q"]:
+                    o["d"][k] = 1
+            held[b][o["q"]] = i
+        order.setdefault(o["q"], []).append(o)
     order["Y"].sort(key=lambda o: (o["st"], o["i"]))
     return order
 

import math
import numpy as np
from concourse.bass import DstId, RemoteDMATransfer
from concourse.mybir import AluOpType as OP, ActivationFunctionType as AF, AxisListType as AX

V, H2 = 5, 2
PCS = 2
PE_NS, CY_NS, GATH = 0.4167, 0.83, 1.56
LAT, WAKE = 4.5, 0.14
SEED, TRIES, MOVES = 7, 700, 20000
SC = 2.0 ** 25
CL, CF, CP = -2.0 ** 24, 8192.0, 2.0 ** 21
GATE = 2.0 ** 25
MID = 2.0 ** 18 - 128 + 31.0 / 64
START, DFOLD, DSMALL, BACK = 1.9, 2.8, 0.4, 2.8
LTAB, FIRST = (0.0, 14.0, 25.0, 31.0), 2.0
XW = 4096 + 16
EDGE = {"a": ("pg", "sg"), "b": ("sg", "lg"), "c": ("pg", "lg"), "d": ("qg", "sg")}
TESTS = {"a": (-1, 0, 0, 0), "b": (-2, SC, SC, 0), "c": (2, -SC, 0, 0), "d": (0, 0, -SC, 0), "o": (0, 0, 0, SC)}
_CHOSEN = {}
MOG = False
FAR, GF, POWER = 1.0, 1.0, 25
SETTINGS = ((1.15, 0.83, 0.9, 98.0), (1.05, 1.0, 1.0, 98.5), (1.3, 1.2, 1.0, 128.5), (1.05, 0.9, 1.2, 109.0))
SLOW, BIAS = 0.15, 2.0
HEAT, STEP = (0.07, 0.05, 0.01), 40


def FOLD(t, h):
    return "" if LESS(t, h) else {(4, 1): ""}.get((t, h), "ab")


def MAX(t, h):
    return {(4, 0): "c", (4, 1): "bc"}.get((t, h), "")


def LESS(t, h):
    return False


def SRELU(t, h):
    return ""


def JOINM(t):
    return False


def JOINE(t):
    return False


def ENG(n, t, h):
    if n[1] == "g":
        return "V" if n[-1] == "0" and n[0] in {(0, 0): "sp", (0, 1): "p"}.get((t, h), "l" if t == 4 or (t, h) == (2, 1) else "lp") else "S"
    return "S" if t >= 0 else "SV"


def QUARTERS(e, t, h):
    return 4


def EFIRST(t, h):
    return 0


def BOTH(t, h):
    return t > 0


def CALLS(e, t, h):
    return 1


def PIECES(nm, t, h):
    return 2


def BANKS(t, h):
    return ("d0", "d0", "d0") if (t, h) == (4, 1) else ("bE", "bE", "d1" if h == 0 else "d0")


def FUSED(t, h):
    return t == 0 and "d" not in FOLD(t, h)


def OMAX(t, h):
    return {(4, 0): 0}.get((t, h), 4)


def _weights(t, h):
    w = {}

    def add(nm, e, c):
        w[nm] = tuple(a + c * b for a, b in zip(w.get(nm, (0, 0, 0, 0)), TESTS[e]))

    for e, (x, y) in EDGE.items():
        if e == "d" and t:
            continue
        if e in FOLD(t, h) + MAX(t, h):
            add("m" + e, e, 2), add(x, e, -1), add(y, e, -1)
        elif e == "d" and FUSED(t, h) or e in "bc" and LESS(t, h):
            add("m" + e, e, 2), add(x, e, -1)
        else:
            add("m" + e, e, 2), add(x, e, -1), add(y, e, 1)
    add("ao", "o", 2), add("sg" if t and not LESS(t, h) else "lg", "o", -1)
    out = {}
    for nm, c in w.items():
        nz = [i for i in range(4) if c[i]]
        if nz:
            out[nm] = (nz[0], c[nz[0]:nz[-1] + 1])
    return out


def _row(i, run):
    return [(r, j) for r, c in enumerate(ROWS) for j in range(5 - len(run) if i or len(run) == 1 else 1) if c[j:j + len(run)] == run][:1]


RUNS = []
for _t in range(V):
    for _h in range(H2):
        RUNS += list(_weights(_t, _h).values())
ROWS = []
for _i, _c in sorted(set(RUNS), key=lambda c: (-len(c[1]), c)):
    if not _row(_i, _c):
        ROWS.append((0,) * _i + _c + (0,) * (4 - _i - len(_c)))
NR = len(ROWS)
LONG = ("sg", "lg", "pg", "qg", "ma", "mb", "mc", "md", "ao", "mx")
TURN = {"sg": 2, "pg": 3}

SCRATCH, SEMAPHORES = {}, ["sT", "sV", "sS", "sG", "lsem"]


def _buf(name, cols, dtype, where="sbuf"):
    SCRATCH[name] = (where, [128, cols], dtype)


def _bn(nm, t, h):
    return nm + str(h) + "o" * (t % TURN.get(nm, 1))


for _n in ("d0", "d1", "bY", "bD", "bE"):
    _buf(_n, 512, "float32", "psum")
for _n in ("bA0", "bA1", "bA2"):
    SCRATCH[_n] = ("psum", [128, 8, 16, 4], "float32")
SCRATCH["fun"] = ("sbuf", [128, 8, 3 * NR, 4], "bfloat16")
SCRATCH["rowlo"] = ("sbuf", [128, 8, 16, 4], "bfloat16")
for _t in range(4):
    _buf("x%d" % _t, XW, "bfloat16")
    _buf("thm%d" % _t, 256, "bfloat16")
    _buf("wb%d" % _t, 128, "bfloat16")
LANDS = sorted({_bn(_n, _t, _h) for _n in LONG for _t in range(V) for _h in range(2)})
for _n in LANDS:
    _buf(_n, 2048, "bfloat16")
for _h in range(2):
    for _n in ("fl", "fz", "absd"):
        _buf(_n + str(_h), 128, "bfloat16")
ITMP, FTMP = ("r1", "t2"), ("z", "y", "m3", "r3", "m1", "xq")
_buf("eq", 256, "float16")
_buf("itmp", len(ITMP) * 256, "int32")
_buf("ftmp", len(FTMP) * 256, "float32")
_buf("mo", V * 256, "bfloat16")
_buf("mi", V * 256, "bfloat16")
_buf("u16l", 7 * 256, "uint16")
_buf("u16q", 256, "uint16")
_buf("lst", 5 * 256, "float32")
_buf("lh", 6 * 256, "float16")
_buf("raw", 6 * 256, "int32")
_buf("qst", 256, "float32")
_buf("outs", 4 * 256, "float32")
for _t in range(V):
    _buf("e%d" % _t, 272, "bfloat16")
    _buf("eo%d" % _t, 272, "bfloat16")
    for _h in range(2):
        SEMAPHORES.append("rm%d%d" % (_t, _h))
        SEMAPHORES += ["f%s%d%d%d" % (_e, _t, _h, _w) for _e in FOLD(_t, _h) for _w in range(CALLS(_e, _t, _h))]
        if _t:
            SEMAPHORES.append("re%d%d" % (_t, _h))
SEMAPHORES += ["rx1", "rx2", "rx3"] + ["px%d%d" % (_r, _w) for _r in range(4) for _w in range(2)]
for _n in ("pl", "sl", "ll", "ql"):
    _buf("i_" + _n, 256, "int32")
    _buf("f_" + _n, 256, "float16")
_buf("i_tw", 2, "int32")
_buf("i_th", 2, "int32")
_buf("ka", 128, "float16")
_buf("k37", 128, "float32")
_buf("acol", 1, "int32")
_buf("cnt", 2 + V, "float32")
_buf("onec", 128, "bfloat16")
_buf("one32", 128, "float32")
_buf("i32", 128, "float32")
_buf("i16", 128, "float16")
_buf("n16", 128, "float16")
for _n in ("one", "ib", "nib", "i1024", "im512", "i4096", "bt", "b128", "nbsc", "uj0", "uj1"):
    _buf(_n, 128, "bfloat16")
_buf("msk", 2048 // PCS, "bfloat16")
_buf("rowb", 384, "bfloat16")
LOADS = ["sl", "xt0", "xt1", "pl", "th", "wt", "ll", "ql", "ed0", "ed1"]
STORES = ["%s%d" % (_n, _h) for _n in ("yp", "ys", "yl", "yq", "ye") for _h in range(2)]
SEMAPHORES += ["d_" + _n for _n in LOADS + STORES]


def _helpers(T, topo):
    port, hands = {}, {}
    for c in T.cores:
        free = [k for k in topo.cores_of(c) if T.rank_of(k) is None and topo.die(k) == topo.die(c)]
        p = [k for k in free if all(topo.may_write(k, o) for o in T.cores)][0]
        port.setdefault(topo.chip(c), {})[topo.die(c)] = p
        hands[c] = [k for k in free if k != p]
    return port, hands


def _piece(ap, i):
    return ap[:, i * XW // 4:(i + 1) * XW // 4]


def _write(g, T, topo, items):
    trs = []
    for srcs, (c, d), en, sem in items:
        rid, pid, _ = topo.addr(c)
        trs.append(RemoteDMATransfer(dst_ids=[DstId(rid=rid, pnc=pid)], dma_engine_mask=sum(1 << e for e in en), remote_sem=T.sem[sem],
                                     srcs=srcs, dsts=[d], alu_op=2 if len(srcs) > 1 else 0))
    return g.remote_dma_fused(trs, local_sem=T.sem["lsem"])


def _port_program(g, core, T, topo, die):
    port, _ = _helpers(T, topo)
    N, chip = len(T.cores), topo.chip(core)
    here = [r for r in range(N) if topo.chip(T.cores[r]) == chip]
    far = [r for r in range(N) if r not in here]
    off = topo.engines(core, T.cores[far[0]])
    on = [e for e in topo.engines(core, T.cores[here[0]]) if e not in off]
    i = sorted(port[chip]).index(die)
    jobs = [sorted(((r - h) % N, r, h, en) for r in here for h in homes if h != r) for homes, en in ((far, off), (here, on))]
    item = lambda t, r, h, en, p: ([_piece(T["x%d" % r], p)], (T.cores[h], _piece(T["x%d" % t], p)), en, "rx%d" % t)
    for w in range(2):
        for r in here:
            g.wait_ge(T.sem["px%d%d" % (r, w)], 8)
        _write(g, T, topo, [item(*j[0], 2 * w + i) for j in jobs])
    for k in range(1, max(len(j) for j in jobs)):
        _write(g, T, topo, [item(t, r, h, en[4 * w:4 * w + 4], 2 * w + i) for t, r, h, en in [j[k] for j in jobs if k < len(j)] for w in range(2)])
    g.wait_ge(T.sem["lsem"], sum(len(j[3]) for js in jobs for j in js + js[:1]))


def _hand_program(g, core, T, topo, owner, calls):
    sent = 0
    en = topo.engines(core, owner)
    for c, land, sem, cnt, back, _ in calls:
        if c == core:
            g.wait_ge(T.sem[sem], cnt)
            _write(g, T, topo, [([land], (owner, back), en, sem)])
            sent += len(en)
    g.wait_ge(T.sem["lsem"], sent)


def _plan(g, core, T, topo):
    rank, N = T.rank_of(core), len(T.cores)
    ops, last_w, readers, accs, banks, half = [], {}, {}, {}, {}, ["0"]
    now = [-1, 0]

    def op(q, cost, fns, r=(), w=(), a=(), b=(), sig=None, lat=0.0, after=()):
        o = {"q": q, "c": cost, "f": fns, "d": {}, "sig": sig, "lat": lat, "i": len(ops), "n": (list(w) + list(a) + list(r) + ["?"])[0]}
        for x in after:
            o["d"][x["i"]] = 1
        r, w, a, b = [[k + half[0] if k in ("A", "AL", "AG", "bA") else k for k in ks] for ks in (r, w, a, b)]
        for k in r:
            for x in [last_w.get(k)] + accs.get(k, []):
                if x is not None:
                    o["d"][x["i"]] = 1
        for k in a:
            if last_w.get(k) is not None:
                o["d"][last_w[k]["i"]] = 1
            for x in readers.get(k, []):
                o["d"][x["i"]] = 1
        for k in w:
            for x in [last_w.get(k)] + accs.get(k, []) + readers.get(k, []):
                if x is not None:
                    o["d"][x["i"]] = 1
        for k in r:
            readers.setdefault(k, []).append(o)
        for k in a:
            accs.setdefault(k, []).append(o)
        for k in w:
            last_w[k], accs[k], readers[k] = o, [], []
        o["b"] = b
        o["d"].pop(o["i"], None)
        ops.append(o)
        return o

    def vec(n, cyc=1.0):
        return max(64.0, n * cyc) * CY_NS / 1000

    def mm(fns, cyc, **kw):
        return op("T", cyc * PE_NS / 1000, fns, **kw)

    def MM(out, lhsT, rhs, start, stop):
        return lambda: g.tensor.matmul(out, lhsT, rhs, start, stop)

    def v(fn, n, cyc=1.0, **kw):
        return op("V", vec(n, cyc), [fn], **kw)

    def s(fn, n, **kw):
        return op("S", vec(n), [fn], **kw)

    def vs(fv, fs, n, **kw):
        o = op("X", vec(n), None, **kw)
        o["alt"] = {"V": [fv], "S": [fs]}
        o["e"] = ENG(o["n"], *now)
        return o

    def scaled(out, x, c, n, **kw):
        return vs(ts(out, x, float(c), OP.mult), act(out, x, AF.Copy, 0.0, float(c)), n, **kw)

    def shifted(out, a, c, n, **kw):
        return vs(ts(out, a, float(c), OP.add), act(out, a, AF.Copy, float(c)), n, **kw)

    def relu(out, a, n, **kw):
        return vs(ts(out, a, 0.0, OP.max), act(out, a, AF.Relu), n, **kw)

    def tt(out, a, b, o):
        return lambda: g.vector.tensor_tensor(out, a, b, o)

    def ts(out, a, s1, o1, s2=None, o2=None):
        if o2 is None:
            return lambda: g.vector.tensor_scalar(out, a, s1, None, o1)
        return lambda: g.vector.tensor_scalar(out, a, s1, s2, o1, o2)

    def cp(out, a):
        return lambda: g.vector.tensor_copy(out, a)

    def act(out, a, f, bias=0.0, scale=1.0):
        return lambda: g.scalar.activation(out, a, f, bias=bias, scale=scale)

    def load(name, out, in_, key):
        return op("Y", 0.0, [lambda: g.sync.dma_start(out, in_)], w=[key], sig=("d_" + name, 16),
                  lat={"sl": 2.2, "xt0": 3.1, "th": 3.2, "wt": 3.25, "xt1": 4.0}.get(name, 3.7 + 0.1 * len(ops)))

    def send(name, out, in_, dst, eng, key, lat, rkey, after=()):
        eng = [e for e in eng]
        m = sum(1 << e for e in eng)
        rid, pid, _ = topo.addr(dst)
        so = op("G", 1.3, [lambda: g.remote_dma(out, in_, T.sem[name], T.sem["lsem"], pid, rid, m)], r=key, sig=("send", len(eng)), after=after)
        so["dma"] = DSMALL
        op("R", 0.0, [], w=rkey, sig=(name, len(eng)), after=[so], lat=lat)
        return so

    def dst(k):
        return T.cores[(rank + k) % N]

    def cb(name, i, h, n=128):
        c = i * 256 + h * 128
        return T[name][:, c:c + n]

    load("sl", T.i_sl[:], T.sl[:], "i_sl")
    load("xt0", T.x0[:, 0:XW // 2], T.xt[:, 0:XW // 2], "x0")
    load("th", T.i_tw[:, 0:1], T.th[:], "i_th")
    load("wt", T.i_tw[:, 1:2], T.wt[:], "i_wt")
    load("xt1", T.x0[:, XW // 2:4096], T.xt[:, XW // 2:4096], "x0b")
    load("pl", T.i_pl[:], T.pl[:], "i_pl")
    load("ll", T.i_ll[:], T.ll[:], "i_ll")
    load("ql", T.i_ql[:], T.ql[:], "i_ql")
    load("ed0", T.e0[:, 0:128], T.ed[:, 0:128], "e00")
    load("ed1", T.e0[:, 128:256], T.ed[:, 128:256], "e01")
    ms = lambda ap, c: (lambda: g.vector.memset(ap, c))
    v(ms(T.one32[:], 1.0), 128, w=["one32"])
    v(ms(T.one[:], 1.0), 128, 0.5, w=["one"])
    v(ms(T.onec[:], 1.0 / GATE), 128, 0.5, w=["onec"])
    gq = lambda fn, n, **kw: op("G", 0.2 + n * 2 * CY_NS / 1000, [fn], **kw)
    gq(lambda: g.affine_select(T.i32[:], T.one32[:], [[-1, 128]], OP.is_equal, 0.0, 0, 1), 128, r=["one32"], w=["i32"])
    gq(lambda: g.affine_select(T.bt[:], T.one[:], [[-16, 8], [0, 16]], OP.is_ge, 0.0, 0, 1), 128, r=["one"], w=["bt"])
    gq(lambda: g.affine_select(T.b128[:], T.bt[:], [[16, 8], [0, 16]], OP.is_ge, 0.0, 15, -1), 128, r=["bt"], w=["b128"])
    gq(lambda: g.iota(T.k37[:], [[0, 8], [37, 16]], 0, 0, allow_small_or_imprecise_dtypes=True), 128, w=["k37"])
    for nm, c in (("ib", 1.0), ("nib", -1.0), ("i1024", 1024.0 / GATE), ("im512", -512.0 / GATE), ("i4096", -4096.0), ("i16", 1.0), ("n16", -1.0)):
        if nm in ("i16", "n16"):
            v(ts(T[nm][:], T.i32[:], c, OP.mult), 128, r=["i32"], w=[nm])
        else:
            scaled(T[nm][:], T.i32[:], c, 128, r=["i32"], w=[nm])
    scaled(T.nbsc[:], T.b128[:], -SC, 128, r=["b128"], w=["nbsc"])
    v(ms(T.msk[:], 1.0), 2048 // PCS, 0.5, w=["msk"])
    v(ms(T.msk[:, 0::16], 0.0), 128 // PCS, 0.5, w=["msk"])
    v(ms(T.fun[:], 0.0), 96 * NR, 0.5, w=["fun"])
    for r, row in enumerate(ROWS):
        for i, c in enumerate(row):
            if c:
                scaled(T.fun[:, :, 2 * NR + r, i], T.b128[:, 0::16], c, 8, r=["b128"], a=["fun"])
    v(cp(T.fun[:, :, 0:NR, 0], T.fun[:, :, 2 * NR:, 0]), 8 * NR, 0.5, r=["fun"], w=["funx"])
    v(cp(T.fun[:, :, NR:2 * NR, 1:4], T.fun[:, :, 2 * NR:, 1:4]), 24 * NR, 0.5, r=["fun"], w=["funt"])
    for p, a, c in ((2, 0, CL), (2, 128, CL + 2.0 ** 18), (1, 0, 2048.0), (1, 128, 2048.0 + CF - 128), (1, 256, 129.0 * 4096)):
        v(ms(T.rowb[0:p, a:a + 128], c), 128, 0.5, w=["rowb%d" % a])
    for i, c in enumerate((0.0, -SC / 2, CL, SC / 2)):
        v(ms(T.rowlo[0:1, :, :, i], c), 128, 0.5, a=["rowlo"])
    for h in range(H2):
        v(ms(T["fz%d" % h][:], 0.0), 128, 0.5, w=["fz0%d" % h])
    CB_ = ["rowb0", "rowb128", "rowb256"]
    one_row = T.one[0:1, :]
    v(ts(T.i_th[:, 0:1], T.i_tw[:, 0:1], 4, OP.arith_shift_right), 1, r=["i_th"], w=["thh"])
    v(ts(T.i_th[:, 1:2], T.i_tw[:, 0:1], 15, OP.bitwise_and), 1, r=["i_th"], w=["thl"])
    v(ms(T.x0[:, 4096:4112], 0.0), 16, w=["xe0"])
    v(ts(T.x0[:, 4096:4097], T.i_th[:, 0:1], -SC * 16, OP.mult), 1, r=["thh"], w=["xe0"])
    v(ts(T.x0[:, 4097:4098], T.i_th[:, 1:2], -SC, OP.mult), 1, r=["thl"], w=["xe0"])
    v(cp(T.x0[:, 4098:4099], T.i_tw[:, 1:2]), 1, r=["i_wt"], w=["xe0"])
    first = {}
    port, hands = _helpers(T, topo)
    pc = [port[topo.chip(core)][d] for d in sorted(port[topo.chip(core)])]
    every = topo.engines(core, pc[0])
    so = None
    for w, keys in enumerate((["x0"], ["x0b", "xe0"])):
        items = [([_piece(T.x0, 2 * w + i)], (pc[i], _piece(T["x%d" % rank], 2 * w + i)), every[8 * i:8 * i + 8], "px%d%d" % (rank, w)) for i in range(2)]
        so = op("G", 1.3, [lambda items=items: _write(g, T, topo, items)], r=keys, sig=("send", 16), after=[so] if so else [])
        so["dma"] = DFOLD / 2
    for t in range(1, N):
        op("R", 0.0, [], w=["x%d" % t], sig=("rx%d" % t, 16 if t > 1 else 32), after=[so], lat=LTAB[t])
    landed, sentE = [0], {}

    def fold(t, h, edges):
        for e in edges:
            land = LANDS[landed[0]]
            landed[0] += 1
            nq = QUARTERS(e, t, h) // CALLS(e, t, h)
            for w in range(CALLS(e, t, h)):
                items, calls, sem = [], [], "f%s%d%d%d" % (e, t, h, w)
                for i, c in enumerate(hands[core]):
                    sl = slice(256 * nq * (2 * w + i), 256 * nq * (2 * w + i + 1))
                    items.append(([T[_bn(x, t, h)][:, sl] for x in EDGE[e]], (c, T[land][:, sl]), every[8 * i:8 * i + 8], sem))
                    calls.append((c, T[land][:, sl], sem, 8, T[_bn("m" + e, t, h)][:, sl], 256 * nq))
                rd = [_bn(x, t, h) + "p%d" % j for x in EDGE[e] for j in range(nq * w, nq * w + nq)]
                wr = [_bn("m" + e, t, h) + "p%d" % j for j in range(nq * w, nq * w + nq)]
                so = op("G", 1.3, [lambda items=items: _write(g, T, topo, items)], r=rd, w=wr, sig=("send", 16),
                        after=[sentE[h]] if e == "b" and t and EFIRST(t, h) else [])
                so["calls"], so["dma"] = calls, DFOLD * nq / 4
                op("R", 0.0, [], r=rd, w=wr, sig=(sem, 32), after=[so], lat=START + so["dma"] * 1.25 + BACK + (FIRST if t == 0 else 0.0))

    for nm, i in (("sl", 1), ("pl", 0), ("ll", 2)):
        v(cp(T.u16l[:, 256 * i:256 * i + 256], T["i_" + nm][:]), 256, r=["i_" + nm], w=["u16l%d0" % i, "u16l%d1" % i])
    v(cp(T.u16q[:, 0:256], T.i_ql[:]), 256, r=["i_ql"], w=["u16q00", "u16q01"])
    for nm, lst, i in (("ll", "u16l", 2), ("ql", "u16q", 0), ("pl", "u16l", 0), ("sl", "u16l", 1)):
        v(ts(T["f_" + nm][:], T[lst][:, 256 * i:256 * i + 256], 2048.0, OP.subtract), 256, 0.5, r=["%s%d0" % (lst, i)], w=["f_" + nm])

    def first_page_form(h):
        hs = slice(128 * h, 128 * h + 128)
        for c, nm in enumerate(("ll", "ql", "pl", "sl")):
            mm([MM(T.bE[:, 128 * c:128 * c + 128], T["f_" + nm][:, hs], T.i16[:], True, True)], 128, r=["f_" + nm, "i16"], w=["bE%d" % c], b=["bE"])
        v(cp(cb("lh", 0, h), T.bE[:, 0:128]), 128, r=["bE0"], w=["lh0%d" % h], b=["bE"])
        shifted(cb("qst", 0, h), T.bE[:, 128:256], 2048.0, 128, r=["bE1"], w=["qst0%d" % h], b=["bE"])
        v(ts(cb("raw", 0, h), T.bE[:, 0:128], 2048.0, OP.add), 128, r=["bE0"], w=["raw0%d" % h], b=["bE"])
        for i, c in ((0, 2), (1, 3)):
            shifted(cb("lst", i, h), T.bE[:, 128 * c:128 * c + 128], CP + 2048.0, 128, r=["bE%d" % c], w=["lst%d%d" % (i, h)], b=["bE"])

    P = 2048 // PCS
    dn = [0]

    def tabs(t):
        x = "x%d" % t
        e = ["xe0"] if t == 0 else [x]
        late = [first[(t - 1, 1)]] if t else []
        v(ts(T["thm%d" % t][:, 0:128], T.ib[:], T[x][:, 4096:4097], OP.mult), 128, 0.5, r=["ib"] + e, w=["thm%d" % t], after=late)
        v(ts(T["thm%d" % t][:, 128:256], T.ib[:], T[x][:, 4097:4098], OP.mult), 128, 0.5, r=["ib"] + e, w=["thn%d" % t], after=late)
        v(ts(T["wb%d" % t][:], T.b128[:], T[x][:, 4098:4099], OP.mult), 128, 0.5, r=["b128"] + e, w=["wb%d" % t], after=late)

    def big(t, h):
        hh = str(h)
        x = "x%d" % (t % 4)
        win = T[x][:, 0:4096]
        B = {n: T[_bn(n, t, h)] for n in LONG}
        xk = [x, "x0b"] if t % 4 == 0 else [x]
        fo = FOLD(t, h)

        def off(buf, i, j, n=PCS):
            c = i * 256 + h * 128 + j * (128 // n)
            return T[buf][:, c:c + 128 // n]

        K = lambda n, j: _bn(n, t, h) + "p%d" % j
        KP = lambda n, j, m=PCS: [K(n, jj) for jj in range(4 * j // m, 4 * (j + 1) // m)]

        q4 = lambda d: [d + str(i) for i in range(4)]

        def turn():
            dn[0] += 1
            return BANKS(t, h)[2] if BOTH(t, h) and dn[0] % 2 else "d%d" % h

        def gather(nm, lst, i):
            n = PIECES(nm, t, h)
            for j in range(n):
                sl = slice(2048 // n * j, 2048 // n * (j + 1))
                kw = dict(r=xk + ["%s%d%d" % (lst, i, h)], w=KP(nm, j, n))
                src = win.indirect(off(lst, i, j, n))
                o = vs(cp(B[nm][:, sl], src), act(B[nm][:, sl], src, AF.Copy), 2048 // n * GATH + 70, **kw)
            return o

        def size(e):
            for j in range(4):
                d, sl, gp = turn(), slice(512 * j, 512 * j + 512), j
                for nm, mat, st in zip(EDGE[e], ("ib", "nib"), (True, False)):
                    mm([MM(T[d][:], T[mat][:], B[nm][:, sl], st, not st)], 512, r=[K(nm, gp), mat], w=q4(d), b=[d])
                relu(B["m" + e][:, sl], T[d][:], 512, r=q4(d), w=[K("m" + e, j)], b=[d])

        def less(nm, lst, i, y, e):
            n = PIECES(nm, t, h)
            for j in range(n):
                sl = slice(2048 // n * j, 2048 // n * (j + 1))
                v(tt(B[nm][:, sl], win.indirect(off(lst, i, j, n)), B[y][:, sl], OP.subtract), 2048 // n * GATH + 70,
                  r=xk + ["%s%d%d" % (lst, i, h)] + KP(y, j, n), w=KP(nm, j, n))
                kw = dict(r=KP(nm, j, n), w=KP("m" + e, j, n))
                if e in SRELU(t, h):
                    s(act(B["m" + e][:, sl], B[nm][:, sl], AF.Relu), 2048 // n, **kw)
                else:
                    v(ts(B["m" + e][:, sl], B[nm][:, sl], 0.0, OP.max), 2048 // n, 0.5, **kw)

        if LESS(t, h):
            gather("lg", "u16l", t + 2)
            less("sg", "u16l", t + 1, "lg", "b")
            less("pg", "u16l", t, "lg", "c")
        else:
            gather("sg", "u16l", t + 1)
            first[(t, h)] = gather("pg", "u16l", t)
            gather("lg", "u16l", t + 2)
        if t == 0 and not FUSED(t, h):
            gather("qg", "u16q", t)
        for grp in ("a", "d", "bc"):
            ed = [e for e in grp if e in fo]
            fold(t, h, [e for e in ed if QUARTERS(e, t, h)])
        for j in range(PCS):
            sl = slice(P * j, P * j + P)
            v(lambda a=B["mx"][:, sl], b=B["lg"][:, sl]: g.vector.tensor_tensor_scan(a, T.msk[:], b, 0.0, OP.mult, OP.max), P, 0.5,
              r=["msk"] + KP("lg", j), w=[K("mx", j)])
        mo = "mo%d%d" % (t, h)
        if MOG:
            gq(lambda: g.affine_select(cb("mo", t, h), B["mx"][:, 15::16], [[0, 128]], OP.is_ge, 0.0, 0, 0), 128, r=[K("mx", j) for j in range(PCS)], w=[mo])
        else:
            v(cp(cb("mo", t, h), B["mx"][:, 15::16]), 128, 0.5, r=[K("mx", j) for j in range(PCS)], w=[mo])
        d2 = dst(2)
        if h or not JOINM(t):
            hs = range(0 if JOINM(t) else h, h + 1)
            send("rm%d%d" % (t, h), cb("mi", t, hs[0], 128 * len(hs)), cb("mo", t, hs[0], 128 * len(hs)), d2, topo.engines(core, d2)[:8],
                 ["mo%d%d" % (t, a) for a in hs], LAT, ["mi%d%d" % (t, a) for a in hs])
        if FUSED(t, h):
            less("qg", "u16q", t, "sg", "d")
        for e in "a" if LESS(t, h) else "abc" if t or FUSED(t, h) else "abcd":
            if e not in fo + MAX(t, h):
                size(e)
            for j in range(QUARTERS(e, t, h), 4) if e in fo else range(4) if e in MAX(t, h) else []:
                sl, (x_, y_) = slice(512 * j, 512 * j + 512), EDGE[e]
                v(tt(B["m" + e][:, sl], B[x_][:, sl], B[y_][:, sl], OP.max), 512, r=[K(x_, j), K(y_, j)], w=[K("m" + e, j)])
        e, ol, ed = "e%d%d" % (t, h), "sg" if t and not LESS(t, h) else "lg", cb("e%d" % t, 0, h)
        for k in range(4 * OMAX(t, h)):
            v(tt(B["ao"][:, 128 * k:128 * k + 128], B[ol][:, k::16], ed, OP.max), 128, r=KP(ol, 0, 1) + [e], a=[K("ao", k // 4)])
        for j in range(OMAX(t, h), 4):
            d = turn()
            fn = []
            for i in range(4):
                o_ = T[d][:, 128 * i:128 * i + 128]
                fn += [MM(o_, T.ib[:], B[ol][:, 4 * j + i::16], True, False), MM(o_, T.nib[:], ed, False, True)]
            mm(fn, 1024, r=KP(ol, 0, 1) + [e, "ib", "nib"], w=q4(d), b=[d])
            relu(B["ao"][:, 512 * j:512 * j + 512], T[d][:], 512, r=q4(d), w=[K("ao", j)], b=[d])

    def logic(t, h):
        hh, n = str(h), 128
        tm = t % 4
        B = {nm: T[_bn(nm, t, h)] for nm in LONG}
        half[0] = str((2 * t + h) % 3)
        A, D = T["bA" + half[0]], T.bD
        k_ = lambda nm: nm + hh
        pcs = lambda nm: [_bn(nm, t, h) + "p%d" % j for j in range(4)]
        fl = T["fl" + hh]
        it = lambda nm: cb("itmp", ITMP.index(nm), h)
        ft = lambda nm: cb("ftmp", FTMP.index(nm), h)
        e, eo, mi = "e%d%d" % (t, h), "eo%d%d" % (t, h), "mi%d%d" % (t, h)
        ed, edo = cb("e%d" % t, 0, h), cb("eo%d" % t, 0, h)
        XF, X1, X2, X3 = A[:, :, 0, 0], A[:, :, :, 1], A[:, :, :, 2], A[:, :, :, 3]
        mm([MM(A[:], one_row, T.rowlo[0:1], True, False)], 512, r=["one", "rowlo"], w=["A"], b=["bA"])
        for i, key in enumerate(("thm", "thn")[:2 if t else 1]):
            mm([MM(X3, T.one[:], T["thm%d" % tm][:, 128 * i:128 * i + 128], False, False)], 128, r=["one", key + str(tm)], a=["A"], b=["bA"])

        def sums(nm, i, run):
            (r, j), w, fn = _row(i, run)[0], len(run), []
            for k in range(16):
                lt = B[nm][:, 128 * k:128 * k + 128] if nm == "ao" else B[nm][:, k::16]
                if i == 0 and w > 1 and k:
                    fn.append(MM(A[:, :, 0:k + 1:k, 0:w], lt, T.fun[:, :, r:NR + r + 1:NR, 0:w], False, False))
                else:
                    fn.append(MM(A[:, :, k if i else 0, i:i + w], lt, T.fun[:, :, 2 * NR + r, j:j + w], False, False))
            mm(fn, 64 * len(fn), r=pcs(nm) + ["fun", "funx", "funt"], a=["A"], b=["bA"])

        for nm, (i, run) in _weights(t, h).items():
            sums(nm, i, run)
        r, j = _row(3, (2 * SC,))[0]
        mm([MM(X3, ed, T.nbsc[:], False, False)] +
           [MM(A[:, :, k, 3], ed, T.fun[:, :, 2 * NR + r, j], False, False) for k in range(4 * OMAX(t, h), 16)],
           128 + 256 * (4 - OMAX(t, h)), r=[e, "nbsc", "fun"], a=["A"], b=["bA"])
        if t:
            mm([MM(X2, one_row, T.rowb[0:1, 0:128], False, False), MM(X2, T.i16[:], cb("lh", t, h), False, True)], 256,
               r=["one", "i16", "lh%d%d" % (t, h)] + CB_, w=["A"], b=["bA"])
        else:
            mm([MM(X3, T.one[:], T.thm0[:, 128:256], False, True)], 128, r=["one", "thn0"], w=["A"], b=["bA"])
        U = cb("bY", 1, h)
        mm([MM(U, ed, T["wb%d" % tm][:], True, True)], 128, r=[e, "wb%d" % tm], w=[k_("U")], b=["bY"])
        uj, c4 = T["uj" + hh][:], 128.5 + 1.0 / 8192
        vs(ts(uj, U, 1.0 / 4096, OP.mult, c4, OP.add), act(uj, U, AF.Copy, c4, 1.0 / 4096), n, r=[k_("U")], w=[k_("uj")], b=["bY"])
        mm([MM(U, ed, T["wb%d" % tm][:], True, False), MM(U, one_row, T.rowb[0:1, 256:384], False, False),
            MM(U, T.i4096[:], uj, False, True)], 3 * 128, r=[e, "wb%d" % tm, "one", "i4096", k_("uj")] + CB_, w=[k_("U")], b=["bY"])
        if (t, h) == (0, 0):
            v(cp(T.ka[:], T.k37[:]), n, r=["k37"], w=["ka"])
        lh, raw = cb("lh", t, h), cb("raw", t, h)
        qo, qk = (cb("raw", t - 1, h), "raw%d%d" % (t - 1, h)) if t else (cb("qst", 0, h), "qst0%d" % h)
        bE = BANKS(t, h)[0]
        E, (E0, E1, E2, E3) = T[bE], [bE + str(i) for i in range(4)]
        PL, PY = E[:, 256:384], cb("bY", 0, h)
        if t + 2 < V:
            mm([MM(PL, T.one[0:2, :], T.rowb[0:2, 0:128], True, False), MM(PL, T.i16[:], lh, False, True)], 2 * 128,
               r=["one", "i16", "lh%d%d" % (t, h)] + CB_, w=[E2], b=[bE])
            shifted(cb("lst", t + 2, h), PL, CP - CL, n, r=[E2], w=["lst%d%d" % (t + 2, h)], b=[bE])
        fn = [MM(PY, T.one[0:2, :], T.rowb[0:2, 128:256], True, False), MM(PY, T.i16[:], lh, False, False), MM(PY, T.i16[:], T.ka[:], False, True)]
        mm(fn, 3 * 128, r=["one", "i16", "lh%d%d" % (t, h), "ka"] + CB_, w=[k_("PY")], b=["bY"])
        v(tt(ft("z"), raw, U, OP.mult), n, r=[k_("U"), "raw%d%d" % (t, h)], w=[k_("z")], b=["bY"])
        ac = T.cnt[:, 2 + t:3 + t]
        if h == 0 and t:
            shifted(ac, T["e%d" % t][:, 256:257], -MID, 1, r=["e%d1" % t], w=["am%d" % t])
        elif h == 0:
            v(ms(ac, -MID), 1, w=["am0"])
        vs(ts(ft("z"), ft("z"), 1.0 / 32, OP.mult, ac, OP.add), act(ft("z"), ft("z"), AF.Identity, ac, 1.0 / 32), n, r=["am%d" % t, k_("z")], w=[k_("z")])
        v(tt(ft("y"), ft("z"), PY, OP.add), n, r=[k_("z"), k_("PY")], w=[k_("y")], b=["bY"])
        ms_, fz = T.msk[:, 0:128], T["fz" + hh]
        v(ts(fz[:, 0::16], XF, 0.0, OP.is_ge, GATE, OP.mult), 8, r=["A", "fz0" + hh], w=[k_("fz")], b=["bA"])
        v(lambda: g.vector.tensor_tensor_scan(fl[:], ms_, fz[:], 0.0, OP.mult, OP.add), n, 0.5, r=["msk", k_("fz")], w=[k_("fl") + "a"])
        FL = [k_("fl") + "a"]
        mm([MM(D[:, 256:384], T.ib[:], ed, True, False), MM(D[:, 256:384], T.nib[:], cb("mi", t, h), False, True)], 256,
           r=[e, mi, "ib", "nib"], w=["Dd"], b=["bD"])
        absd = T["absd" + hh][:]
        s(act(absd, D[:, 256:384], AF.Abs), n, r=["Dd"], w=[k_("absd")], b=["bD"])
        mm([MM(D[:, 384:512], T.ib[:], ed, True, False), MM(D[:, 384:512], T.ib[:], cb("mi", t, h), False, False),
            MM(D[:, 384:512], fl[:], T.i1024[:], False, True),
            MM(D[:, 128:256], fl[:], T.im512[:], True, False), MM(D[:, 128:256], T.ib[:], absd, False, True)], 5 * 128,
           r=FL + [e, mi, k_("absd"), "ib", "im512", "i1024"], w=["De"], b=["bD"])
        v(ts(it("t2"), D[:, 384:512], 0.5, OP.mult, 512.25, OP.subtract), n, r=["De"], w=[k_("t2")], b=["bD"])
        v(tt(edo, it("t2"), D[:, 128:256], OP.max), n, r=[k_("t2"), "De"], w=[eo], b=["bD"])
        if t < V - 1:
            if h == 1:
                mm([MM(D[:, 0:8], T.onec[:], T["fl%d" % a][:, 0::16], a == 0, a == 1) for a in range(2)], 128, r=FL + ["fl0a", "onec"], w=["Du"], b=["bD"])
                v(lambda: g.vector.tensor_reduce(T.cnt[:, 0:1], D[:, 0:8], AX.X, OP.add, negate=True), 8, r=["Du"], w=["cnt"], b=["bD"])
                v(ts(T.acol[:], T.cnt[:, 0:1], 15.5, OP.subtract, 1.0 / 32, OP.mult), 1, r=["cnt"], w=["ac0"])
                v(ts(T["eo%d" % t][:, 256:257], T.acol[:], -32.0, OP.mult, T.cnt[:, 0:1], OP.add), 1, r=["ac0", "cnt"], w=[eo + "A"])
            d1 = dst(-1)
            if h or not JOINE(t):
                hs = range(0 if JOINE(t) else h, h + 1)
                sl = slice(128 * hs[0], 128 + 129 * h)
                sentE[h] = send("re%d%d" % (t + 1, h), T["e%d" % (t + 1)][:, sl], T["eo%d" % t][:, sl], d1, topo.engines(core, d1)[-8:],
                                ["eo%d%d" % (t, a) for a in hs] + [eo + "A"] * h, LAT, ["e%d%d" % (t + 1, a) for a in hs])
        else:
            op("Y", 0.1, [lambda: g.sync.dma_start(T.ye[:, 128 * h:128 * h + 128], edo)], r=[eo], sig=("d_ye%d" % h, 16), lat=2.0)
        pst, last = cb("lst", t, h), t == V - 1
        lk, ln = "lh%d%d" % (t, h), "lh%d%d" % (t + 1, h)
        if last:
            mm([MM(D[:, 0:128], one_row, T.rowb[0:1, 0:128], True, False), MM(D[:, 0:128], lh, T.i16[:], False, True)], 2 * 128,
               r=["one", "i16", lk] + CB_, w=["Du"], b=["bD"])
        v(tt(ft("m3"), ft("y"), X3, OP.min), n, r=[k_("y"), "A"], w=[k_("m3")], b=["bA"])
        r3 = "m3" if t else "r3"
        if not t:
            v(tt(ft("r3"), ft("m3"), PL, OP.max), n, r=[k_("m3"), E2], w=[k_("r3")], b=[bE])
        v(tt(E[:, 0:128], qo, X2, OP.min), n, r=[qk, "A"], w=[E0], b=["bA", bE])
        v(tt(E[:, 128:256], pst, X1, OP.min), n, r=["lst%d%d" % (t, h), "A"], w=[E1], b=["bA", bE])
        v(tt(ft("m1"), E[:, 128:256], fl[:], OP.subtract), n, r=FL + [E1], w=[k_("m1")], b=[bE])
        v(tt(E[:, 0:128], ft(r3), E[:, 0:128], OP.max), n, r=[k_(r3), E0], w=[E0], b=[bE])
        v(tt(it("r1"), ft("m1"), E[:, 0:128], OP.max), n, r=[k_("m1"), E0], w=[k_("r1")], b=[bE])
        nw, nk, lhn = cb("raw", t + 1, h), "raw%d%d" % (t + 1, h), cb("lh", t + 1, h)
        v(ts(nw, it("r1"), 4095, OP.bitwise_and), n, r=[k_("r1")], w=[nk])
        v(ts(lhn, nw, 2048.0, OP.subtract), n, r=[nk], w=[ln])
        mm([MM(E[:, 256:384], lhn, T.i16[:], True, True)], 128, r=["i16", ln], w=[E2], b=[bE])
        if not last:
            v(ts(cb("u16l", t + 3, h), E[:, 256:384], 2048.0, OP.add), n, r=[E2], w=["u16l%d%d" % (t + 3, h)], b=[bE])
        term = lambda o_, a, m, st, sp: MM(o_, a, m, st, sp) if last else MM(o_, m, a, st, sp)
        EL, bL, kL = E[:, 256:384], bE, E2
        bE = BANKS(t, h)[1]
        E, (E0, E1, E2, E3) = T[bE], [bE + str(i) for i in range(4)]
        eq, o_ = cb("eq", 0, h), E[:, 128:256]
        if last:
            mm([term(o_, lhn, T.i16[:], True, False), term(o_, lh, T.n16[:], False, True)], 2 * 128, r=["i16", "n16", lk, ln], w=[E1], b=[bE])
            v(ts(eq, o_, 0.0, OP.is_equal), n, r=[E1], w=[k_("eq")], b=[bE])
        else:
            v(tt(eq, lhn, lh, OP.is_equal), n, r=[lk, ln], w=[k_("eq")])
        o_ = E[:, 384:512]
        if t:
            mm([term(o_, ft("xq"), T.i32[:], True, False), term(o_, lh, T.i16[:], False, False), term(o_, cb("lh", t - 1, h), T.n16[:], False, True)],
               6 * 128, r=["i32", "i16", "n16", lk, "lh%d%d" % (t - 1, h), k_("xq")], w=[E3], b=[bE])
        else:
            hs = slice(128 * h, 128 * h + 128)
            mm([MM(o_, T.f_ll[:, hs], T.i16[:], True, False), MM(o_, T.f_ql[:, hs], T.n16[:], False, True)], 2 * 128,
               r=["i16", "n16", "f_ll", "f_ql"], w=[E3], b=[bE])
        v(tt(ft("xq"), eq, E[:, 384:512], OP.mult), n, r=[k_("eq"), E3], w=[k_("xq")], b=[bE])
        if t >= 2:
            o_ = cb("outs", t - 2, h)
            nm = ("yp", "ys", "yl")[t - 2]
            shifted(o_, EL, 2048.0, n, r=[kL], w=["outs%d%d" % (t - 2, h)], b=[bL])
            op("Y", 0.1, [lambda: g.sync.dma_start(T[nm][:, 128 * h:128 * h + 128], o_)], r=["outs%d%d" % (t - 2, h)], sig=("d_%s%d" % (nm, h), 16), lat=2.0)
        if last:
            oq = cb("outs", 3, h)
            v(tt(oq, D[:, 0:128], ft("xq"), OP.subtract), n, r=["Du", k_("xq")], w=["outs3%d" % h], b=["bD"])
            op("Y", 0.1, [lambda: g.sync.dma_start(T.yq[:, 128 * h:128 * h + 128], oq)], r=["outs3%d" % h], sig=("d_yq%d" % h, 16), lat=2.0)

    for h in range(H2):
        first_page_form(h)
    for t in range(V):
        if t < 4:
            tabs(t)
        for f in (big, logic):
            for h in range(H2):
                now[:] = [t, h]
                f(t, h)
    return ops


def _choose(ops):
    n, Q = len(ops), "TVSGYR"
    q, dma = [o["q"] for o in ops], [o.get("dma", 0.0) for o in ops]
    names = sorted({b for o in ops for b in o["b"]})
    bank = [[3 * names.index(b) for b in o["b"]] for o in ops]
    other = ((1, 2), (0, 2), (0, 1))
    can = [[Q.index(e) for e in o.get("e", o["q"])] for o in ops]
    anc, pred, succ = [], [], [[] for _ in ops]
    for i, o in enumerate(ops):
        far = 0
        for d in o["d"]:
            far |= anc[d]
        pred.append(sorted(d for d in o["d"] if not far >> d & 1))
        anc.append(far | sum(1 << d for d in pred[i]))
        for d in pred[i]:
            succ[d].append(i)
    waits = [[d for d in pred[i] if not q[i] == q[d] == "T"] for i in range(n)]

    def costs(slow, gath, far):
        f = [1.0 if e not in "TVSX" else slow * gath if o["n"][1:2] == "g" else slow for e, o in zip(q, ops)]
        return ([o["c"] * x for o, x in zip(ops, f)], [o["lat"] * (far if e == "R" else 1.0) + WAKE * far ** 3 for e, o in zip(q, ops)],
                [x * far for x in dma], START * far)

    def first(gaps, x):
        lo, hi = 0, len(gaps)
        while lo < hi:
            m = (lo + hi) // 2
            if gaps[m][1] < x:
                lo = m + 1
            else:
                hi = m
        return lo

    def fit(gaps, r, d):
        k = first(gaps, r + d)
        while True:
            a, b = gaps[k]
            if a < r:
                a = r
            if a + d <= b + 1e-9:
                return a
            k += 1

    def cut(gaps, x, y):
        k = lo = first(gaps, x + 1e-9)
        new, (a, b) = [], gaps[k]
        while a < y:
            if x - a > 0.04:
                new.append((a, x))
            k += 1
            if b - y > 0.04:
                new.append((y, b))
                break
            a, b = gaps[k]
        gaps[lo:k] = new

    def place(key, forward, tab, bias):
        c, la, dm, st = tab
        gaps, free = [[(0.0, 1e9)] for _ in range(7)], [[(0.0, 1e9)] for _ in range(3 * len(names))]
        start, eng = [0.0] * n, [0] * n
        ready = [0.0 if forward or succ[i] else la[i] for i in range(n)]
        for i in sorted(range(n), key=lambda i: key[i]):
            r, d, best = ready[i], c[i], None
            if dm[i] and not forward:
                s = fit(gaps[6], max(r - st - dm[i], 0.0), dm[i])
                cut(gaps[6], s, s + dm[i])
                r = max(r, s + dm[i] + st)
            for e in can[i]:
                s, s2 = -1.0, r
                while s2 > s:
                    s = s2 = fit(gaps[e], s2, d)
                    for b in bank[i]:
                        s2 = fit(free[b + e], s2, d)
                if best is None or s + bias < best[0]:
                    best = (s, e)
            s, e = start[i], eng[i] = best
            if d:
                cut(gaps[e], s, s + d)
            for b in bank[i]:
                for x in other[e]:
                    cut(free[b + x], s - WAKE, s + d + WAKE)
            f = s + d
            if dm[i] and forward:
                s = fit(gaps[6], f + st, dm[i])
                cut(gaps[6], s, s + dm[i])
                f = s - st
            for k in succ[i] if forward else pred[i]:
                x = f + (1e-6 if q[i] == q[k] == "T" else la[i if forward else k])
                if x > ready[k]:
                    ready[k] = x
        return start, eng

    def run(seq, eng, tab, p0, state, fin, marks=None, why=None):
        c, la, dm, st = tab
        free, held, dfree = state[0][:], state[1][:], state[2]
        last, lastd = [-1] * (6 + len(held)), -1
        for p, i in enumerate(seq[p0:], p0):
            e, bs = eng[i], bank[i]
            s = free[e]
            for d in waits[i]:
                if fin[d] > s:
                    s = fin[d]
            if bs:
                x, y = other[e]
                for b in bs:
                    if held[b + x] > s:
                        s = held[b + x]
                    if held[b + y] > s:
                        s = held[b + y]
            if marks:
                if p % STEP == 0:
                    marks[p // STEP] = (free[:], held[:], dfree)
                w = (last[e], 1) if s == free[e] else ([(d, 0) for d in waits[i] if fin[d] == s] +
                                                       [(last[6 + b + x], 1) for b in bs for x in other[e] if held[b + x] == s])[0]
                why[i] = (w, lastd if dm[i] and dfree > s + c[i] + st else -1, s)
                last[e] = i
                for b in bs:
                    last[6 + b + e] = i
                if dm[i]:
                    lastd = i
            f = s + c[i]
            if e != 5:
                free[e] = f
            for b in bs:
                held[b + e] = f + WAKE
            if dm[i]:
                dfree = max(f + st, dfree) + dm[i]
                f = dfree - st - dm[i]
            fin[i] = f + la[i]
        return max(fin) - WAKE

    zero, tabs = ([0.0] * 6, [0.0] * (3 * len(names)), 0.0), [costs(*m[:3]) for m in SETTINGS]
    worth = lambda j, span: 100.0 / (POWER * len(tabs)) * (span / SETTINGS[j][3]) ** POWER
    rs = np.random.RandomState(SEED)
    tab, key = tabs[0], [0.0] * n
    for i in reversed(range(n)):
        key[i] = min([key[k] for k in succ[i]] + [0.0]) - tab[0][i] - tab[1][i]
    best = cur = None
    for turn in range(TRIES):
        slow, bias, size, at = rs.random_sample(4).tolist()
        tab, bias = costs(1.0 + SLOW * slow, GF, FAR), BIAS * bias
        if cur:
            at, key = 110 * at - 15, []
            for i, x in enumerate(rs.random_sample(n).tolist()):
                key.append(max([cur[1][i] + (size * size * x if at <= cur[1][i] <= at + 25 else 0.0)] + [key[d] + 1e-6 for d in pred[i]]))
        start, eng = place(key, True, tab, bias)
        for _ in range(2 if cur else 6):
            back = place([-s - c for s, c in zip(start, tab[0])], False, tab, bias)[0]
            start, eng = place([-s - c for s, c in zip(back, tab[0])], True, tab, bias)
            seq = sorted(range(n), key=lambda i: start[i])
            val = sum(worth(j, run(seq, eng, t, 0, zero, [0.0] * n)) for j, t in enumerate(tabs))
            if cur is None or val < cur[0] + HEAT[0] * slow:
                cur = (val, start, seq, eng)
            if best is None or val < best[0]:
                best = cur

    def full(seq):
        out = []
        for t in tabs:
            fin, marks, why = [0.0] * n, [None] * (n // STEP + 1), [None] * n
            span, pairs = run(seq, eng, t, 0, zero, fin, marks, why), []
            i, byq = fin.index(max(fin)), False
            while i >= 0:
                (d, kind), dd, _ = why[i]
                if dd >= 0 and not byq:
                    d, kind = dd, 2
                if kind and d >= 0:
                    pairs.append((d, i))
                i, byq = d, kind == 1
            out.append((span, fin, marks, why, pairs))
        pos = [0] * n
        for k, i in enumerate(seq):
            pos[i] = k
        return out, sum(worth(j, r[0]) for j, r in enumerate(out)), pos

    seq, eng = best[2], best[3][:]
    res, val, pos = full(seq)
    best, taken = (val, seq, eng[:], res[0][3]), 0
    for turn in range(MOVES):
        a, b, kind, far, heat = rs.random_sample(5).tolist()
        pairs = res[int(a * len(res))][4]
        u, v = pairs[int(b * len(pairs))]
        far, new, flip = int(-12 * math.log(1 - far)), seq, None
        if kind < 0.2:
            flip = u if kind < 0.1 else v
            if q[flip] != "X":
                continue
            eng[flip], p0 = 3 - eng[flip], pos[flip]
        elif kind < 0.6:
            p0 = max([pos[d] + 1 for d in pred[v]] + [0, pos[u] - far])
            if p0 > pos[u]:
                continue
            new = seq[:p0] + [v] + seq[p0:pos[v]] + seq[pos[v] + 1:]
        else:
            p0, k = pos[u], min([pos[d] - 1 for d in succ[u]] + [n - 1, pos[v] + far])
            if k < pos[v]:
                continue
            new = seq[:p0] + seq[p0 + 1:k + 1] + [u] + seq[k + 1:]
        k = p0 // STEP
        x, room = 0.0, -HEAT[1] * (HEAT[2] / HEAT[1]) ** (turn / MOVES) * math.log(1 - heat)
        for j in range(len(res)):
            j = (j + int(a * len(res))) % len(res)
            x += worth(j, run(new, eng, tabs[j], k * STEP, res[j][2][k], res[j][1][:])) - worth(j, res[j][0])
            if x > room + 0.1:
                break
        if x <= room:
            seq, taken = new, taken + 1
            res, val, pos = full(seq)
            if taken % 20 == 0:
                seq = sorted(seq, key=lambda i: res[0][3][i][2])
                res, val, pos = full(seq)
            if val < best[0]:
                best = (val, seq, eng[:], res[0][3])
        elif flip is not None:
            eng[flip] = 3 - eng[flip]
    return best[1], [Q[e] for e in best[2]], [w[2] for w in best[3]]


def _order(ops):
    if len(ops) not in _CHOSEN:
        _CHOSEN[len(ops)] = _choose(ops)
    seq, took, start = _CHOSEN[len(ops)]
    order, held = {}, {}
    for i in seq:
        o = ops[i]
        if o["q"] == "X":
            o["f"] = o["alt"][took[i]]
        o["st"], o["q"] = start[i], took[i]
        for b in o["b"]:
            for e, k in held.setdefault(b, {}).items():
                if e != o["q"]:
                    o["d"][k] = 1
            held[b][o["q"]] = i
        order.setdefault(o["q"], []).append(o)
    order["Y"].sort(key=lambda o: (o["st"], o["i"]))
    return order


def rank_program(g, core, T, topo):
    if T.rank_of(core) is None:
        port, hands = _helpers(T, topo)
        for die, c in port.get(topo.chip(core), {}).items():
            if c == core:
                _port_program(g, core, T, topo, die)
        for owner in hands:
            if core in hands[owner]:
                calls = [c for o in _order(_plan(g, owner, T, topo))["G"] for c in o.get("calls", [])]
                _hand_program(g, core, T, topo, owner, calls)
        return
    ops = _plan(g, core, T, topo)
    order = _order(ops)
    qs = {"T": g.tensor, "V": g.vector, "S": g.scalar, "G": g, "Y": g.sync}
    qsem = {"T": "sT", "V": "sV", "S": "sS", "G": "sG"}
    known = {q: {} for q in qs}
    sent = 0
    glob = [o for q in order for o in order[q]]
    for q in ("T", "V", "S", "G"):
        c = 0
        for o in order[q]:
            if o["sig"] is None:
                c += len(o["f"])
                o["val"] = (qsem[q], c)
            elif o["sig"][0] == "send":
                o["val"] = None
    for q in ("Y", "R"):
        for o in order[q]:
            o["val"] = o["sig"]
    for o in sorted(glob, key=lambda o: (o["st"], o["i"])):
        o["w"] = []
        if o["q"] == "R":
            o["clk"] = {o["val"][0]: o["val"][1]}
            continue
        kn = known[o["q"]]
        need = {}
        for d in o["d"]:
            x = ops[d]
            if x["val"] is None or (x["q"] == "T" and o["q"] == "T"):
                continue
            sm, vl = x["val"]
            if kn.get(sm, 0) < vl and need.get(sm, (0, None))[0] < vl:
                need[sm] = (vl, x)
        for sm in sorted(need, key=lambda m: -need[m][1]["st"]):
            vl, x = need[sm]
            if kn.get(sm, 0) < vl:
                o["w"].append((sm, vl))
                for a, b in list(x["clk"].items()) + [(sm, vl)]:
                    if kn.get(a, 0) < b:
                        kn[a] = b
        o["clk"] = dict(kn)
        if o["val"] is not None:
            o["clk"][o["val"][0]] = o["val"][1]
    for q in qs:
        eng = qs[q]
        for o in order.get(q, []):
            for sm, vl in o["w"]:
                eng.wait_ge(T.sem[sm], vl)
            for f in o["f"]:
                ins = f()
                if o["sig"] is None:
                    ins.then_inc(T.sem[qsem[q]], 1)
                elif o["sig"][0] == "send":
                    sent += o["sig"][1]
                else:
                    ins.then_inc(T.sem[o["sig"][0]], 16)
    for q in ("T", "V", "S", "G"):
        tot = max([o["val"][1] for o in order[q] if o["val"] is not None] + [0])
        g.sync.wait_ge(T.sem[qsem[q]], tot)
    for nm in STORES:
        g.sync.wait_ge(T.sem["d_" + nm], 16)
    g.wait_ge(T.sem["lsem"], sent)
